import numpy as np, ml_dtypes
CORES = [5,29,101,125,133,157,229,253]
N = 8
BF = ml_dtypes.bfloat16
CA, LV, NS, RO, HA, HB = 16, 128, 4, 2, 1, 4
W, KC = CA * LV, LV // 4
K = CA * KC
def water(rng, m=16):
    z = np.linspace(1.5, -1.5, LV); res = []
    for sg in (1.0, -1.0):
        v = sg * rng.uniform(0.5, 1.5, (N, 8, 1, CA, 1)) * z + 0.5 * rng.standard_normal((N, 8, 1, CA, 1))
        v = v.astype(np.float32) + 0.25 * rng.standard_normal((N, 8, 1, CA, LV), dtype=np.float32)
        res.append(v + 0.35 * rng.standard_normal((N, 8, m, CA, LV), dtype=np.float32))
    return res
def coef(rng, m=16):
    return np.stack([rng.uniform(0.5, 1.5, (N, 8, m)), rng.uniform(2.0 ** -13, 2.0 ** -11, (N, 8, m)), rng.uniform(0.5, 1.5, (N, 8, m))], axis=-1)
def pack(te, sa, co, cu):
    return {"te": np.ascontiguousarray(te.reshape(N, 128, W)).astype(BF), "sa": np.ascontiguousarray(sa.reshape(N, 128, W)).astype(BF),
            "co": np.ascontiguousarray(co.reshape(N, 128, 3)).astype(np.float32), "cu": np.ascontiguousarray(cu.reshape(N, 8, W)).astype(np.int32)}
def setup_inputs(rng):
    te, sa = water(rng)
    return pack(te, sa, coef(rng), rng.integers(0, CA, (N, 8, W)))
def setup_inputs_spread(rng):
    te, sa = water(rng); k = (N, 8, 1, CA, LV)
    te = te * np.exp2(rng.integers(-3, 4, k)) * (rng.random(k) > 0.0625); sa = sa * np.exp2(rng.integers(-3, 4, k)) * (rng.random(k) > 0.0625)
    co = np.stack([np.exp2(rng.uniform(-2, 2, (N, 8, 16))), rng.uniform(2.0 ** -20, 2.0 ** -10, (N, 8, 16)), np.exp2(rng.uniform(-2, 2, (N, 8, 16)))], axis=-1)
    cu = np.minimum((CA * rng.random((N, 8, W)) ** 3).astype(np.int64), CA - 1)
    return pack(te, sa, co, cu)
def setup_inputs_ends(rng):
    b = 4096.0; pt = np.ones((8, CA, LV)); ps = np.ones((8, CA, LV)); pc = np.zeros((8, CA, LV), np.int64)
    pt[:, 0] = -1; ps[:, 0] = -1; pc[:, 0] = CA - 1
    for c in range(1, CA - 1):
        if c % 4 == 3: ps[:, c] = -1; pt[:, c, :2] = -1; ps[:, c, :2] = 1; pc[:, c] = CA - 1
        else: pt[:, c] = -1; pt[:, c, LV - 2:] = 1; ps[:, c, LV - 2:] = -1
    pt[1::2, CA - 1, LV - 4] = -1; ps[1::2, CA - 1, LV - 2:] = -1
    def turned(m, share, col):
        t = (rng.random((N, 8, m, CA, LV), dtype=np.float32) < share) ^ (rng.random((N, 8, 1, CA, LV), dtype=np.float32) < col)
        t[..., :8] = False; t[..., LV - 8:] = False; t[:, :, :, 0] = False; t[:, :, :, CA - 1] = False
        return t
    te = np.where(turned(16, 0.15, 0.1), -b, b).astype(np.float32) * pt[None, :, None].astype(np.float32)
    sa = np.where(turned(16, 0.15, 0.1), -b, b).astype(np.float32) * ps[None, :, None].astype(np.float32)
    n = te[:, :, :, 4:CA - 1:4].shape
    te[:, :, :, 4:CA - 1:4] = rng.uniform(-b, b, n); sa[:, :, :, 4:CA - 1:4] = rng.uniform(-b, b, n)
    cu = np.where(turned(1, 0.2, 0.0)[:, :, 0], CA - 1 - pc[None], pc[None])
    cu[:, :, 4:CA - 1:4] = (CA - 1) * rng.integers(0, 2, cu[:, :, 4:CA - 1:4].shape)
    good = np.argsort(rng.random((N, 8, 16)), axis=-1) < 11
    co = np.stack([np.where(good | (rng.random((N, 8, 16)) < 0.5), 4.0, 0.25), np.where(rng.random((N, 8, 16)) < 0.5, 0.0, 2.0 ** -10), np.where(good | (rng.random((N, 8, 16)) < 0.5), 0.25, 4.0)], axis=-1)
    return pack(te, sa, co, cu)
def setup_inputs_corners(rng):
    te, sa = water(rng); te = te + rng.choice(np.array([-3.0, 0.0, 3.0]), (N, 8, 1, 1, 1))
    own = np.repeat(np.arange(CA), LV); lev = np.arange(W) % LV; cu = rng.integers(0, CA, (N, 8, W)); any3 = rng.integers(0, 3, (N, 8, W))
    for r in range(N):
        for g in range(8):
            k = (r + g) % 8
            if k == 0: cu[r, g] = own
            elif k == 1: cu[r, g] = 0
            elif k == 2: cu[r, g] = CA - 1
            elif k == 3: cu[r, g] = (own + 1) % CA
            elif k == 4: cu[r, g] = CA - 1 - own
            elif k == 5: cu[r, g] = np.where((lev >> 2) % 2 == 0, 0, CA - 1)
            elif k == 6: cu[r, g] = np.where(any3[r, g] == 0, 0, np.where(any3[r, g] == 1, CA - 1, own))
    co = coef(rng); h = CA // 2
    te[:, 2::4, :, :h] = 0; te[:, 2::4, :, h:] = 1; sa[:, 2::4, :, :h] = 0; sa[:, 2::4, :, h:] = 1
    for r in range(N):
        for g in (2, 6):
            x0 = 128 * (KC // 4 + 1 + 2 * int(rng.integers(0, KC // 8)))
            a0 = rng.uniform(0.5, 1.5, 4096).astype(np.float32); a1 = (rng.uniform(0.5, 1.0, 4096) / x0).astype(np.float32)
            two = a1 * np.float32(x0) + a0; one = (a1.astype(np.float64) * x0 + a0.astype(np.float64)).astype(np.float32)
            k = np.argsort(np.where(one > two, 0, 1), kind="stable")[:16]
            co[r, g] = np.stack([a0[k], a1[k], two[k]], axis=-1); cu[r, g] = rng.integers(h, CA, W)
    f4 = np.float32
    for r in range(N):
        ra = (r + HA) % N; rb = (r + HB) % N
        for g in (1, 3, 4, 5, 7):
            j = KC // 4 + 1 + int(rng.integers(0, KC // 4)); l = 4 * j + 1; x0 = 128 * j + (28 if g == 4 else 24)
            a0 = rng.uniform(0.5, 1.5, 4096).astype(f4); a1 = (rng.uniform(0.5, 1.0, 4096) / x0).astype(f4); w = a1 * f4(x0) + a0
            tu = np.full(4096, 32, f4); su = np.full(4096, 32, f4); b0 = np.nextafter(w, f4(0)); ok = np.ones(4096, bool)
            if g == 1:
                b0 = w; ok = ((a1 * f4(x0 - 8) + a0) + a1 * f4(8)) > w
            if g in (3, 7):
                tu = (2 * rng.integers(64, 128, 4096)).astype(f4); su = (2 * rng.integers(64, 128, 4096)).astype(f4)
                left = tu * w; b0 = left / su; ok = (su * b0 == left) & (b0 < 4)
                if g == 3: ok = ok & (tu.astype(np.float64) * w.astype(np.float64) > su.astype(np.float64) * b0.astype(np.float64))
                else: ok = ok & (left * (f4(1) / b0) > su)
                b0 = np.minimum(b0, f4(4))
            k = np.argsort(np.where(ok, 0, 1), kind="stable")[:16]
            tl, tr = (2816, -1280) if g == 4 else (1792, -2304)
            sl, sr, s1 = 0.0, 0.0, -su[k]
            if g == 4: sl, sr, s1 = 1.25 * 2.0 ** -18, -128.0, np.full(16, -128.0)
            if g == 5: sl, sr, s1 = -224.0, 288.0, np.full(16, -2.0 ** -18)
            te[ra, g, :, 1, :l + 1] = tl; te[ra, g, :, 1, l + 1:] = tr
            sa[ra, g, :, 1, :l + 1] = sl; sa[ra, g, :, 1, l + 1:] = sr
            te[r, g, :, 4:, 4 * j] = (-256 - tu[k])[:, None]; sa[r, g, :, 4:, 4 * j] = s1[:, None]
            cu[r, g, 4 * LV + 4 * j::LV] = 1; cu[ra, g, LV + l] = int(rng.integers(4, CA))
            co[ra, g] = np.stack([a0[k], a1[k], b0[k]], axis=-1)
        te[r, 7, :, 4:, LV - 4] = -544; sa[r, 7, :, 4:, LV - 4] = -32; cu[r, 7, 5 * LV - 4::LV] = 2
        te[ra, 7, :, 2] = -288; sa[ra, 7, :, 2] = -32; cu[ra, 7, 3 * LV - 2] = 3
        te[rb, 0, :, 3, LV - 2] = 3328; te[rb, 0, :, 3, LV - 1] = -768; sa[rb, 0, :, 3, LV - 2:] = 0
        xm = 32 * (LV - 2) + 28
        a0 = rng.uniform(0.5, 1.5, 16).astype(f4); a1 = (rng.uniform(0.5, 1.0, 16) / xm).astype(f4)
        co[rb, 0] = np.stack([a0, a1, a1 * f4(xm - 1) + a0], axis=-1)
    return pack(te, sa, co, cu)
def setup_inputs_crowd(rng):
    te, sa = water(rng, 1); e = rng.permutation(16); sg = np.ones((8, 16), np.float32)
    for g in range(8): sg[g, e[:(0, 1, 7, 8)[g % 4]]] = -1
    te = te * sg[None, :, :, None, None]; sa = sa * sg[None, :, :, None, None]
    co = np.repeat(coef(rng, 1), 16, axis=2)
    one = rng.integers(0, CA, (N, 8)); cu = np.repeat(one[:, :, None], W, axis=2)
    for r in range(N):
        for g in range(1, 8, 2): cu[r, g, 4 * int(rng.integers(0, K))] = (one[r, g] + 1 + int(rng.integers(0, CA - 1))) % CA
    return pack(te, sa, co, cu)
def setup_inputs_calm(rng):
    te, sa = water(rng); co = coef(rng); cu = rng.integers(0, CA, (N, 8, CA, LV))
    e = rng.permutation(16); up = np.zeros(16, bool); up[e[:8]] = True
    t = 0.25 * rng.integers(-4, 5, 16); s = 0.25 * rng.integers(-4, 5, 16)
    sa[:, :, :, :4] = s[None, None, :, None, None]; sa[:, :, :, :, :2] = s[None, None, :, None, None]; sa[:, :, :, :, LV - 4:] = s[None, None, :, None, None]
    te[:, :, :, :4] = t[None, None, :, None, None]; te[:, :, :, 3] += 1; te[:, :, int(e[0]), 0] += 0.9
    for g in range(4):
        a1 = t + 1 - 16 / (2 * g + 1); b1 = t - 1 + 16 / (1.0, 1.0, 1.5, 1.8)[g]
        te[:, g, :, 4:, 0] = np.where(up, t + 1, t - 1)[None, :, None]; te[:, g, :, 4:, 1] = np.where(up, a1, b1)[None, :, None]
    for g in range(4, 8):
        for lv, v in ((LV - 4, -1.0), (LV - 3, -1.3684), (LV - 2, 2.0), (LV - 1, 2.0 if g % 2 == 0 else 2 - 16 / 13)): te[:, g, :, 4:, lv] = (t + v)[None, :, None]
    cu[:, :4, 4:, :4] = 0; cu[:, 4:, 4:, LV - 4:] = 2; cu[:, :, 0] = 1; cu[:, :, 2] = 3
    cu[:, :, 0, 8:] = rng.integers(4, CA, (N, 8, LV - 8))
    return pack(te, sa, co, cu)
def check_inputs(d):
    bad = []
    if np.min(d["cu"]) < 0 or np.max(d["cu"]) > CA - 1: bad.append("range of cu")
    for k in ("te", "sa"):
        a = np.abs(np.asarray(d[k]).astype(np.float32))
        if not np.max(a) <= 4096: bad.append("range of " + k)
        if np.any((a > 0) & (a < 2.0 ** -60)): bad.append("least size in " + k)
    c = np.asarray(d["co"]).astype(np.float64)
    for j, lo, hi in ((0, 0.25, 4.0), (1, 0.0, 2.0 ** -10), (2, 0.25, 4.0)):
        if not (np.min(c[..., j]) >= lo and np.max(c[..., j]) <= hi): bad.append("range of co, column " + str(j))
    if np.any((c[..., 1] > 0) & (c[..., 1] < 2.0 ** -20)): bad.append("least size in co, column 1")
    return bad
def reference(te, sa, co, cu):
    tw = te.astype(np.float32).reshape(N, 8, 16, W); sw = sa.astype(np.float32).reshape(N, 8, 16, W)
    cf = co.astype(np.float32).reshape(N, 8, 16, 3); cr = cu.astype(np.int64)
    base = (np.arange(N * 128) * W).reshape(N, 8, 16, 1); cbase = (np.arange(N * 8) * W).reshape(N, 8, 1)
    def pick(a, at):
        return np.take(a.reshape(-1), base + at[:, :, None, :])
    def moved(a, o, sh):
        return np.roll(a, (-o, -sh), (0, 1))
    def frac(k):
        return k.astype(np.float32)[:, :, None, :] * np.float32(0.0625)
    def passed(tv, sv, t1, s1, x, c):
        w = c[..., 1:2] * x.astype(np.float32)[:, :, None, :] + c[..., 0:1]
        yes = (tv - t1) * w > (sv - s1) * c[..., 2:3]
        return np.add.reduce(yes.astype(np.int64), axis=2) >= 9
    home = np.ascontiguousarray(np.broadcast_to(np.arange(K) // KC, (N, 8, K)))
    dep = np.ascontiguousarray(np.broadcast_to(64 * (np.arange(K) % KC), (N, 8, K)))
    for rnd in range(RO):
        d = dep; c = home; col = c * LV + (d >> 4); k = frac(d & 15)
        lo = pick(tw, col); t1 = lo + (pick(tw, col + 1) - lo) * k
        lo = pick(sw, col); s1 = lo + (pick(sw, col + 1) - lo) * k
        cnow = cr
        for hop, (o, sh) in enumerate(((HA, 0), (HB, 1), (0, 0))):
            c = np.take(cnow.reshape(-1), cbase + c * LV + (d >> 4)) if hop < 2 else home
            cnow = moved(cr, o, sh); th = moved(tw, o, sh); sh_ = moved(sw, o, sh); ch = moved(cf, o, sh)
            l = d >> 4
            for j in range(NS - 1, -1, -1):
                st = 2 ** j
                ok = passed(pick(th, c * LV + l), pick(sh_, c * LV + l), t1, s1, d + 16 * l, ch)
                l = np.where(ok, np.minimum(l + st, LV - 2), np.maximum(l - st, 0))
            ta = pick(th, c * LV + l); tb = pick(th, c * LV + l + 1) - ta
            sa_ = pick(sh_, c * LV + l); sb = pick(sh_, c * LV + l + 1) - sa_
            q = np.zeros_like(l)
            for h in (8, 4, 2):
                k = frac(q + h)
                ok = passed(ta + tb * k, sa_ + sb * k, t1, s1, d + 16 * l + q + h, ch)
                q = np.where(ok, q + h, q)
            k = frac(q); t1 = ta + tb * k; s1 = sa_ + sb * k; d = 16 * l + q
        dep = dep + ((d - dep) >> 1)
        old = tw[..., rnd::4]; tw[..., rnd::4] = old + (t1 - old) * np.float32(0.25)
        old = sw[..., rnd::4]; sw[..., rnd::4] = old + (s1 - old) * np.float32(0.25)
    return {"yt": np.ascontiguousarray(tw[..., RO - 1::4]).reshape(N, 128, K), "ys": np.ascontiguousarray(sw[..., RO - 1::4]).reshape(N, 128, K), "yd": dep.astype(np.float32)}

@@ -1,0 +1,808 @@
+from concourse.bass import DstId, RemoteDMATransfer
+from concourse.mybir import AluOpType, ActivationFunctionType
+
+NST = 2
+NW = 512 // NST
+NC = NW // 16
+NREL = 4
+FUSE_S = (1, 1, 1, 1)
+FUSE_N = (1, 1)
+PICK2 = 0
+SLIM = 0
+NOWAR = 0
+WT4_V = 4096
+ROLE = {'vof10.4': 100, 'spb0256.1': 600, 'vqs01536.1': -2400, 'vof048.2': -600, 'vst1128.1': -1100, 'vqs1512.1': -3000, 'tpa10.1': -600, 'vfo10.1': -1200, 'avsb0242.1': 300, 'swg10.7': 600, 'avmisc0.1': -3000, 'vwg00.1': -300, 'vpc10.12': -3000, 'vst164.1': 600, 'vst116.1': -1200, 'vst096.1': -1200, 'vqt0256.1': 1200, 'sqs00.1': 1200, 'vpc10.13': -600, 'tpc0256.3': 600, 'avsa10.1': 3000, 'vpc00.10': 600, 'vfb02.1': 600, 'vof016.3': -3000, 'srr00.5': 300, 'vst1176.1': 1200, 'voutb256.1': -3000, 'vpc00.12': -100, 'vqt01536.1': 1200, 'spd0256.1': -100, 'sqs10.1': 3000, 'mspa0256.1': -1200, 'sfb11.1': 600, 'spb1256.1': -1200, 'srr10.4': -100, 'swg10.6': -1800, 'vpc10.11': -600, 'ssa11.2': -3600, 'ssa01.3': 100, 'avmm112.1': -600, 'ss110.1': -600, 'avmm48.1': -300, 'vst0112.1': -3000, 'vof064.1': 100, 'vso00.3': 300, 'vof196.1': -3000, 'ssa11.1': 3000, 'voutb512.1': 600, 'vst0176.1': -3000, 'vof148.1': -300, 'vsa03.1': -3000, 'spd00.1': 3000, 'vqs0768.1': -600, 'vof164.1': 3000, 'vof016.4': -300, 'vof116.2': 100, 'spd1256.1': -600}
+TUNE = dict(lead=1500.0, look=0.0, noise=0.0, seed=1, role=ROLE)
+PAR = dict(cyc=1.04, g=1.56, wake=120.0, same=60.0, pe=0.52, dma=2000.0, bw=160.0, call=900.0, leg=2500.0, link=45.0)
+BIG = 1.0e6
+
+SCRATCH = {
+    "own0": ("sbuf", [128, 4096], "bfloat16"), "w1b": ("sbuf", [128, 4096], "bfloat16"),
+    "w4b": ("sbuf", [128, 4096], "bfloat16"), "stage4": ("sbuf", [128, 4096], "bfloat16"),
+    "we0": ("sbuf", [128, 2048], "bfloat16"), "we1": ("sbuf", [128, 2048], "bfloat16"),
+    "f0": ("sbuf", [128, 4096], "float32"), "f1": ("sbuf", [128, 4096], "float32"), "f4": ("sbuf", [128, 4096], "float32"),
+    "wt1": ("sbuf", [128, 7680], "float32"), "wt4": ("sbuf", [128, 3840], "float32"), "wt0": ("sbuf", [128, 3840], "float32"),
+    "cu0": ("sbuf", [128, 2048], "bfloat16"), "cu1": ("sbuf", [128, 2048], "bfloat16"),
+    "cui": ("sbuf", [128, 128], "int32"), "cub0": ("sbuf", [128, 128], "bfloat16"), "cub1": ("sbuf", [128, 128], "bfloat16"),
+    "ktab": ("sbuf", [128, 2048], "bfloat16"), "mm": ("sbuf", [128, 2048], "bfloat16"),
+    "ones": ("sbuf", [128, 128], "float32"), "ident": ("sbuf", [128, 128], "float32"),
+    "misc": ("sbuf", [128, 132], "float32"), "misc1": ("sbuf", [128, 132], "float32"),
+    "misc4": ("sbuf", [128, 33], "float32"), "co4": ("sbuf", [128, 4], "float32"),
+    "newb": ("sbuf", [128, 1024], "float32"), "new1": ("sbuf", [128, 1024], "float32"),
+    "new4": ("sbuf", [128, 1024], "float32"), "new4s": ("sbuf", [128, 1024], "float32"),
+    "outb": ("sbuf", [128, 1024], "float32"), "ydb": ("sbuf", [128, 512], "float32"),
+    "ci": ("sbuf", [128, 32], "int32"), "cf": ("sbuf", [128, 64], "float32"),
+}
+for _s in range(NST):
+    for _n in ("tg", "wg", "rr", "s1"):
+        SCRATCH["%s%d" % (_n, _s)] = ("sbuf", [128, NW], "float32")
+    for _n in ("qt", "qs"):
+        SCRATCH["%s%d" % (_n, _s)] = ("sbuf", [128, 7 * 256], "float32")
+    for _n in ("fa", "fb", "fo"):
+        SCRATCH["%s%d" % (_n, _s)] = ("sbuf", [128, 4 * NC], "float32")
+    SCRATCH["yes%d" % _s] = ("sbuf", [128, NW], "bfloat16")
+    SCRATCH["cug%d" % _s] = ("sbuf", [128, NW], "bfloat16")
+    SCRATCH["st%d" % _s] = ("sbuf", [128, 12 * NC], "float32")
+    SCRATCH["sa%d" % _s] = ("sbuf", [128, 5 * NC], "float32")
+    SCRATCH["sb%d" % _s] = ("sbuf", [128, 20 * NC], "float32")
+    SCRATCH["so%d" % _s] = ("sbuf", [128, 5 * NC], "float32")
+    SCRATCH["di%d" % _s] = ("sbuf", [128, 4 * NC], "int32")
+    SCRATCH["of%d" % _s] = ("sbuf", [128, 8 * NC], "uint16")
+    for _n in ("pa", "pb", "pc", "pd"):
+        SCRATCH["%s%d" % (_n, _s)] = ("psum", [128, 512], "float32")
+
+
+def R(name, a, b, step=1, p0=0, p1=128, ps=1):
+    return (name, a, b, step, p0, p1, ps)
+
+
+def IND(win, off):
+    return ("ind", win, off)
+
+
+def _n(r):
+    return 16 * _n(r[2]) if r[0] == "ind" else len(range(r[1], r[2], r[3]))
+
+
+def _space(r):
+    return "ind" if r[0] == "ind" else SCRATCH.get(r[0], ("hbm",))[0]
+
+
+def _two(r):
+    return r[0] != "ind" and r[0] in SCRATCH and SCRATCH[r[0]][2] in ("bfloat16", "uint16")
+
+
+def _bytes(r):
+    w = 2 if (r[0] in ("te", "sa") or _two(r)) else 4
+    return _n(r) * len(range(r[4], r[5], r[6])) * w
+
+
+def cost(op, P):
+    k, a = op["k"], op["a"]
+    c = P["cyc"]
+    if k in ("tt", "ts", "cp", "act", "scan"):
+        n = _n(a[0])
+        if a[1][0] == "ind":
+            t = (65 if k == "act" else 50) + n * P["g"] * c
+        elif k == "tt":
+            t = c * max(64, n * (2 if _space(a[1]) == "sbuf" and _space(a[2]) == "sbuf" else 1))
+        elif k != "act" and _two(a[0]) and _two(a[1]):
+            t = c * max(64, n / 2)
+        else:
+            t = c * max(64, n)
+        return t, t
+    if k == "ms":
+        t = c * max(64, _n(a[0]) / (2 if _two(a[0]) else 1))
+        return t, t
+    if k == "mm":
+        t = sum(P["pe"] * max(min(64, _n(m[1])), _n(m[2])) * (1 if _two(m[1]) else 4) for m in a)
+        return t, t + 60
+    if k in ("iota", "sel"):
+        t = 150 + 2 * c * _n(a[0])
+        return t, t
+    if k == "dma":
+        return (P["call"] if op["e"] == "g" else 60), P["dma"] + op.get("ahead", 0) / P["bw"] + _bytes(a[0]) / P["bw"]
+    if k == "send":
+        return P["call"], P["leg"] + a[1] / P["bw"]
+    if k == "arr":
+        return 0, a[2] * P["leg"] + a[3] / P["link"]
+    raise ValueError(k)
+
+
+def build():
+    ops, acc, bank, cur, seen = [], {}, {}, [None, "a"], {}
+
+    def add(e, k, a, rd, wr, after=(), **kw):
+        i = len(ops)
+        deps, soft = set(after), set()
+        flat = []
+        for r in rd:
+            flat += [(r[1], False), (r[2], False)] if r[0] == "ind" else [(r, False)]
+        flat += [(r, True) for r in wr]
+        for r, w in flat:
+            if r[0] not in SCRATCH:
+                continue
+            for (x, j, jw) in acc.setdefault(r[0], []):
+                if (w or jw) and x[1] < r[2] and r[1] < x[2] and x[4] < r[5] and r[4] < x[5]:
+                    own = w and NOWAR and ops[j]["e"] == e and e in "vst" and "dma" not in (k, ops[j]["k"])
+                    (soft if own else deps).add(j)
+            if SCRATCH[r[0]][0] == "psum":
+                b = bank.setdefault(r[0], [e, [], []])
+                if b[0] != e:
+                    b[0], b[2], b[1] = e, b[1], []
+                deps.update(b[2])
+                b[1].append(i)
+        for r, w in flat:
+            if r[0] not in SCRATCH:
+                continue
+            if w:
+                full = r[3] == 1 and r[4] == 0 and r[5] == 128 and r[6] == 1
+                acc[r[0]] = [t for t in acc[r[0]] if t[1] == i or not (t[0] == r or (full and r[1] <= t[0][1] and t[0][2] <= r[2]))]
+            acc[r[0]].append((r, i, w))
+        deps.discard(i)
+        key = "%s%s%d" % (e, wr[0][0], wr[0][1]) if wr else "send"
+        seen[key] = seen.get(key, 0) + 1
+        ops.append(dict(e=e, k=k, a=a, deps=sorted(deps), sdeps=[], soft=sorted(soft - deps - {i}), s=cur[0], role="%s%s.%d" % (cur[1], key, seen[key]), **kw))
+        return i
+
+    def phase(s, tag):
+        cur[0], cur[1] = s, tag
+        seen.clear()
+
+    def refs(*xs):
+        return [x for x in xs if isinstance(x, tuple)]
+
+    def tt(o, x, y, op):
+        return add("v", "tt", (o, x, y, op), [x, y], [o])
+
+    def ts(o, x, s1, op0, s2=None, op1=None):
+        return add("v", "ts", (o, x, s1, s2, op0, op1), refs(x, s1, s2), [o])
+
+    def cp(o, x):
+        return add("v", "cp", (o, x), [x], [o])
+
+    def ms(o, val):
+        return add("v", "ms", (o, val), [], [o])
+
+    def act(o, x, scale=None, bias=None):
+        return add("s", "act", (o, x, scale, bias), refs(x, scale, bias), [o])
+
+    def iota(o, pat, base, cm):
+        return add("g", "iota", (o, pat, base, cm), [], [o])
+
+    def dma(q, o, x, after=(), ahead=0):
+        return add(q, "dma", (o, x), [x], [o], after, ahead=ahead)
+
+    def send(what, rd, nbytes, after=(), behind=()):
+        i = add("g", "send", (what, nbytes), rd, [], after)
+        ops[i]["sdeps"] += list(behind)
+        return i
+
+    def arrive(sem, n, wr, mirror, legs, nbytes):
+        i = add(None, "arr", (sem, n, legs, nbytes), [], wr)
+        ops[i]["sdeps"] += list(mirror)
+        return i
+
+    def count(o, src):
+        g = [(o, R("mm", 128 * e, 128 * e + 128), R(src, e, NW, 16), e == 0, e == 15) for e in range(16)]
+        return add("t", "mm", g, [R("mm", 0, 2048), R(src, 0, NW)], [o])
+
+    ms(R("misc", 0, 4), 0.0)
+    d0 = dma("y", R("cui", 0, 128), R("cu", 0, 2048, 1, 0, 8))
+    dma("s", R("misc", 0, 3), R("co", 0, 3))
+    d1 = dma("y", R("own0", 0, 2048), R("te", 0, 2048))
+    d2 = dma("y", R("own0", 2048, 4096), R("sa", 0, 2048), ahead=1 << 19)
+    ops[d0]["first"], ops[d1]["first"], ops[d2]["first"] = 3, 2, 1
+    cp(R("misc", 4, 132), R("cui", 0, 128))
+    for h in (0, 1):
+        act(R("we0", 1024 * h, 1024 * h + 512), R("own0", 2048 * h, 2048 * h + 1024, 2))
+        cp(R("we0", 1024 * h + 512, 1024 * h + 1024), R("own0", 2048 * h + 1024, 2048 * h + 2048, 2))
+    s_m = send("misc", [R("misc", 0, 132)], 1 << 16)
+    s_e0 = send("even0", [R("we0", 0, 1024)], 1 << 18)
+    s_e1 = send("even1", [R("we0", 1024, 2048)], 1 << 18)
+    arrive("am0", (1, 0), [R("misc1", 0, 33)], [s_m], 1, 0)
+    arrive("am1", (3, 0), [R("misc1", 33, 132)], [s_m], 1, 0)
+    arrive("am4", (0, 1), [R("misc4", 0, 33)], [s_m], 0, 0)
+    a_e0 = arrive("ae0", (2, 0), [R("we1", 0, 1024)], [s_e0], 1, 1 << 17)
+    a_e1 = arrive("ae1", (2, 0), [R("we1", 1024, 2048)], [s_e1], 1, 1 << 17)
+    s_t = send("bulk0", [R("own0", 0, 2048)], 1 << 19, behind=[])
+    s_s = send("bulk1", [R("own0", 2048, 4096)], 1 << 19)
+    ops[s_t]["late"], ops[s_s]["late"] = s_e1, s_t
+    a_t = arrive("ab0", (2, 0), [R("w1b", 0, 2048)], [s_t, a_e1], 0, 1 << 18)
+    a_s = arrive("ab1", (2, 0), [R("w1b", 2048, 4096)], [s_s, a_t], 0, 1 << 18)
+    dma("y", R("co4", 0, 4, 1, 0, 112), R("misc4", 0, 4, 1, 16, 128))
+    dma("y", R("co4", 0, 4, 1, 112, 128), R("misc4", 0, 4, 1, 0, 16))
+    for h, src in enumerate(("te", "sa")):
+        dma("y", R("stage4", 2048 * h, 2048 * h + 2048, 1, 0, 112), R(src, 0, 2048, 1, 16, 128), [a_e1], ahead=h << 19)
+        dma("y", R("stage4", 2048 * h, 2048 * h + 2048, 1, 112, 128), R(src, 0, 2048, 1, 0, 16), [a_e1], ahead=h << 19)
+    s_4 = send("bulk4", [R("stage4", 0, 4096)], 1 << 19, [a_t])
+    a_4 = arrive("ab4", (1, 1), [R("w4b", 0, 4096)], [s_4, a_s], 1, 1 << 19)
+    for f, b in (("f1", "w1b"), ("f0", "own0"), ("f4", "w4b")):
+        dma("g", R(f, 0, 4096), R(b, 0, 4096), [a_4])
+
+    iota(R("ci", 0, 8), [[-16, 8]], 0, 1)
+    iota(R("ci", 8, 9), [[0, 1]], 0, 1)
+    iota(R("wt1", 0, 256), [[-16, 256]], 4080, 0)
+    iota(R("cf", 16, 32), [[1, 16]], 0, 0)
+    iota(R("cf", 32, 32 + NC), [[0, NC // 2], [-64, 2]], 0, 0)
+    ts(R("ci", 16, 24), R("ci", 0, 8), 4, "arith_shift_right")
+    ts(R("cf", 0, 8), R("ci", 16, 24), 0.0, "is_equal")
+    ts(R("ci", 9, 10), R("ci", 8, 9), 15, "bitwise_and")
+    ts(R("cf", 8, 9), R("ci", 9, 10), -4.0, "mult")
+    cp(R("cf", 10, 11), R("ci", 9, 10))
+    iota(R("cf", 48, 48 + NC), [[16, NC]], 0, 0)
+    ms(R("cf", 9, 10), 257.0)
+    ms(R("mm", 0, 2048), 0.0)
+    for g in range(8):
+        v = R("mm", 16 * g, 16 * g + 129 * 15 + 1, 129)
+        ts(v, v, R("cf", g, g + 1), "add")
+    ms(R("cf", 11, 12), -1280.0)
+    later = [iota(R("ktab", 1024 * h, 1024 * h + 1024), [[1, 8], [0, 128]], 8 * h, 0) for h in (0, 1)]
+    later += [iota(R("cu1", 1024 * h, 1024 * h + 1024), [[0, 1024]], 0, 0) for h in (0, 1)]
+    later += [iota(R("wt1", 3840 + 768 * h, 3840 + 768 * h + 768), [[2, 3], [-16, 256]], 4081 + 6 * h, 0) for h in range(5)]
+    for i in later:
+        ops[i]["late"] = s_s
+    ms(R("cu0", 0, 2048), 0.0)
+    ts(R("cub0", 0, 128), R("misc", 4, 132), 128.0, "mult")
+    dma("y", R("cu0", 0, 2048, 1, 0, 128, 16), R("cub0", 0, 128))
+    ts(R("cub1", 0, 128), R("misc1", 4, 132), 128.0, "mult")
+    dma("y", R("cu1", 0, 2048, 1, 0, 128, 16), R("cub1", 0, 128))
+    ms(R("ones", 0, 128), 1.0)
+    i_id = add("g", "sel", (R("ident", 0, 128), R("ones", 0, 128)), [R("ones", 0, 128)], [R("ident", 0, 128)])
+    ops[i_id]["sdeps"].append(s_4)
+    ts(R("wt1", 256, 512), R("wt1", 0, 256), 2.0, "add")
+    ts(R("wt1", 512, 1024), R("wt1", 0, 512), 4.0, "add")
+    ts(R("wt1", 1024, 2048), R("wt1", 0, 1024), 8.0, "add")
+    ts(R("wt1", 2048, 2944), R("wt1", 0, 896), 16.0, "add")
+    ts(R("wt1", 2944, 3840), R("wt1", 896, 1792), 16.0, "add")
+    blocks = [(0, 256), (256, 1024), (1024, 2048), (2048, 2944), (2944, 3840)]
+    for a, b in blocks:
+        act(R("wt0", a, b), R("wt1", a, b), scale=R("misc", 1, 2))
+        if a < WT4_V:
+            ts(R("wt4", a, b), R("wt1", a, b), R("co4", 1, 2), "mult", R("co4", 0, 1), "add")
+        else:
+            act(R("wt4", a, b), R("wt1", a, b), scale=R("co4", 1, 2))
+            act(R("wt4", a, b), R("wt4", a, b), bias=R("co4", 0, 1))
+    for a, b in blocks:
+        act(R("wt0", a, b), R("wt0", a, b), bias=R("misc", 0, 1))
+    for a, b in blocks[:3]:
+        ts(R("wt1", a, b), R("wt1", a, b), R("misc1", 1, 2), "mult", R("misc1", 0, 1), "add")
+    for a in range(2048, 7680, 512):
+        act(R("wt1", a, a + 512), R("wt1", a, a + 512), scale=R("misc1", 1, 2))
+        act(R("wt1", a, a + 512), R("wt1", a, a + 512), bias=R("misc1", 0, 1))
+
+    PP, VC0, C128, KQ, XI, HOME, DF, T1, T2, NL, N2, VX = range(12)
+    OCOL, OXI, OCOL1, OKQ, OXR, OC0, OX0, OKF = range(8)
+
+    def st(s, i, n=1):
+        return R("st%d" % s, NC * i, NC * (i + n))
+
+    def of(s, i, n=1):
+        return R("of%d" % s, NC * i, NC * (i + n))
+
+    def di(s, i):
+        return R("di%d" % s, NC * i, NC * (i + 1))
+
+    def B(name, s, h=0):
+        return R("%s%d" % (name, s), NW * h, NW * (h + 1))
+
+    def slot(name, s, e, j=0):
+        return R("%s%d" % (name, s), 5 * NC * j + e, 5 * NC * (j + 1) - 4 + e, 5)
+
+    def cnt(s):
+        return R("pc%d" % s, NW, NW + NC)
+
+    def cast_of(s, table):
+        act(B("cug", s), IND(R(table, 0, 2048), of(s, OCOL)))
+        count(cst(s, C128), "cug%d" % s)
+
+    def cst(s, c):
+        return R("pc%d" % s, NW + NC, NW + 2 * NC) if c == C128 else st(s, c)
+
+    def first_col(s, c, half=False):
+        tt(st(s, VC0), cst(s, c), slot("sa", s, 1), "subtract")
+        if half:
+            ts(of(s, OC0), st(s, VC0), 0.5, "mult")
+        else:
+            cp(of(s, OC0), st(s, VC0))
+
+    def Qs(s, h, k):
+        return R(("qt%d", "qs%d")[h] % s, 256 * k, 256 * k + NW)
+
+    def PS(s, h, k):
+        return B(("pb", "pd")[h], s, k)
+
+    def fslot(name, s, e):
+        return R("%s%d" % (name, s), e, 4 * NC - 3 + e, 4)
+
+    def vote(s, tv, sv, w, b0):
+        ds = Qs(s, 1, 3)
+        tt(ds, sv, B("s1", s) if sv[0] == "ind" else B("pa", s, 1), "subtract")
+        act(B("wg", s), w)
+        act(B("rr", s), ds, scale=b0)
+        tt(B("pc", s), tv, B("pa", s), "subtract")
+        tt(B("pc", s), B("wg", s), B("pc", s), "mult")
+        tt(B("yes", s), B("pc", s), B("rr", s), "is_gt")
+        count(cnt(s), "yes%d" % s)
+
+    def levels(s, tab, half):
+        for h in (1, 0):
+            win = R(tab, 2048 * h, 2048 * h + 2048)
+            act(Qs(s, h, 0), IND(win, of(s, OCOL)))
+            act(PS(s, h, 0), Qs(s, h, 0))
+            if FUSE_N[h]:
+                tt(Qs(s, h, 1), IND(win, of(s, OCOL1)), Qs(s, h, 0), "subtract")
+                if half:
+                    act(Qs(s, h, 2), Qs(s, h, 1), scale=0.5)
+                    tt(Qs(s, h, 4), Qs(s, h, 2), PS(s, h, 0), "add")
+                act(PS(s, h, 1), Qs(s, h, 1))
+            else:
+                act(Qs(s, h, 1), IND(win, of(s, OCOL1)))
+                tt(PS(s, h, 1), Qs(s, h, 1), PS(s, h, 0), "subtract")
+                if half:
+                    act(Qs(s, h, 2), PS(s, h, 1), scale=0.5)
+                    tt(Qs(s, h, 4), Qs(s, h, 2), PS(s, h, 0), "add")
+
+    def at_depth(s, off, start, out):
+        act(Qs(s, 0, 3), IND(R("ktab", start, 2048), off), scale=0.0625)
+        for h in (1, 0):
+            tt(Qs(s, h, 2), Qs(s, 0, 3), PS(s, h, 1), "mult")
+            tt(out[h], Qs(s, h, 2), PS(s, h, 0), "add")
+
+    def chosen(s, h):
+        return IND(R(("qt%d", "qs%d")[h] % s, 0, 7 * 256), of(s, OKF))
+
+    def hop(s, tab, wt, wend, co, c, nxt, even=None):
+        phase(s, "")
+        b0 = R(co, 2, 3)
+        for j in range(4):
+            step = 8 >> j
+            oc, ox = (OC0, OX0) if j == 0 else (OCOL, OXI)
+            wt_, ws_ = (R(even, 0, 1024), R(even, 1024, 2048)) if even else (R(tab, 0, 2048), R(tab, 2048, 4096))
+            act(B("tg", s), IND(wt_, of(s, oc)))
+            sv = IND(ws_, of(s, oc))
+            if not FUSE_S[j]:
+                act(Qs(s, 1, 1), sv)
+                sv = Qs(s, 1, 1)
+            vote(s, B("tg", s), sv, IND(R(wt, 0, wend[0]), of(s, ox)), b0)
+            ts(slot("sb", s, 0, j), cnt(s), 8.5, "is_ge", 2.0 * step, "mult")
+            o, x, y = R("so%d" % s, 0, 5 * NC), R("sa%d" % s, 0, 5 * NC), R("sb%d" % s, 5 * NC * j, 5 * NC * (j + 1))
+            add("v", "scan", (o, x, y, "subtract", "min"), [x, y], [o])
+            if even and j < 3:
+                ts(of(s, OCOL), slot("so", s, 4), float(step), "subtract", 0.5, "mult")
+            else:
+                ts(of(s, OCOL), slot("so", s, 4), float(step), "subtract")
+            if j == 3:
+                cp(of(s, OCOL1), slot("so", s, 4))
+            ts(of(s, OXI), slot("so", s, 3), step - 1.0, "add")
+            act(slot("sa", s, 1), slot("so", s, 2), scale=-1.0, bias=R("cf", 16 + step, 17 + step))
+        if nxt is not None:
+            act(st(s, NL), slot("so", s, 2), scale=-1.0, bias=R("cf", 9, 10))
+            act(st(s, N2), slot("so", s, 2), scale=-2.0, bias=R("cf", 9, 10))
+        levels(s, tab, True)
+        vote(s, Qs(s, 0, 4), Qs(s, 1, 4), IND(R(wt, 1024, wend[1]), of(s, OXI)), b0)
+        if PICK2:
+            for h in (1, 0):
+                act(Qs(s, h, 6), Qs(s, h, 1) if FUSE_N[h] else PS(s, h, 1), scale=1.5)
+            ts(fslot("fb", s, 0), cnt(s), 8.5, "is_ge", 1024.0, "mult")
+            tt(st(s, KQ), fslot("fa", s, 3), fslot("fb", s, 0), "add")
+            tt(st(s, XI), slot("so", s, 3), fslot("fb", s, 0), "add")
+            cp(of(s, OKQ, 2), st(s, KQ, 2))
+        elif SLIM & 1:
+            ts(st(s, KQ), cnt(s), 8.5, "is_ge", 1024.0, "mult")
+            tt(st(s, XI), slot("so", s, 3), st(s, KQ), "add")
+            cp(of(s, OKQ, 2), st(s, KQ, 2))
+            act(fslot("fb", s, 0), st(s, KQ))
+        else:
+            ts(of(s, OKQ), cnt(s), 8.5, "is_ge", 1024.0, "mult")
+            ts(fslot("fb", s, 0), cnt(s), 8.5, "is_ge", 1024.0, "mult")
+            tt(st(s, XI), slot("so", s, 3), fslot("fb", s, 0), "add")
+            cp(of(s, OXR), st(s, XI))
+        if nxt == "home":
+            first_col(s, HOME)
+        elif nxt is not None:
+            cast_of(s, nxt)
+            first_col(s, C128)
+        for j, h in ((1, 4), (2, 2)):
+            if j == 1 and PICK2:
+                for x in (1, 0):
+                    act(Qs(s, x, 1), IND(R(("qt%d", "qs%d")[x] % s, 512, 7 * 256), of(s, OKQ)), scale=0.5)
+                    tt(Qs(s, x, 5), Qs(s, x, 1), PS(s, x, 0), "add")
+            else:
+                at_depth(s, of(s, OKQ), 128 * h, [Qs(s, 0, 4 + j), Qs(s, 1, 4 + j)])
+            vote(s, Qs(s, 0, 4 + j), Qs(s, 1, 4 + j), IND(R(wt, 128 * h, wend[1]), of(s, OXR)), b0)
+            if j == 1:
+                ts(st(s, PP), cnt(s), 8.5, "is_ge", 128.0 * h, "mult")
+                tt(st(s, KQ), fslot("fb", s, 0), st(s, PP), "add")
+                tt(st(s, XI), st(s, XI), st(s, PP), "add")
+                cp(of(s, OKQ, 2), st(s, KQ, 2))
+                act(fslot("fb", s, 1), st(s, PP), scale=2.5)
+            else:
+                ts(fslot("fb", s, 2), cnt(s), 8.5, "is_ge", 1536.0, "mult")
+                if nxt is None or SLIM & 2:
+                    add("s", "act", (st(s, PP), fslot("fb", s, 2), "relu", R("cf", 11, 12)), [fslot("fb", s, 2), R("cf", 11, 12)], [st(s, PP)])
+                else:
+                    ts(st(s, PP), cnt(s), 8.5, "is_ge", 128.0 * h, "mult")
+                tt(st(s, KQ), st(s, KQ), st(s, PP), "add")
+        o, x, y = R("fo%d" % s, 0, 4 * NC), R("fa%d" % s, 0, 4 * NC), R("fb%d" % s, 0, 4 * NC)
+        add("v", "scan", (o, x, y, "add", "max"), [x, y], [o])
+        cp(of(s, OKF), fslot("fo", s, 3))
+        if nxt is not None:
+            tt(st(s, VX), st(s, KQ), st(s, N2), "add")
+            cp(of(s, OX0), st(s, VX))
+            tt(slot("sa", s, 3), st(s, KQ), st(s, NL), "add")
+            tt(slot("sa", s, 4), slot("sa", s, 3), cst(s, HOME if nxt == "home" else C128), "add")
+            act(B("s1", s), chosen(s, 1))
+            act(B("rr", s), chosen(s, 0))
+            act(B("pa", s), B("rr", s))
+            act(B("pa", s, 1), B("s1", s))
+
+    def finish(s, rnd, out):
+        for h in (1, 0):
+            a = 2048 * h + 4 * NW * s + rnd
+            old = R("own0", a, a + 4 * NW - 3, 4)
+            df = B(("tg", "wg")[h], s)
+            tt(df, chosen(s, h), old, "subtract")
+            act(PS(s, h, 0), df, scale=0.25)
+            tt(R(out, 512 * h + NW * s, 512 * h + NW * (s + 1)), PS(s, h, 0), old, "add")
+
+    def depart(s):
+        ts(st(s, T1), slot("sa", s, 1), -16.0, "mult")
+        tt(st(s, T1), st(s, T1), di(s, 0), "subtract")
+        ts(st(s, T2), st(s, KQ), 1.0 / 128, "mult")
+        tt(di(s, 1), st(s, T1), st(s, T2), "add")
+        ts(di(s, 2), di(s, 1), 1, "arith_shift_right")
+        tt(di(s, 0), di(s, 0), di(s, 2), "add")
+
+    def spread(f, src, s, h, on):
+        a = 2048 * h + 4 * NW * s
+        (cp if on == "v" else act)(R(f, a, a + 4 * NW - 3, 4), R(src, 512 * h + NW * s, 512 * h + NW * (s + 1)))
+
+    def start(s, half):
+        tt(slot("sa", s, 3), st(s, T1), slot("sa", s, 1), "add")
+        tt(st(s, VX), slot("sa", s, 3), slot("sa", s, 1), "add")
+        ts(of(s, OX0), st(s, VX), 1.0, "subtract")
+        tt(st(s, VC0), st(s, HOME), slot("sa", s, 1), "subtract")
+        cp(of(s, OCOL), st(s, VC0))
+        ts(of(s, OCOL1), st(s, VC0), 1.0, "add")
+        cast_of(s, "cu0")
+        first_col(s, C128, half)
+        tt(slot("sa", s, 4), slot("sa", s, 3), cst(s, C128), "add")
+
+    for s in range(NST):
+        cur[0] = s
+        ms(R("sa%d" % s, 0, 5 * NC), BIG)
+        ms(slot("sa", s, 2), 0.0)
+        if s == 0:
+            ms(R("sb0", 0, 20 * NC), BIG)
+            for j in range(4):
+                ms(slot("sb", s, 1, j), -float(8 >> j))
+                ms(slot("sb", s, 2, j), 126.0 + (8 >> j))
+            for x in range(1, NST):
+                act(R("sb%d" % x, 0, 20 * NC), R("sb0", 0, 20 * NC))
+        iota(st(s, HOME), [[128, NC // 2], [0, 2]], 4 * NW * s, 0)
+        ts(slot("sa", s, 1), R("cf", 32, 32 + NC), R("cf", 8, 9), "add")
+        ts(di(s, 0), slot("sa", s, 1), -16.0, "mult")
+        ms(st(s, T1), 256.0)
+        start(s, True)
+        act(B("pa", s), R("own0", 4 * NW * s, 4 * NW * (s + 1) - 3, 4))
+        act(B("s1", s), R("own0", 2048 + 4 * NW * s, 2048 + 4 * NW * (s + 1) - 3, 4))
+        act(B("pa", s, 1), B("s1", s))
+        ms(R("fa%d" % s, 0, 4 * NC), 0.0)
+        ms(fslot("fa", s, 0), -BIG)
+        ts(fslot("fa", s, 3), R("cf", 48, 48 + NC), R("cf", 10, 11), "add")
+        ms(R("fb%d" % s, 0, 4 * NC), -BIG)
+    for s in range(NST):
+        hop(s, "w1b", "wt1", (256, 2048), "misc1", C128, "cu1", "we1")
+        hop(s, "w4b", "wt4", (3840, 3840), "co4", C128, "home")
+        hop(s, "own0", "wt0", (3840, 3840), "misc", HOME, None)
+        finish(s, 0, "newb")
+    phase(None, "m")
+    arr = []
+    for s in range(NST):
+        sn = send("mid%d" % s, [R("newb", NW * s, NW * s + NW), R("newb", 512 + NW * s, 512 + NW * s + NW)], 1 << 18)
+        for h in (0, 1):
+            arr.append(arrive("an%d" % (2 * s + h), (1, 0), [R("new1", 512 * h + NW * s, 512 * h + NW * (s + 1))], [sn], 1, 1 << 17))
+    s_n = send("mid4", [R("newb", 0, 1024)], 0, arr)
+    arrive("an4", (0, 1), [R("new4", 0, 1024)], [s_n], 0, 1 << 19)
+    dma("y", R("new4s", 0, 1024, 1, 0, 112), R("new4", 0, 1024, 1, 16, 128))
+    dma("y", R("new4s", 0, 1024, 1, 112, 128), R("new4", 0, 1024, 1, 0, 16))
+    for s in range(NST):
+        for h in (0, 1):
+            spread("f0", "newb", s, h, "s")
+            spread("f1", "new1", s, h, "s" if h else "v")
+            spread("f4", "new4s", s, h, "s")
+    for s in range(NST):
+        cur[0] = s
+        depart(s)
+        ts(di(s, 1), di(s, 0), 4, "arith_shift_right")
+        ts(slot("sa", s, 1), di(s, 1), -1.0, "mult")
+        ts(di(s, 2), di(s, 0), 15, "bitwise_and")
+        ts(st(s, KQ), di(s, 2), 128.0, "mult")
+        cp(of(s, OKF), st(s, KQ))
+        ts(di(s, 3), di(s, 0), 1, "bitwise_and")
+        ts(st(s, T2), di(s, 3), 3712.0, "mult", 256.0, "add")
+        tt(st(s, T1), st(s, KQ), st(s, T2), "add")
+        start(s, False)
+        levels(s, "f0", False)
+        at_depth(s, of(s, OKF), 0, [B("pa", s), B("s1", s)])
+        act(B("pa", s, 1), B("s1", s))
+    for s in range(NST):
+        hop(s, "f1", "wt1", (7680, 7680), "misc1", C128, "cu1")
+        hop(s, "f4", "wt4", (3840, 3840), "co4", C128, "home")
+        hop(s, "f0", "wt0", (3840, 3840), "misc", HOME, None)
+        finish(s, 1, "outb")
+        for h, y in enumerate(("yt", "ys")):
+            dma("y", R(y, NW * s, NW * s + NW), R("outb", 512 * h + NW * s, 512 * h + NW * (s + 1)))
+        depart(s)
+        cp(st(s, DF), di(s, 0))
+        g = [(R("pa%d" % s, b, NW, 16, 0, 8), R("ident", b, 128, 16), st(s, DF), True, True) for b in range(16)]
+        add("t", "mm", g, [R("ident", 0, 128), st(s, DF)], [B("pa", s)])
+        act(R("ydb", NW * s, NW * s + NW, 1, 0, 8), R("pa%d" % s, 0, NW, 1, 0, 8))
+        dma("s", R("yd", NW * s, NW * s + NW, 1, 0, 8), R("ydb", NW * s, NW * s + NW, 1, 0, 8))
+    return ops
+
+
+def order(ops, P, U):
+    n = len(ops)
+    cs = [cost(o, P) for o in ops]
+    succ = [[] for _ in ops]
+    left = [0] * n
+    for i, o in enumerate(ops):
+        for d in o["deps"] + o["sdeps"]:
+            succ[d].append(i)
+            left[i] += 1
+    pri = [0.0] * n
+    behind = [[] for _ in ops]
+    for i, o in enumerate(ops):
+        for d in o["soft"]:
+            behind[d].append(i)
+    for i in range(n - 1, -1, -1):
+        pri[i] = cs[i][1] + max([pri[j] + P["wake"] for j in succ[i]] + [pri[j] for j in behind[i]] + [0.0])
+    x = U["seed"]
+    for i, o in enumerate(ops):
+        x = (x * 1103515245 + 12345) % 2147483648
+        pri[i] += U["noise"] * x / 2147483648 + (U["lead"] if o["s"] == 0 else 0.0) + 1e9 * o.get("first", 0) + U["role"].get(o["role"], 0)
+    ready = [0.0] * n
+    pool = {e: [] for e in "vstgy"}
+    free = {e: 0.0 for e in "vstgy"}
+    seq, end = [], [0.0] * n
+    held = {}
+    for i, o in enumerate(ops):
+        for j in o["soft"] + ([o["late"]] if "late" in o else []):
+            held.setdefault(j, []).append(i)
+            left[i] += 1
+
+    def done(i):
+        for j in succ[i]:
+            same = ops[j]["e"] == ops[i]["e"] and ops[i]["k"] not in ("dma", "send")
+            ready[j] = max(ready[j], end[i] + (P["same"] if same else P["wake"]))
+            left[j] -= 1
+            if left[j] == 0:
+                enter(j)
+        for j in held.get(i, []):
+            left[j] -= 1
+            if left[j] == 0:
+                enter(j)
+
+    def enter(j):
+        if ops[j]["e"] is None:
+            end[j] = ready[j] + cs[j][1]
+            seq.append(j)
+            done(j)
+        else:
+            pool[ops[j]["e"]].append(j)
+
+    for i in [i for i in range(n) if left[i] == 0]:
+        enter(i)
+    while len(seq) < n:
+        t, e = min((max(free[e], min(ready[j] for j in pool[e])), e) for e in pool if pool[e])
+        i = max((j for j in pool[e] if ready[j] <= t + U["look"]), key=lambda j: (pri[j], -j))
+        t = max(t, ready[i])
+        pool[e].remove(i)
+        free[e] = t + cs[i][0]
+        end[i] = t + cs[i][1]
+        seq.append(i)
+        done(i)
+    return seq, end
+
+
+INORDER = 1
+POOL = {"v": 1, "s": 1, "t": 1, "g": 1} if INORDER else {"v": 32, "s": 32, "t": 8, "g": 6}
+
+
+def plan(U):
+    ops = build()
+    seq, end = order(ops, PAR, U)
+    known = {e: 0 for e in "vstgy"}
+    K, waits, raised, before, pre = {}, {}, set(), {}, {e: 0 for e in "vstgy"}
+    for i in seq:
+        e = ops[i]["e"]
+        if e is None:
+            K[i] = 0
+            continue
+        w = []
+        for d in sorted(ops[i]["deps"], key=lambda d: -end[d]):
+            if not known[e] >> d & 1:
+                w.append(d)
+                raised.add(d)
+                known[e] |= K[d] | (1 << d) | before.get(d, 0)
+        K[i], waits[i] = known[e], w
+        if INORDER and ops[i]["k"] not in ("dma", "send"):
+            before[i] = pre[e]
+            pre[e] |= (1 << i) | K[i]
+    sem, names, turn, last, tail = {}, [], {e: 0 for e in POOL}, {}, []
+    for i in seq:
+        o = ops[i]
+        if o["k"] == "dma":
+            names.append("d%d" % len(names))
+            sem[i] = (names[-1], 16)
+            if i not in raised:
+                tail.append(i)
+        elif o["k"] not in ("arr", "send") and i in raised:
+            e = o["e"]
+            nm = "%s%d" % (e, turn[e] % POOL[e])
+            sem[i] = (nm, turn[e] // POOL[e] + 1)
+            turn[e] += 1
+            if not INORDER and nm in last and not K[i] >> last[nm] & 1:
+                waits[i].append(last[nm])
+            last[nm] = i
+    names += ["%s%d" % (e, k) for e in POOL for k in range(POOL[e])]
+    return ops, seq, waits, sem, names, tail, end
+
+
+OPS, SEQ, WAITS, SEM, _NAMES, TAIL, END = plan(TUNE)
+SEMAPHORES = _NAMES + ["am0", "am1", "am4", "ae0", "ae1", "ab0", "ab1", "ab4", "an0", "an1", "an2", "an3", "an4",
+                       "sent", "rm", "re", "rb", "rf", "rn"]
+
+
+def bits(es):
+    return sum(1 << e for e in es)
+
+
+def relays(T, topo, core, dst):
+    cs = [c for c in topo.cores_of(core) if c != core and T.rank_of(c) is None and topo.may_write(c, dst)]
+    near = [c for c in cs if topo.die(c) == topo.die(core)]
+    far = [c for c in cs if topo.die(c) != topo.die(core)]
+    return [near[0], far[0], near[1], far[1]]
+
+
+def piece(T, kind, k, landed):
+    if kind == "m":
+        return T["misc1" if landed else "misc"][:, 33 * k:33 * k + 33]
+    if kind == "e":
+        return T["we1" if landed else "we0"][:, 512 * k:512 * k + 512]
+    if kind == "b":
+        return T["w1b" if landed else "own0"][:, 1024 * k:1024 * k + 1024]
+    if kind == "f":
+        return T["w4b" if landed else "stage4"][:, 2048 * k:2048 * k + 2048]
+    a = 512 * (k % 2) + NW * (k // 2)
+    return T["new1" if landed else "newb"][:, a:a + NW]
+
+
+def relay_program(g, core, T, topo, src, down, far, k):
+    on, off = topo.engines(src, core), topo.engines(src, far)
+    rest = len(on) - len(off)
+    steps = [("m", k, rest // NREL, down, "am0" if k == 0 else "am1"), ("e", k, len(on) // 2, down, "ae%d" % (k // 2)),
+             ("b", (k + 2) % NREL, len(on) // 2, down, "ab%d" % (1 - k // 2))]
+    if k == 1:
+        steps.append(("f", 1, rest, far, "ab4"))
+    steps.append(("n", k, len(on) // 2, down, "an%d" % k))
+    total = 0
+    for kind, j, n, dst, sem in steps:
+        rid, pid = topo.addr(dst, core)
+        g.wait_ge(T.sem["r" + kind], n)
+        p = piece(T, kind, j, True)
+        g.remote_dma(p, p, T.sem[sem], T.sem.sent, pid, rid, topo.mask(core, dst))
+        total += len(topo.engines(core, dst))
+    g.wait_ge(T.sem.sent, total)
+
+
+def rank_program(g, core, T, topo):
+    N = len(T.cores)
+    rank = T.rank_of(core)
+    if rank is None:
+        for r, c in enumerate(T.cores):
+            if c in topo.cores_of(core):
+                down, far = T.cores[(r - 1) % N], T.cores[(r - 4) % N]
+                rel = relays(T, topo, c, down)
+                if core in rel:
+                    relay_program(g, core, T, topo, c, down, far, rel.index(core))
+        return
+    down, far = T.cores[(rank - 1) % N], T.cores[(rank - 4) % N]
+    rel = relays(T, topo, core, down)
+    on, off = topo.engines(core, rel[0]), topo.engines(core, far)
+    only_on = [e for e in on if e not in off]
+    up = T.cores[(rank + 1) % N]
+    n_in = len(topo.engines(relays(T, topo, up, core)[0], core))
+    n_far = len(topo.engines(T.cores[(rank + 4) % N], core))
+    Q = {"v": g.vector, "s": g.scalar, "t": g.tensor, "g": g, "y": g.sync}
+    A, F = AluOpType, ActivationFunctionType
+    alu = {"add": A.add, "subtract": A.subtract, "mult": A.mult, "max": A.max, "min": A.min, "is_ge": A.is_ge, "is_gt": A.is_gt,
+           "is_equal": A.is_equal, "arith_shift_right": A.arith_shift_right, "bitwise_and": A.bitwise_and}
+    sent = [0]
+
+    def ap(r):
+        if not isinstance(r, tuple):
+            return r
+        if r[0] == "ind":
+            return ap(r[1]).indirect(ap(r[2]))
+        p = slice(r[4], r[5]) if r[6] == 1 else slice(r[4], r[5], r[6])
+        c = slice(r[1], r[2]) if r[3] == 1 else slice(r[1], r[2], r[3])
+        return T[r[0]][p, c]
+
+    def tr(dst, src_ap, dst_ap, sem, es):
+        rid, pid = topo.addr(dst, core)
+        sent[0] += len(es)
+        return RemoteDMATransfer(dst_ids=[DstId(rid=rid, pnc=pid)], dma_engine_mask=bits(es), remote_sem=T.sem[sem], src=src_ap, dst=dst_ap)
+
+    def do_send(what):
+        if what == "misc":
+            few = len(only_on) // NREL
+            ts_ = [tr(rel[k], piece(T, "m", k, False), piece(T, "m", k, True), "rm", only_on[few * k:few * k + few]) for k in range(NREL)]
+            ts_.append(tr(far, T.misc[:, 0:33], T.misc4[:, 0:33], "am4", off))
+        elif what == "bulk4":
+            ts_ = [tr(far, piece(T, "f", 0, False), piece(T, "f", 0, True), "ab4", off),
+                   tr(rel[1], piece(T, "f", 1, False), piece(T, "f", 1, True), "rf", only_on)]
+        elif what == "mid4":
+            ts_ = [tr(far, T.newb[:], T.new4[:], "an4", off)]
+        else:
+            kind, h = {"b": "b", "e": "e", "m": "n"}[what[0]], int(what[-1])
+            ts_ = [tr(rel[(2 * h + j + (2 if kind == "b" else 0)) % NREL], piece(T, kind, 2 * h + j, False), piece(T, kind, 2 * h + j, True), "r" + kind, on[j::2])
+                   for j in range(2)]
+        g.remote_dma_fused(ts_, local_sem=T.sem.sent)
+
+    for i in SEQ:
+        o = OPS[i]
+        e, k, a = o["e"], o["k"], o["a"]
+        if e is None:
+            continue
+        q = Q[e]
+        for d in WAITS[i]:
+            if OPS[d]["k"] == "arr":
+                nm, n = OPS[d]["a"][0], OPS[d]["a"][1]
+                q.wait_ge(T.sem[nm], n[0] * n_in + n[1] * n_far)
+            else:
+                q.wait_ge(T.sem[SEM[d][0]], SEM[d][1])
+        if k == "send":
+            do_send(a[0])
+            continue
+        if k == "tt":
+            ins = q.tensor_tensor(ap(a[0]), ap(a[1]), ap(a[2]), alu[a[3]])
+        elif k == "ts":
+            if a[5] is None:
+                ins = q.tensor_scalar(ap(a[0]), ap(a[1]), ap(a[2]), None, alu[a[4]])
+            else:
+                ins = q.tensor_scalar(ap(a[0]), ap(a[1]), ap(a[2]), ap(a[3]), alu[a[4]], alu[a[5]])
+        elif k == "scan":
+            ins = q.tensor_tensor_scan(ap(a[0]), ap(a[1]), ap(a[2]), 0.0, alu[a[3]], alu[a[4]])
+        elif k == "cp":
+            ins = q.tensor_copy(ap(a[0]), ap(a[1]))
+        elif k == "ms":
+            ins = q.memset(ap(a[0]), a[1])
+        elif k == "act":
+            if a[2] == "relu":
+                ins = q.activation(ap(a[0]), ap(a[1]), F.Relu, bias=ap(a[3]))
+            elif a[3] is not None:
+                ins = q.activation(ap(a[0]), ap(a[1]), F.Identity, bias=ap(a[3]), scale=1.0 if a[2] is None else a[2])
+            elif a[2] is not None:
+                ins = q.activation(ap(a[0]), ap(a[1]), F.Copy, scale=ap(a[2]))
+            else:
+                ins = q.activation(ap(a[0]), ap(a[1]), F.Copy)
+        elif k == "mm":
+            for m in a:
+                ins = q.matmul(ap(m[0]), ap(m[1]), ap(m[2]), m[3], m[4])
+        elif k == "iota":
+            if SCRATCH[a[0][0]][2] == "int32":
+                ins = q.iota(ap(a[0]), a[1], a[2], a[3])
+            else:
+                ins = q.iota(ap(a[0]), a[1], a[2], a[3], allow_small_or_imprecise_dtypes=True)
+        elif k == "sel":
+            ins = q.affine_select(ap(a[0]), ap(a[1]), [[-1, 128]], A.is_equal, 0.0, 0, 1)
+        else:
+            ins = q.dma_start(ap(a[0]), ap(a[1]))
+        if i in SEM:
+            ins.then_inc(T.sem[SEM[i][0]], 16 if k == "dma" else 1)
+    for i in TAIL:
+        Q[OPS[i]["e"]].wait_ge(T.sem[SEM[i][0]], 16)
+    g.wait_ge(T.sem.sent, sent[0])

@@ -6,14 +6,21 @@ NW = 512 // NST
 NC = NW // 16
 NREL = 4
 FUSE_S = (1, 1, 1, 1)
-FUSE_N = (1, 1)
-PICK2 = 0
+FUSE_N = 1
+MERGE = 0
+FIN_V = 0
+PE0 = 0
 SLIM = 0
 NOWAR = 0
 WT4_V = 4096
-ROLE = {'vof10.4': 100, 'spb0256.1': 600, 'vqs01536.1': -2400, 'vof048.2': -600, 'vst1128.1': -1100, 'vqs1512.1': -3000, 'tpa10.1': -600, 'vfo10.1': -1200, 'avsb0242.1': 300, 'swg10.7': 600, 'avmisc0.1': -3000, 'vwg00.1': -300, 'vpc10.12': -3000, 'vst164.1': 600, 'vst116.1': -1200, 'vst096.1': -1200, 'vqt0256.1': 1200, 'sqs00.1': 1200, 'vpc10.13': -600, 'tpc0256.3': 600, 'avsa10.1': 3000, 'vpc00.10': 600, 'vfb02.1': 600, 'vof016.3': -3000, 'srr00.5': 300, 'vst1176.1': 1200, 'voutb256.1': -3000, 'vpc00.12': -100, 'vqt01536.1': 1200, 'spd0256.1': -100, 'sqs10.1': 3000, 'mspa0256.1': -1200, 'sfb11.1': 600, 'spb1256.1': -1200, 'srr10.4': -100, 'swg10.6': -1800, 'vpc10.11': -600, 'ssa11.2': -3600, 'ssa01.3': 100, 'avmm112.1': -600, 'ss110.1': -600, 'avmm48.1': -300, 'vst0112.1': -3000, 'vof064.1': 100, 'vso00.3': 300, 'vof196.1': -3000, 'ssa11.1': 3000, 'voutb512.1': 600, 'vst0176.1': -3000, 'vof148.1': -300, 'vsa03.1': -3000, 'spd00.1': 3000, 'vqs0768.1': -600, 'vof164.1': 3000, 'vof016.4': -300, 'vof116.2': 100, 'spd1256.1': -600}
-TUNE = dict(lead=1500.0, look=0.0, noise=0.0, seed=1, role=ROLE)
-PAR = dict(cyc=1.04, g=1.56, wake=120.0, same=60.0, pe=0.52, dma=2000.0, bw=160.0, call=900.0, leg=2500.0, link=45.0)
+ROLE = {'vq01024.1': -600, 'vso10.3': -1300, 'vof00.4': 1200, 'vyes10.4': 100, 'vq13328.2': -3000, 'mvq1768.1': -600, 'vso10.1': -100,
+        'vdi116.1': 300, 'vq03328.5': -1200, 'vpc00.2': 300, 'vpc00.6': -3000, 'vnew1512.1': 100, 'vpc10.2': -600, 'vst00.1': 300,
+        'spd0256.1': 1200, 'vfb00.1': -300, 'sst0144.1': -300, 'vpc10.11': -900, 'vyes10.7': 100, 'vpc00.4': -300, 'vpc10.13': -300,
+        'tpc0272.1': -600, 'vsb1240.1': 300, 'vfb12.1': 1200, 'mvdi132.1': 600, 'vpc10.7': -1200, 'vof132.1': -600, 'vpc10.3': -1200,
+        'swg10.2': 300, 'vq03328.7': -300, 'vof048.1': -1200, 'mvdi116.2': 1200, 'vdi10.1': -100, 'spd00.1': 300, 'vst148.1': 100,
+        'aswt01024.2': -600, 'mvq1512.1': 100, 'sq13072.1': -3000, 'vpc00.1': -1200, 'stg10.4': 600, 'srr10.6': -100}
+TUNE = dict(lead=2000.0, look=100.0, noise=0.0, seed=1, role=ROLE)
+PAR = dict(fix=0.0, fixs=0.0, fuse=0.0, cyc=0.95, g=1.56, wake=200.0, same=180.0, pe=0.5, dma=2000.0, bw=160.0, call=900.0, leg=2500.0, link=45.0)
 BIG = 1.0e6
 
 SCRATCH = {
@@ -30,17 +37,19 @@ SCRATCH = {
     "misc4": ("sbuf", [128, 33], "float32"), "co4": ("sbuf", [128, 4], "float32"),
     "newb": ("sbuf", [128, 1024], "float32"), "new1": ("sbuf", [128, 1024], "float32"),
     "new4": ("sbuf", [128, 1024], "float32"), "new4s": ("sbuf", [128, 1024], "float32"),
-    "outb": ("sbuf", [128, 1024], "float32"), "ydb": ("sbuf", [128, 512], "float32"),
+    "identb": ("sbuf", [128, 256], "bfloat16"), "nident": ("sbuf", [128, 128], "float32"),
     "ci": ("sbuf", [128, 32], "int32"), "cf": ("sbuf", [128, 64], "float32"),
 }
 for _s in range(NST):
-    for _n in ("tg", "wg", "rr", "s1"):
+    for _n in ("tg", "wg", "rr"):
         SCRATCH["%s%d" % (_n, _s)] = ("sbuf", [128, NW], "float32")
-    for _n in ("qt", "qs"):
-        SCRATCH["%s%d" % (_n, _s)] = ("sbuf", [128, 7 * 256], "float32")
+    SCRATCH["s1%d" % _s] = ("sbuf", [128, 2 * NW], "float32")
+    SCRATCH["q%d" % _s] = ("sbuf", [128, 14 * NW], "float32")
     for _n in ("fa", "fb", "fo"):
         SCRATCH["%s%d" % (_n, _s)] = ("sbuf", [128, 4 * NC], "float32")
     SCRATCH["yes%d" % _s] = ("sbuf", [128, NW], "bfloat16")
+    SCRATCH["tb%d" % _s] = ("sbuf", [128, NW], "bfloat16")
+    SCRATCH["lb%d" % _s] = ("sbuf", [128, 4 * NW], "bfloat16")
     SCRATCH["cug%d" % _s] = ("sbuf", [128, NW], "bfloat16")
     SCRATCH["st%d" % _s] = ("sbuf", [128, 12 * NC], "float32")
     SCRATCH["sa%d" % _s] = ("sbuf", [128, 5 * NC], "float32")
@@ -48,11 +57,13 @@ for _s in range(NST):
     SCRATCH["so%d" % _s] = ("sbuf", [128, 5 * NC], "float32")
     SCRATCH["di%d" % _s] = ("sbuf", [128, 4 * NC], "int32")
     SCRATCH["of%d" % _s] = ("sbuf", [128, 8 * NC], "uint16")
-    for _n in ("pa", "pb", "pc", "pd"):
+    for _n in ("pa", "pb", "pc", "pd")[:8 // NST]:
         SCRATCH["%s%d" % (_n, _s)] = ("psum", [128, 512], "float32")
 
 
 def R(name, a, b, step=1, p0=0, p1=128, ps=1):
+    if NST > 2 and name[:2] in ("pc", "pd"):
+        name, a, b = ("pa" if name[1] == "c" else "pb") + name[2:], a + 2 * NW, b + 2 * NW
     return (name, a, b, step, p0, p1, ps)
 
 
@@ -90,6 +101,10 @@ def cost(op, P):
             t = c * max(64, n / 2)
         else:
             t = c * max(64, n)
+        if a[1][0] != "ind":
+            t += P["fix"] + (P["fixs"] if k == "act" else 0.0)
+        elif k == "tt":
+            t += n * c * P["fuse"]
         return t, t
     if k == "ms":
         t = c * max(64, _n(a[0]) / (2 if _two(a[0]) else 1))
@@ -190,21 +205,24 @@ def build():
     ms(R("misc", 0, 4), 0.0)
     d0 = dma("y", R("cui", 0, 128), R("cu", 0, 2048, 1, 0, 8))
     dma("s", R("misc", 0, 3), R("co", 0, 3))
-    d1 = dma("y", R("own0", 0, 2048), R("te", 0, 2048))
-    d2 = dma("y", R("own0", 2048, 4096), R("sa", 0, 2048), ahead=1 << 19)
-    ops[d0]["first"], ops[d1]["first"], ops[d2]["first"] = 3, 2, 1
-    cp(R("misc", 4, 132), R("cui", 0, 128))
-    for h in (0, 1):
-        act(R("we0", 1024 * h, 1024 * h + 512), R("own0", 2048 * h, 2048 * h + 1024, 2))
-        cp(R("we0", 1024 * h + 512, 1024 * h + 1024), R("own0", 2048 * h + 1024, 2048 * h + 2048, 2))
+    ops[d0]["first"] = 5
+    for k in range(4):
+        d1 = dma("y", R("own0", 1024 * k, 1024 * k + 1024), R(("te", "sa")[k // 2], 1024 * (k % 2), 1024 * (k % 2) + 1024), ahead=k << 18)
+        ops[d1]["first"] = 4 - k
+    ops[cp(R("misc", 4, 132), R("cui", 0, 128))]["first"] = 1
     s_m = send("misc", [R("misc", 0, 132)], 1 << 16)
-    s_e0 = send("even0", [R("we0", 0, 1024)], 1 << 18)
-    s_e1 = send("even1", [R("we0", 1024, 2048)], 1 << 18)
+    s_e = []
+    for k in range(4):
+        ops[act(R("we0", 512 * k, 512 * k + 192), R("own0", 1024 * k, 1024 * k + 384, 2))]["first"] = 1
+        ops[cp(R("we0", 512 * k + 192, 512 * k + 512), R("own0", 1024 * k + 384, 1024 * k + 1024, 2))]["first"] = 1
+        s_e.append(send("even%d" % k, [R("we0", 512 * k, 512 * k + 512)], 1 << 17))
+        ops[s_e[k]]["late"] = s_e[k - 1] if k else s_m
+    s_e1 = s_e[3]
     arrive("am0", (1, 0), [R("misc1", 0, 33)], [s_m], 1, 0)
     arrive("am1", (3, 0), [R("misc1", 33, 132)], [s_m], 1, 0)
     arrive("am4", (0, 1), [R("misc4", 0, 33)], [s_m], 0, 0)
-    a_e0 = arrive("ae0", (2, 0), [R("we1", 0, 1024)], [s_e0], 1, 1 << 17)
-    a_e1 = arrive("ae1", (2, 0), [R("we1", 1024, 2048)], [s_e1], 1, 1 << 17)
+    a_e0 = arrive("ae0", (4, 0), [R("we1", 0, 1024)], [s_e[1]], 1, 1 << 16)
+    a_e1 = arrive("ae1", (4, 0), [R("we1", 1024, 2048)], [s_e[3]], 1, 1 << 16)
     s_t = send("bulk0", [R("own0", 0, 2048)], 1 << 19, behind=[])
     s_s = send("bulk1", [R("own0", 2048, 4096)], 1 << 19)
     ops[s_t]["late"], ops[s_s]["late"] = s_e1, s_t
@@ -249,7 +267,15 @@ def build():
     dma("y", R("cu1", 0, 2048, 1, 0, 128, 16), R("cub1", 0, 128))
     ms(R("ones", 0, 128), 1.0)
     i_id = add("g", "sel", (R("ident", 0, 128), R("ones", 0, 128)), [R("ones", 0, 128)], [R("ident", 0, 128)])
-    ops[i_id]["sdeps"].append(s_4)
+    if PE0:
+        cp(R("identb", 0, 128), R("ident", 0, 128))
+        ts(R("identb", 128, 256), R("ident", 0, 128), -1.0, "mult")
+        ts(R("nident", 0, 128), R("ident", 0, 128), -1.0, "mult")
+        for s in range(NST):
+            act(R("s1%d" % s, 0, NW), R("own0", 4 * NW * s, 4 * NW * (s + 1) - 3, 4))
+            ms(R("q%d" % s, 512, 1024), 0.0)
+    else:
+        ops[i_id]["sdeps"].append(s_4)
     ts(R("wt1", 256, 512), R("wt1", 0, 256), 2.0, "add")
     ts(R("wt1", 512, 1024), R("wt1", 0, 512), 4.0, "add")
     ts(R("wt1", 1024, 2048), R("wt1", 0, 1024), 8.0, "add")
@@ -307,50 +333,79 @@ def build():
             cp(of(s, OC0), st(s, VC0))
 
     def Qs(s, h, k):
-        return R(("qt%d", "qs%d")[h] % s, 256 * k, 256 * k + NW)
+        a = 2 * NW * (0, 1, 5, 6, 2, 3, 4)[k]
+        return R("q%d" % s, a, a + 2 * NW) if h == 2 else R("q%d" % s, a + NW * h, a + NW * h + NW)
 
     def PS(s, h, k):
-        return B(("pb", "pd")[h], s, k)
+        return R("%s%d" % (("pb", "pd")[k], s), 0, 2 * NW) if h == 2 else B(("pb", "pd")[k], s, h)
+
+    def both(bit):
+        return (2,) if MERGE & bit else (1, 0)
 
     def fslot(name, s, e):
         return R("%s%d" % (name, s), e, 4 * NC - 3 + e, 4)
 
     def vote(s, tv, sv, w, b0):
         ds = Qs(s, 1, 3)
-        tt(ds, sv, B("s1", s) if sv[0] == "ind" else B("pa", s, 1), "subtract")
+        tt(ds, sv, B("s1", s, 1) if sv[0] == "ind" else B("pa", s, 1), "subtract")
         act(B("wg", s), w)
         act(B("rr", s), ds, scale=b0)
-        tt(B("pc", s), tv, B("pa", s), "subtract")
+        if _two(tv):
+            add("t", "mm", [(B("pc", s), R("nident", 0, 128), B("s1", s), True, False)], [R("nident", 0, 128), B("s1", s)], [B("pc", s)])
+            add("t", "mm", [(B("pc", s), R("identb", 0, 128), tv, False, True)], [R("identb", 0, 128), tv, B("pc", s)], [B("pc", s)])
+        else:
+            tt(B("pc", s), tv, B("pa", s), "subtract")
         tt(B("pc", s), B("wg", s), B("pc", s), "mult")
         tt(B("yes", s), B("pc", s), B("rr", s), "is_gt")
         count(cnt(s), "yes%d" % s)
 
     def levels(s, tab, half):
+        if PE0 & 2 and _two(R(tab, 0, 1)):
+            for h in (1, 0):
+                win, lo, hi = R(tab, 2048 * h, 2048 * h + 2048), B("lb", s, h), B("lb", s, 2 + h)
+                act(lo, IND(win, of(s, OCOL)))
+                act(hi, IND(win, of(s, OCOL1)))
+            lo, hi, p, m = R("lb%d" % s, 0, 512), R("lb%d" % s, 512, 1024), R("identb", 0, 128), R("identb", 128, 256)
+            add("t", "mm", [(PS(s, 2, 0), p, lo, True, True)], [p, lo], [PS(s, 2, 0)])
+            add("t", "mm", [(PS(s, 2, 1), m, lo, True, False), (PS(s, 2, 1), p, hi, False, True)], [p, m, lo, hi], [PS(s, 2, 1)])
+            act(Qs(s, 2, 2), PS(s, 2, 1), scale=0.5)
+            tt(Qs(s, 2, 4), Qs(s, 2, 2), PS(s, 2, 0), "add")
+            act(Qs(s, 2, 0), lo)
+            return
         for h in (1, 0):
-            win = R(tab, 2048 * h, 2048 * h + 2048)
-            act(Qs(s, h, 0), IND(win, of(s, OCOL)))
+            act(Qs(s, h, 0), IND(R(tab, 2048 * h, 2048 * h + 2048), of(s, OCOL)))
+        for h in both(1):
             act(PS(s, h, 0), Qs(s, h, 0))
-            if FUSE_N[h]:
-                tt(Qs(s, h, 1), IND(win, of(s, OCOL1)), Qs(s, h, 0), "subtract")
-                if half:
-                    act(Qs(s, h, 2), Qs(s, h, 1), scale=0.5)
-                    tt(Qs(s, h, 4), Qs(s, h, 2), PS(s, h, 0), "add")
+        if FUSE_N:
+            for h in (1, 0):
+                tt(Qs(s, h, 1), IND(R(tab, 2048 * h, 2048 * h + 2048), of(s, OCOL1)), Qs(s, h, 0), "subtract")
+        else:
+            for h in (1, 0):
+                act(Qs(s, h, 1), IND(R(tab, 2048 * h, 2048 * h + 2048), of(s, OCOL1)))
+            tt(PS(s, 2, 1), Qs(s, 2, 1), PS(s, 2, 0), "subtract")
+        if half:
+            for h in both(2):
+                act(Qs(s, h, 2), Qs(s, h, 1) if FUSE_N else PS(s, h, 1), scale=0.5)
+            for h in both(4):
+                tt(Qs(s, h, 4), Qs(s, h, 2), PS(s, h, 0), "add")
+        if FUSE_N:
+            for h in both(1):
                 act(PS(s, h, 1), Qs(s, h, 1))
-            else:
-                act(Qs(s, h, 1), IND(win, of(s, OCOL1)))
-                tt(PS(s, h, 1), Qs(s, h, 1), PS(s, h, 0), "subtract")
-                if half:
-                    act(Qs(s, h, 2), PS(s, h, 1), scale=0.5)
-                    tt(Qs(s, h, 4), Qs(s, h, 2), PS(s, h, 0), "add")
 
     def at_depth(s, off, start, out):
         act(Qs(s, 0, 3), IND(R("ktab", start, 2048), off), scale=0.0625)
         for h in (1, 0):
             tt(Qs(s, h, 2), Qs(s, 0, 3), PS(s, h, 1), "mult")
+        for h in (both(8) if len(out) == 3 else (1, 0)):
             tt(out[h], Qs(s, h, 2), PS(s, h, 0), "add")
 
     def chosen(s, h):
-        return IND(R(("qt%d", "qs%d")[h] % s, 0, 7 * 256), of(s, OKF))
+        return IND(R("q%d" % s, NW * h, 10 * NW), of(s, OKF))
+
+    def small(o, x, scale, bias=None):
+        if SLIM & 4:
+            return ts(o, x, scale, "mult", bias, None if bias is None else "add")
+        return act(o, x, scale=scale, bias=bias)
 
     def hop(s, tab, wt, wend, co, c, nxt, even=None):
         phase(s, "")
@@ -359,12 +414,13 @@ def build():
             step = 8 >> j
             oc, ox = (OC0, OX0) if j == 0 else (OCOL, OXI)
             wt_, ws_ = (R(even, 0, 1024), R(even, 1024, 2048)) if even else (R(tab, 0, 2048), R(tab, 2048, 4096))
-            act(B("tg", s), IND(wt_, of(s, oc)))
+            tg = B("tb" if PE0 & 1 and _two(wt_) else "tg", s)
+            act(tg, IND(wt_, of(s, oc)))
             sv = IND(ws_, of(s, oc))
             if not FUSE_S[j]:
                 act(Qs(s, 1, 1), sv)
                 sv = Qs(s, 1, 1)
-            vote(s, B("tg", s), sv, IND(R(wt, 0, wend[0]), of(s, ox)), b0)
+            vote(s, tg, sv, IND(R(wt, 0, wend[0]), of(s, ox)), b0)
             ts(slot("sb", s, 0, j), cnt(s), 8.5, "is_ge", 2.0 * step, "mult")
             o, x, y = R("so%d" % s, 0, 5 * NC), R("sa%d" % s, 0, 5 * NC), R("sb%d" % s, 5 * NC * j, 5 * NC * (j + 1))
             add("v", "scan", (o, x, y, "subtract", "min"), [x, y], [o])
@@ -375,52 +431,44 @@ def build():
             if j == 3:
                 cp(of(s, OCOL1), slot("so", s, 4))
             ts(of(s, OXI), slot("so", s, 3), step - 1.0, "add")
-            act(slot("sa", s, 1), slot("so", s, 2), scale=-1.0, bias=R("cf", 16 + step, 17 + step))
+            small(slot("sa", s, 1), slot("so", s, 2), -1.0, R("cf", 16 + step, 17 + step))
         if nxt is not None:
-            act(st(s, NL), slot("so", s, 2), scale=-1.0, bias=R("cf", 9, 10))
-            act(st(s, N2), slot("so", s, 2), scale=-2.0, bias=R("cf", 9, 10))
+            small(st(s, NL), slot("so", s, 2), -1.0, R("cf", 9, 10))
+            small(st(s, N2), slot("so", s, 2), -2.0, R("cf", 9, 10))
         levels(s, tab, True)
         vote(s, Qs(s, 0, 4), Qs(s, 1, 4), IND(R(wt, 1024, wend[1]), of(s, OXI)), b0)
-        if PICK2:
-            for h in (1, 0):
-                act(Qs(s, h, 6), Qs(s, h, 1) if FUSE_N[h] else PS(s, h, 1), scale=1.5)
-            ts(fslot("fb", s, 0), cnt(s), 8.5, "is_ge", 1024.0, "mult")
-            tt(st(s, KQ), fslot("fa", s, 3), fslot("fb", s, 0), "add")
-            tt(st(s, XI), slot("so", s, 3), fslot("fb", s, 0), "add")
-            cp(of(s, OKQ, 2), st(s, KQ, 2))
-        elif SLIM & 1:
+        if SLIM & 1:
             ts(st(s, KQ), cnt(s), 8.5, "is_ge", 1024.0, "mult")
             tt(st(s, XI), slot("so", s, 3), st(s, KQ), "add")
             cp(of(s, OKQ, 2), st(s, KQ, 2))
-            act(fslot("fb", s, 0), st(s, KQ))
+            kq = st(s, KQ)
+            act(fslot("fb", s, 0), kq, scale=NW / 256)
         else:
+            kq = fslot("fb", s, 0) if NW == 256 else st(s, KQ)
             ts(of(s, OKQ), cnt(s), 8.5, "is_ge", 1024.0, "mult")
-            ts(fslot("fb", s, 0), cnt(s), 8.5, "is_ge", 1024.0, "mult")
-            tt(st(s, XI), slot("so", s, 3), fslot("fb", s, 0), "add")
+            ts(kq, cnt(s), 8.5, "is_ge", 1024.0, "mult")
+            tt(st(s, XI), slot("so", s, 3), kq, "add")
             cp(of(s, OXR), st(s, XI))
+            if NW != 256:
+                act(fslot("fb", s, 0), kq, scale=NW / 256)
         if nxt == "home":
             first_col(s, HOME)
         elif nxt is not None:
             cast_of(s, nxt)
             first_col(s, C128)
         for j, h in ((1, 4), (2, 2)):
-            if j == 1 and PICK2:
-                for x in (1, 0):
-                    act(Qs(s, x, 1), IND(R(("qt%d", "qs%d")[x] % s, 512, 7 * 256), of(s, OKQ)), scale=0.5)
-                    tt(Qs(s, x, 5), Qs(s, x, 1), PS(s, x, 0), "add")
-            else:
-                at_depth(s, of(s, OKQ), 128 * h, [Qs(s, 0, 4 + j), Qs(s, 1, 4 + j)])
+            at_depth(s, of(s, OKQ), 128 * h, [Qs(s, x, 4 + j) for x in range(3)])
             vote(s, Qs(s, 0, 4 + j), Qs(s, 1, 4 + j), IND(R(wt, 128 * h, wend[1]), of(s, OXR)), b0)
             if j == 1:
                 ts(st(s, PP), cnt(s), 8.5, "is_ge", 128.0 * h, "mult")
-                tt(st(s, KQ), fslot("fb", s, 0), st(s, PP), "add")
+                tt(st(s, KQ), kq, st(s, PP), "add")
                 tt(st(s, XI), st(s, XI), st(s, PP), "add")
                 cp(of(s, OKQ, 2), st(s, KQ, 2))
-                act(fslot("fb", s, 1), st(s, PP), scale=2.5)
+                small(fslot("fb", s, 1), st(s, PP), 6.0 * NW / 512)
             else:
-                ts(fslot("fb", s, 2), cnt(s), 8.5, "is_ge", 1536.0, "mult")
-                if nxt is None or SLIM & 2:
-                    add("s", "act", (st(s, PP), fslot("fb", s, 2), "relu", R("cf", 11, 12)), [fslot("fb", s, 2), R("cf", 11, 12)], [st(s, PP)])
+                ts(fslot("fb", s, 2), cnt(s), 8.5, "is_ge", 8.0 * NW, "mult")
+                if SLIM & 2:
+                    act(st(s, PP), fslot("fb", s, 2), scale=32.0 / NW)
                 else:
                     ts(st(s, PP), cnt(s), 8.5, "is_ge", 128.0 * h, "mult")
                 tt(st(s, KQ), st(s, KQ), st(s, PP), "add")
@@ -432,10 +480,13 @@ def build():
             cp(of(s, OX0), st(s, VX))
             tt(slot("sa", s, 3), st(s, KQ), st(s, NL), "add")
             tt(slot("sa", s, 4), slot("sa", s, 3), cst(s, HOME if nxt == "home" else C128), "add")
-            act(B("s1", s), chosen(s, 1))
-            act(B("rr", s), chosen(s, 0))
-            act(B("pa", s), B("rr", s))
-            act(B("pa", s, 1), B("s1", s))
+            act(B("s1", s, 1), chosen(s, 1))
+            act(B("s1", s), chosen(s, 0))
+            if MERGE & 16:
+                act(R("pa%d" % s, 0, 2 * NW), R("s1%d" % s, 0, 2 * NW))
+            else:
+                act(B("pa", s), B("s1", s))
+                act(B("pa", s, 1), B("s1", s, 1))
 
     def finish(s, rnd, out):
         for h in (1, 0):
@@ -443,7 +494,10 @@ def build():
             old = R("own0", a, a + 4 * NW - 3, 4)
             df = B(("tg", "wg")[h], s)
             tt(df, chosen(s, h), old, "subtract")
-            act(PS(s, h, 0), df, scale=0.25)
+            if FIN_V >> h & 1:
+                ts(PS(s, h, 0), df, 0.25, "mult")
+            else:
+                act(PS(s, h, 0), df, scale=0.25)
             tt(R(out, 512 * h + NW * s, 512 * h + NW * (s + 1)), PS(s, h, 0), old, "add")
 
     def depart(s):
@@ -455,8 +509,8 @@ def build():
         tt(di(s, 0), di(s, 0), di(s, 2), "add")
 
     def spread(f, src, s, h, on):
-        a = 2048 * h + 4 * NW * s
-        (cp if on == "v" else act)(R(f, a, a + 4 * NW - 3, 4), R(src, 512 * h + NW * s, 512 * h + NW * (s + 1)))
+        a = 2048 * h + 1024 * s
+        (cp if on == "v" else act)(R(f, a, a + 1024 - 3, 4), R(src, 512 * h + 256 * s, 512 * h + 256 * (s + 1)))
 
     def start(s, half):
         tt(slot("sa", s, 3), st(s, T1), slot("sa", s, 1), "add")
@@ -486,8 +540,8 @@ def build():
         ms(st(s, T1), 256.0)
         start(s, True)
         act(B("pa", s), R("own0", 4 * NW * s, 4 * NW * (s + 1) - 3, 4))
-        act(B("s1", s), R("own0", 2048 + 4 * NW * s, 2048 + 4 * NW * (s + 1) - 3, 4))
-        act(B("pa", s, 1), B("s1", s))
+        act(B("s1", s, 1), R("own0", 2048 + 4 * NW * s, 2048 + 4 * NW * (s + 1) - 3, 4))
+        act(B("pa", s, 1), B("s1", s, 1))
         ms(R("fa%d" % s, 0, 4 * NC), 0.0)
         ms(fslot("fa", s, 0), -BIG)
         ts(fslot("fa", s, 3), R("cf", 48, 48 + NC), R("cf", 10, 11), "add")
@@ -499,15 +553,18 @@ def build():
         finish(s, 0, "newb")
     phase(None, "m")
     arr = []
-    for s in range(NST):
-        sn = send("mid%d" % s, [R("newb", NW * s, NW * s + NW), R("newb", 512 + NW * s, 512 + NW * s + NW)], 1 << 18)
-        for h in (0, 1):
-            arr.append(arrive("an%d" % (2 * s + h), (1, 0), [R("new1", 512 * h + NW * s, 512 * h + NW * (s + 1))], [sn], 1, 1 << 17))
+    for s in range(2):
+        for h in (1, 0):
+            sn = send("mid%d" % (2 * s + h), [R("newb", 512 * h + 256 * s, 512 * h + 256 * (s + 1))], 1 << 17)
+            if arr:
+                ops[sn]["late"] = last_sn
+            last_sn = sn
+            arr.append(arrive("an%d" % (2 * s + h), (2, 0), [R("new1", 512 * h + 256 * s, 512 * h + 256 * (s + 1))], [sn], 1, 1 << 16))
     s_n = send("mid4", [R("newb", 0, 1024)], 0, arr)
     arrive("an4", (0, 1), [R("new4", 0, 1024)], [s_n], 0, 1 << 19)
     dma("y", R("new4s", 0, 1024, 1, 0, 112), R("new4", 0, 1024, 1, 16, 128))
     dma("y", R("new4s", 0, 1024, 1, 112, 128), R("new4", 0, 1024, 1, 0, 16))
-    for s in range(NST):
+    for s in range(2):
         for h in (0, 1):
             spread("f0", "newb", s, h, "s")
             spread("f1", "new1", s, h, "s" if h else "v")
@@ -525,21 +582,24 @@ def build():
         tt(st(s, T1), st(s, KQ), st(s, T2), "add")
         start(s, False)
         levels(s, "f0", False)
-        at_depth(s, of(s, OKF), 0, [B("pa", s), B("s1", s)])
-        act(B("pa", s, 1), B("s1", s))
+        at_depth(s, of(s, OKF), 0, [B("pa", s), B("s1", s, 1)])
+        act(B("pa", s, 1), B("s1", s, 1))
     for s in range(NST):
         hop(s, "f1", "wt1", (7680, 7680), "misc1", C128, "cu1")
         hop(s, "f4", "wt4", (3840, 3840), "co4", C128, "home")
         hop(s, "f0", "wt0", (3840, 3840), "misc", HOME, None)
-        finish(s, 1, "outb")
+        finish(s, 1, "new1")
+        a, b = NW * (s + 1) - 256, NW * (s + 1)
         for h, y in enumerate(("yt", "ys")):
-            dma("y", R(y, NW * s, NW * s + NW), R("outb", 512 * h + NW * s, 512 * h + NW * (s + 1)))
+            if b % 256 == 0:
+                dma("y", R(y, a, b), R("new1", 512 * h + a, 512 * h + b))
         depart(s)
         cp(st(s, DF), di(s, 0))
         g = [(R("pa%d" % s, b, NW, 16, 0, 8), R("ident", b, 128, 16), st(s, DF), True, True) for b in range(16)]
         add("t", "mm", g, [R("ident", 0, 128), st(s, DF)], [B("pa", s)])
-        act(R("ydb", NW * s, NW * s + NW, 1, 0, 8), R("pa%d" % s, 0, NW, 1, 0, 8))
-        dma("s", R("yd", NW * s, NW * s + NW, 1, 0, 8), R("ydb", NW * s, NW * s + NW, 1, 0, 8))
+        act(R("new4s", NW * s, NW * s + NW, 1, 0, 8), R("pa%d" % s, 0, NW, 1, 0, 8))
+        if NW * (s + 1) % 256 == 0:
+            dma("s", R("yd", a, NW * s + NW, 1, 0, 8), R("new4s", a, NW * s + NW, 1, 0, 8))
     return ops
 
 
@@ -562,7 +622,7 @@ def order(ops, P, U):
     x = U["seed"]
     for i, o in enumerate(ops):
         x = (x * 1103515245 + 12345) % 2147483648
-        pri[i] += U["noise"] * x / 2147483648 + (U["lead"] if o["s"] == 0 else 0.0) + 1e9 * o.get("first", 0) + U["role"].get(o["role"], 0)
+        pri[i] += U["noise"] * x / 2147483648 + (U["lead"] * (NST - 1 - o["s"]) if o["s"] is not None else 0.0) + 1e9 * o.get("first", 0) + U["role"].get(o["role"], 0)
     ready = [0.0] * n
     pool = {e: [] for e in "vstgy"}
     free = {e: 0.0 for e in "vstgy"}
@@ -653,7 +713,7 @@ def plan(U):
 
 OPS, SEQ, WAITS, SEM, _NAMES, TAIL, END = plan(TUNE)
 SEMAPHORES = _NAMES + ["am0", "am1", "am4", "ae0", "ae1", "ab0", "ab1", "ab4", "an0", "an1", "an2", "an3", "an4",
-                       "sent", "rm", "re", "rb", "rf", "rn"]
+                       "sent", "rm", "re0", "re1", "rb0", "rf", "rn0", "rn1"]
 
 
 def bits(es):
@@ -671,27 +731,28 @@ def piece(T, kind, k, landed):
     if kind == "m":
         return T["misc1" if landed else "misc"][:, 33 * k:33 * k + 33]
     if kind == "e":
-        return T["we1" if landed else "we0"][:, 512 * k:512 * k + 512]
+        return T["we1" if landed else "we0"][:, 256 * k:256 * k + 256]
     if kind == "b":
         return T["w1b" if landed else "own0"][:, 1024 * k:1024 * k + 1024]
     if kind == "f":
         return T["w4b" if landed else "stage4"][:, 2048 * k:2048 * k + 2048]
-    a = 512 * (k % 2) + NW * (k // 2)
-    return T["new1" if landed else "newb"][:, a:a + NW]
+    a = 512 * (k // 2 % 2) + 256 * (k // 4) + 128 * (k % 2)
+    return T["new1" if landed else "newb"][:, a:a + 128]
 
 
 def relay_program(g, core, T, topo, src, down, far, k):
     on, off = topo.engines(src, core), topo.engines(src, far)
     rest = len(on) - len(off)
-    steps = [("m", k, rest // NREL, down, "am0" if k == 0 else "am1"), ("e", k, len(on) // 2, down, "ae%d" % (k // 2)),
-             ("b", (k + 2) % NREL, len(on) // 2, down, "ab%d" % (1 - k // 2))]
+    half = len(on) // 2
+    steps = [("m", k, rest // NREL, down, "am0" if k == 0 else "am1", "rm"), ("e", k, half, down, "ae0", "re0"),
+             ("e", k + 4, half, down, "ae1", "re1"), ("b", k, half, down, "ab%d" % (k // 2), "rb0")]
     if k == 1:
-        steps.append(("f", 1, rest, far, "ab4"))
-    steps.append(("n", k, len(on) // 2, down, "an%d" % k))
+        steps.append(("f", 1, rest, far, "ab4", "rf"))
+    steps += [("n", k, half, down, "an%d" % (k // 2), "rn0"), ("n", k + 4, half, down, "an%d" % (k // 2 + 2), "rn1")]
     total = 0
-    for kind, j, n, dst, sem in steps:
+    for kind, j, n, dst, sem, got in steps:
         rid, pid = topo.addr(dst, core)
-        g.wait_ge(T.sem["r" + kind], n)
+        g.wait_ge(T.sem[got], n)
         p = piece(T, kind, j, True)
         g.remote_dma(p, p, T.sem[sem], T.sem.sent, pid, rid, topo.mask(core, dst))
         total += len(topo.engines(core, dst))
@@ -748,7 +809,7 @@ def rank_program(g, core, T, topo):
             ts_ = [tr(far, T.newb[:], T.new4[:], "an4", off)]
         else:
             kind, h = {"b": "b", "e": "e", "m": "n"}[what[0]], int(what[-1])
-            ts_ = [tr(rel[(2 * h + j + (2 if kind == "b" else 0)) % NREL], piece(T, kind, 2 * h + j, False), piece(T, kind, 2 * h + j, True), "r" + kind, on[j::2])
+            ts_ = [tr(rel[(2 * h + j) % NREL], piece(T, kind, 2 * h + j, False), piece(T, kind, 2 * h + j, True), "r%s%d" % (kind, h // 2), on[j::2])
                    for j in range(2)]
         g.remote_dma_fused(ts_, local_sem=T.sem.sent)
 

@@ -1,69 +1,87 @@
+import math
 from concourse.bass import DstId, RemoteDMATransfer
 from concourse.mybir import AluOpType, ActivationFunctionType
 
-NST = 2
-NW = 512 // NST
-NC = NW // 16
+OPT = dict(nw=(256, 256),
+           fuse_s=(1, 1, 1, 1),
+           fuse_n=(1, 1),
+           first=0,
+           pe_copy=(0, 0),
+           pe_ds=(0, 0),
+           pe_dt=(0, 0),
+           pe_h=((0, 0), (0, 0)),
+           split=("mul", "yes", "sub", "rr"), rsplit=("yes", "mul", "rr", "sub", "ds"), wt4_v=0)
 NREL = 4
-FUSE_S = (1, 1, 1, 1)
-FUSE_N = 1
-MERGE = 0
-FIN_V = 0
-PE0 = 0
-SLIM = 0
-NOWAR = 0
-WT4_V = 4096
-ROLE = {'vq01024.1': -600, 'vso10.3': -1300, 'vof00.4': 1200, 'vyes10.4': 100, 'vq13328.2': -3000, 'mvq1768.1': -600, 'vso10.1': -100,
-        'vdi116.1': 300, 'vq03328.5': -1200, 'vpc00.2': 300, 'vpc00.6': -3000, 'vnew1512.1': 100, 'vpc10.2': -600, 'vst00.1': 300,
-        'spd0256.1': 1200, 'vfb00.1': -300, 'sst0144.1': -300, 'vpc10.11': -900, 'vyes10.7': 100, 'vpc00.4': -300, 'vpc10.13': -300,
-        'tpc0272.1': -600, 'vsb1240.1': 300, 'vfb12.1': 1200, 'mvdi132.1': 600, 'vpc10.7': -1200, 'vof132.1': -600, 'vpc10.3': -1200,
-        'swg10.2': 300, 'vq03328.7': -300, 'vof048.1': -1200, 'mvdi116.2': 1200, 'vdi10.1': -100, 'spd00.1': 300, 'vst148.1': 100,
-        'aswt01024.2': -600, 'mvq1512.1': 100, 'sq13072.1': -3000, 'vpc00.1': -1200, 'stg10.4': 600, 'srr10.6': -100}
-TUNE = dict(lead=2000.0, look=100.0, noise=0.0, seed=1, role=ROLE)
+TUNE = dict(lead=2000.0, look=100.0, noise=0.0, seed=1, role={}, leads=(1000.0, 2000.0), looks=(0.0, 100.0), rounds=15, turns=3000)
 PAR = dict(fix=0.0, fixs=0.0, fuse=0.0, cyc=0.95, g=1.56, wake=200.0, same=180.0, pe=0.5, dma=2000.0, bw=160.0, call=900.0, leg=2500.0, link=45.0)
 BIG = 1.0e6
+ALPHA = 4096.0
+NX = 2032
 
-SCRATCH = {
-    "own0": ("sbuf", [128, 4096], "bfloat16"), "w1b": ("sbuf", [128, 4096], "bfloat16"),
-    "w4b": ("sbuf", [128, 4096], "bfloat16"), "stage4": ("sbuf", [128, 4096], "bfloat16"),
-    "we0": ("sbuf", [128, 2048], "bfloat16"), "we1": ("sbuf", [128, 2048], "bfloat16"),
-    "f0": ("sbuf", [128, 4096], "float32"), "f1": ("sbuf", [128, 4096], "float32"), "f4": ("sbuf", [128, 4096], "float32"),
-    "wt1": ("sbuf", [128, 7680], "float32"), "wt4": ("sbuf", [128, 3840], "float32"), "wt0": ("sbuf", [128, 3840], "float32"),
-    "cu0": ("sbuf", [128, 2048], "bfloat16"), "cu1": ("sbuf", [128, 2048], "bfloat16"),
-    "cui": ("sbuf", [128, 128], "int32"), "cub0": ("sbuf", [128, 128], "bfloat16"), "cub1": ("sbuf", [128, 128], "bfloat16"),
-    "ktab": ("sbuf", [128, 2048], "bfloat16"), "mm": ("sbuf", [128, 2048], "bfloat16"),
-    "ones": ("sbuf", [128, 128], "float32"), "ident": ("sbuf", [128, 128], "float32"),
-    "misc": ("sbuf", [128, 132], "float32"), "misc1": ("sbuf", [128, 132], "float32"),
-    "misc4": ("sbuf", [128, 33], "float32"), "co4": ("sbuf", [128, 4], "float32"),
-    "newb": ("sbuf", [128, 1024], "float32"), "new1": ("sbuf", [128, 1024], "float32"),
-    "new4": ("sbuf", [128, 1024], "float32"), "new4s": ("sbuf", [128, 1024], "float32"),
-    "identb": ("sbuf", [128, 256], "bfloat16"), "nident": ("sbuf", [128, 128], "float32"),
-    "ci": ("sbuf", [128, 32], "int32"), "cf": ("sbuf", [128, 64], "float32"),
-}
-for _s in range(NST):
-    for _n in ("tg", "wg", "rr"):
-        SCRATCH["%s%d" % (_n, _s)] = ("sbuf", [128, NW], "float32")
-    SCRATCH["s1%d" % _s] = ("sbuf", [128, 2 * NW], "float32")
-    SCRATCH["q%d" % _s] = ("sbuf", [128, 14 * NW], "float32")
-    for _n in ("fa", "fb", "fo"):
-        SCRATCH["%s%d" % (_n, _s)] = ("sbuf", [128, 4 * NC], "float32")
-    SCRATCH["yes%d" % _s] = ("sbuf", [128, NW], "bfloat16")
-    SCRATCH["tb%d" % _s] = ("sbuf", [128, NW], "bfloat16")
-    SCRATCH["lb%d" % _s] = ("sbuf", [128, 4 * NW], "bfloat16")
-    SCRATCH["cug%d" % _s] = ("sbuf", [128, NW], "bfloat16")
-    SCRATCH["st%d" % _s] = ("sbuf", [128, 12 * NC], "float32")
-    SCRATCH["sa%d" % _s] = ("sbuf", [128, 5 * NC], "float32")
-    SCRATCH["sb%d" % _s] = ("sbuf", [128, 20 * NC], "float32")
-    SCRATCH["so%d" % _s] = ("sbuf", [128, 5 * NC], "float32")
-    SCRATCH["di%d" % _s] = ("sbuf", [128, 4 * NC], "int32")
-    SCRATCH["of%d" % _s] = ("sbuf", [128, 8 * NC], "uint16")
-    for _n in ("pa", "pb", "pc", "pd")[:8 // NST]:
-        SCRATCH["%s%d" % (_n, _s)] = ("psum", [128, 512], "float32")
+
+def layout(O):
+    nws = O["nw"]
+    S = {
+        "own0": ("sbuf", [128, 4096], "bfloat16"), "w1b": ("sbuf", [128, 4096], "bfloat16"),
+        "w4b": ("sbuf", [128, 4096], "bfloat16"), "stage4": ("sbuf", [128, 4096], "bfloat16"),
+        "we0": ("sbuf", [128, 2048], "bfloat16"), "we1": ("sbuf", [128, 2048], "bfloat16"),
+        "f0": ("sbuf", [128, 4096], "float32"), "f1": ("sbuf", [128, 4096], "float32"), "f4": ("sbuf", [128, 4096], "float32"),
+        "xs": ("sbuf", [128, 2 * NX], "float32"),
+        "wt1": ("sbuf", [128, 2 * NX], "float32"), "wt4": ("sbuf", [128, NX], "float32"), "wt0": ("sbuf", [128, NX], "float32"),
+        "cu0": ("sbuf", [128, 2048], "bfloat16"), "cu1": ("sbuf", [128, 2048], "bfloat16"),
+        "cui": ("sbuf", [128, 128], "int32"), "cub0": ("sbuf", [128, 128], "bfloat16"), "cub1": ("sbuf", [128, 128], "bfloat16"),
+        "mm": ("sbuf", [128, 2048], "bfloat16"),
+        "ones": ("sbuf", [128, 128], "float32"), "ident": ("sbuf", [128, 512], "float32"),
+        "identb": ("sbuf", [128, 256], "bfloat16"),
+        "misc": ("sbuf", [128, 132], "float32"), "misc1": ("sbuf", [128, 132], "float32"),
+        "misc4": ("sbuf", [128, 33], "float32"), "co4": ("sbuf", [128, 4], "float32"),
+        "newb": ("sbuf", [128, 1024], "float32"), "new1": ("sbuf", [128, 1024], "float32"),
+        "new4": ("sbuf", [128, 1024], "float32"), "new4s": ("sbuf", [128, 1024], "float32"),
+        "ci": ("sbuf", [128, 32], "int32"), "cf": ("sbuf", [128, 128], "float32"),
+        "cs": ("sbuf", [128, 28 * 16], "float32"), "cr": ("sbuf", [128, 19 * 16], "float32"), "tp": ("sbuf", [128, 26 * 16], "float32"),
+    }
+    qh = max(nws)
+    for s, nw in enumerate(nws):
+        nc = nw // 16
+        for n in ("tg", "sg", "wg", "rr", "ds", "kk", "dt", "aa"):
+            S["%s%d" % (n, s)] = ("sbuf", [128, nw], "float32")
+        for n in ("s1", "dd"):
+            S["%s%d" % (n, s)] = ("sbuf", [128, 2 * nw], "float32")
+        S["q%d" % s] = ("sbuf", [128, 8 * qh], "float32")
+        S["yes%d" % s] = ("sbuf", [128, nw], "bfloat16")
+        S["cug%d" % s] = ("sbuf", [128, nw], "bfloat16")
+        S["tb%d" % s] = ("sbuf", [128, nw], "bfloat16")
+        S["hb%d" % s] = ("sbuf", [128, 2 * nw], "bfloat16")
+        S["st%d" % s] = ("sbuf", [128, 8 * nc], "float32")
+        S["so%d" % s] = ("sbuf", [128, 26 * nc], "float32")
+        S["di%d" % s] = ("sbuf", [128, 4 * nc], "int32")
+        S["of%d" % s] = ("sbuf", [128, 8 * 16], "uint16")
+    for b in range(8):
+        S["bank%d" % b] = ("psum", [128, 512], "float32")
+    P = {}
+    for s, nw in enumerate(nws):
+        nc = nw // 16
+        if len(nws) == 2:
+            rows = [("t1", "s1"), ("ht", "hs"), ("m0", "m1"), ("ps", "p1", "p2", "p3")]
+            if O["pe_ds"][0] or O["pe_ds"][1]:
+                rows = [("t1", "m0"), ("ht", "hs"), ("m1", "s1"), ("ps", "p1", "p2", "p3")]
+            banks = [4 * s + k for k in range(4)]
+            base = [0, 0, 0, 0]
+        else:
+            rows = [("t1", "s1", "ps", "p1"), ("ht", "hs", "p2", "p3"), ("m0",), ("m1",)]
+            banks = [2 * s, 2 * s + 1, 6, 7]
+            base = [0, 0, sum(nws[:s]), sum(nws[:s])]
+        for names, b, a in zip(rows, banks, base):
+            for n in names:
+                P[(n, s)] = ("bank%d" % b, a)
+                a += {"ps": 7 * nc, "p1": 6 * nc, "p2": 6 * nc, "p3": 7 * nc}.get(n, nw)
+    return S, P
+
+
+SCRATCH, PLACE = layout(OPT)
 
 
 def R(name, a, b, step=1, p0=0, p1=128, ps=1):
-    if NST > 2 and name[:2] in ("pc", "pd"):
-        name, a, b = ("pa" if name[1] == "c" else "pb") + name[2:], a + 2 * NW, b + 2 * NW
     return (name, a, b, step, p0, p1, ps)
 
 
@@ -86,6 +104,14 @@ def _two(r):
 def _bytes(r):
     w = 2 if (r[0] in ("te", "sa") or _two(r)) else 4
     return _n(r) * len(range(r[4], r[5], r[6])) * w
+
+
+def meet(x, r):
+    return (x[1] < r[2] and r[1] < x[2] and x[4] < r[5] and r[4] < x[5] and (x[1] - r[1]) % math.gcd(x[3], r[3]) == 0)
+
+
+def covers(r, x):
+    return r[4] == 0 and r[5] == 128 and r[6] == 1 and r[1] <= x[1] and x[2] <= r[2] and x[3] % r[3] == 0 and (x[1] - r[1]) % r[3] == 0
 
 
 def cost(op, P):
@@ -124,8 +150,13 @@ def cost(op, P):
     raise ValueError(k)
 
 
-def build():
-    ops, acc, bank, cur, seen = [], {}, {}, [None, "a"], {}
+def build(O):
+    ops, acc, bank, cur, seen, pe_last = [], {}, {}, [None, "a"], {}, {}
+    NWS = O["nw"]
+    NST = len(NWS)
+    I0 = [sum(NWS[:s]) for s in range(NST)]
+    QH = max(NWS)
+    NM = QH // 16
 
     def add(e, k, a, rd, wr, after=(), **kw):
         i = len(ops)
@@ -138,21 +169,23 @@ def build():
             if r[0] not in SCRATCH:
                 continue
             for (x, j, jw) in acc.setdefault(r[0], []):
-                if (w or jw) and x[1] < r[2] and r[1] < x[2] and x[4] < r[5] and r[4] < x[5]:
-                    own = w and NOWAR and ops[j]["e"] == e and e in "vst" and "dma" not in (k, ops[j]["k"])
-                    (soft if own else deps).add(j)
+                if (w or jw) and meet(x, r):
+                    (soft if e == "t" and ops[j]["e"] == "t" and kw.get("goes_on") else deps).add(j)
             if SCRATCH[r[0]][0] == "psum":
                 b = bank.setdefault(r[0], [e, [], []])
                 if b[0] != e:
                     b[0], b[2], b[1] = e, b[1], []
                 deps.update(b[2])
                 b[1].append(i)
+                if e == "t":
+                    if r[0] in pe_last:
+                        soft.add(pe_last[r[0]])
+                    pe_last[r[0]] = i
         for r, w in flat:
             if r[0] not in SCRATCH:
                 continue
             if w:
-                full = r[3] == 1 and r[4] == 0 and r[5] == 128 and r[6] == 1
-                acc[r[0]] = [t for t in acc[r[0]] if t[1] == i or not (t[0] == r or (full and r[1] <= t[0][1] and t[0][2] <= r[2]))]
+                acc[r[0]] = [t for t in acc[r[0]] if t[1] == i or not (t[0] == r or covers(r, t[0]))]
             acc[r[0]].append((r, i, w))
         deps.discard(i)
         key = "%s%s%d" % (e, wr[0][0], wr[0][1]) if wr else "send"
@@ -182,6 +215,9 @@ def build():
     def act(o, x, scale=None, bias=None):
         return add("s", "act", (o, x, scale, bias), refs(x, scale, bias), [o])
 
+    def scan(o, x, y):
+        return add("v", "scan", (o, x, y, "subtract", "min"), [x, y], [o])
+
     def iota(o, pat, base, cm):
         return add("g", "iota", (o, pat, base, cm), [], [o])
 
@@ -193,14 +229,19 @@ def build():
         ops[i]["sdeps"] += list(behind)
         return i
 
-    def arrive(sem, n, wr, mirror, legs, nbytes):
-        i = add(None, "arr", (sem, n, legs, nbytes), [], wr)
+    def arrive(sem, n, wr, mirror, legs, nbytes, src):
+        i = add(None, "arr", (sem, n, legs, nbytes), [], wr, src=src)
         ops[i]["sdeps"] += list(mirror)
         return i
 
-    def count(o, src):
-        g = [(o, R("mm", 128 * e, 128 * e + 128), R(src, e, NW, 16), e == 0, e == 15) for e in range(16)]
-        return add("t", "mm", g, [R("mm", 0, 2048), R(src, 0, NW)], [o])
+    def halves(r, on):
+        return [(r[0], r[1] + e, r[2], 2) + r[4:] for e in (0, 1)] if on else [r]
+
+    def count(s, o, src, on):
+        nw = NWS[s]
+        for es in ([range(0, 16, 2), range(1, 16, 2)] if on else [range(16)]):
+            g = [(o, R("mm", 128 * e, 128 * e + 128), R(src, e, nw, 16), e == 0, e == 15) for e in es]
+            add("t", "mm", g, [R("mm", 0, 2048), R(src, es[0], nw, es.step)], [o], goes_on=es[0] == 1)
 
     ms(R("misc", 0, 4), 0.0)
     d0 = dma("y", R("cui", 0, 128), R("cu", 0, 2048, 1, 0, 8))
@@ -218,388 +259,400 @@ def build():
         s_e.append(send("even%d" % k, [R("we0", 512 * k, 512 * k + 512)], 1 << 17))
         ops[s_e[k]]["late"] = s_e[k - 1] if k else s_m
     s_e1 = s_e[3]
-    arrive("am0", (1, 0), [R("misc1", 0, 33)], [s_m], 1, 0)
-    arrive("am1", (3, 0), [R("misc1", 33, 132)], [s_m], 1, 0)
-    arrive("am4", (0, 1), [R("misc4", 0, 33)], [s_m], 0, 0)
-    a_e0 = arrive("ae0", (4, 0), [R("we1", 0, 1024)], [s_e[1]], 1, 1 << 16)
-    a_e1 = arrive("ae1", (4, 0), [R("we1", 1024, 2048)], [s_e[3]], 1, 1 << 16)
+    arrive("am0", (1, 0), [R("misc1", 0, 33)], [s_m], 1, 0, (R("misc", 0, 33), 1))
+    arrive("am1", (3, 0), [R("misc1", 33, 132)], [s_m], 1, 0, (R("misc", 33, 132), 1))
+    arrive("am4", (0, 1), [R("misc4", 0, 33)], [s_m], 0, 0, (R("misc", 0, 33), 4))
+    arrive("ae0", (4, 0), [R("we1", 0, 1024)], [s_e[1]], 1, 1 << 16, (R("we0", 0, 1024), 1))
+    a_e1 = arrive("ae1", (4, 0), [R("we1", 1024, 2048)], [s_e[3]], 1, 1 << 16, (R("we0", 1024, 2048), 1))
     s_t = send("bulk0", [R("own0", 0, 2048)], 1 << 19, behind=[])
     s_s = send("bulk1", [R("own0", 2048, 4096)], 1 << 19)
     ops[s_t]["late"], ops[s_s]["late"] = s_e1, s_t
-    a_t = arrive("ab0", (2, 0), [R("w1b", 0, 2048)], [s_t, a_e1], 0, 1 << 18)
-    a_s = arrive("ab1", (2, 0), [R("w1b", 2048, 4096)], [s_s, a_t], 0, 1 << 18)
+    a_t = arrive("ab0", (2, 0), [R("w1b", 0, 2048)], [s_t, a_e1], 0, 1 << 18, (R("own0", 0, 2048), 1))
+    a_s = arrive("ab1", (2, 0), [R("w1b", 2048, 4096)], [s_s, a_t], 0, 1 << 18, (R("own0", 2048, 4096), 1))
     dma("y", R("co4", 0, 4, 1, 0, 112), R("misc4", 0, 4, 1, 16, 128))
     dma("y", R("co4", 0, 4, 1, 112, 128), R("misc4", 0, 4, 1, 0, 16))
     for h, src in enumerate(("te", "sa")):
         dma("y", R("stage4", 2048 * h, 2048 * h + 2048, 1, 0, 112), R(src, 0, 2048, 1, 16, 128), [a_e1], ahead=h << 19)
         dma("y", R("stage4", 2048 * h, 2048 * h + 2048, 1, 112, 128), R(src, 0, 2048, 1, 0, 16), [a_e1], ahead=h << 19)
     s_4 = send("bulk4", [R("stage4", 0, 4096)], 1 << 19, [a_t])
-    a_4 = arrive("ab4", (1, 1), [R("w4b", 0, 4096)], [s_4, a_s], 1, 1 << 19)
+    a_4 = arrive("ab4", (1, 1), [R("w4b", 0, 4096)], [s_4, a_s], 1, 1 << 19, (R("stage4", 0, 4096), 4))
     for f, b in (("f1", "w1b"), ("f0", "own0"), ("f4", "w4b")):
         dma("g", R(f, 0, 4096), R(b, 0, 4096), [a_4])
 
     iota(R("ci", 0, 8), [[-16, 8]], 0, 1)
     iota(R("ci", 8, 9), [[0, 1]], 0, 1)
-    iota(R("wt1", 0, 256), [[-16, 256]], 4080, 0)
+    iota(R("xs", 0, 256), [[2, 256]], 0, 0)
     iota(R("cf", 16, 32), [[1, 16]], 0, 0)
-    iota(R("cf", 32, 32 + NC), [[0, NC // 2], [-64, 2]], 0, 0)
+    iota(R("cf", 32, 64), [[0, 16], [1024, 2]], 0, 0)
+    iota(R("cf", 64, 96), [[-128, 16], [0, 2]], 0, 0)
+    iota(R("cf", 96, 112), [[16, 16]], 0, 0)
     ts(R("ci", 16, 24), R("ci", 0, 8), 4, "arith_shift_right")
-    ts(R("cf", 0, 8), R("ci", 16, 24), 0.0, "is_equal")
+    ts(R("cf", 0, 8), R("ci", 16, 24), 0.0, "is_equal", -ALPHA, "mult")
     ts(R("ci", 9, 10), R("ci", 8, 9), 15, "bitwise_and")
-    ts(R("cf", 8, 9), R("ci", 9, 10), -4.0, "mult")
-    cp(R("cf", 10, 11), R("ci", 9, 10))
-    iota(R("cf", 48, 48 + NC), [[16, NC]], 0, 0)
-    ms(R("cf", 9, 10), 257.0)
+    ts(R("cf", 8, 9), R("ci", 9, 10), 64.0, "mult")
+    cp(R("cf", 9, 10), R("ci", 9, 10))
+    ms(R("cf", 10, 11), 0.125)
+    ts(R("cf", 96, 112), R("cf", 96, 112), R("cf", 9, 10), "add")
+    J = R("cf", 96, 96 + NM)
     ms(R("mm", 0, 2048), 0.0)
     for g in range(8):
         v = R("mm", 16 * g, 16 * g + 129 * 15 + 1, 129)
         ts(v, v, R("cf", g, g + 1), "add")
-    ms(R("cf", 11, 12), -1280.0)
-    later = [iota(R("ktab", 1024 * h, 1024 * h + 1024), [[1, 8], [0, 128]], 8 * h, 0) for h in (0, 1)]
-    later += [iota(R("cu1", 1024 * h, 1024 * h + 1024), [[0, 1024]], 0, 0) for h in (0, 1)]
-    later += [iota(R("wt1", 3840 + 768 * h, 3840 + 768 * h + 768), [[2, 3], [-16, 256]], 4081 + 6 * h, 0) for h in range(5)]
+    later = [iota(R("cu1", 1024 * h, 1024 * h + 1024), [[0, 1024]], 0, 0) for h in (0, 1)]
+    later += [iota(R("xs", NX + 508 * h, NX + 508 * h + 508), [[2, 508]], 1 + 1016 * h, 0) for h in range(4)]
     for i in later:
         ops[i]["late"] = s_s
     ms(R("cu0", 0, 2048), 0.0)
-    ts(R("cub0", 0, 128), R("misc", 4, 132), 128.0, "mult")
+    ts(R("cub0", 0, 128), R("misc", 4, 132), 128.0 / ALPHA, "mult")
     dma("y", R("cu0", 0, 2048, 1, 0, 128, 16), R("cub0", 0, 128))
-    ts(R("cub1", 0, 128), R("misc1", 4, 132), 128.0, "mult")
+    ts(R("cub1", 0, 128), R("misc1", 4, 132), 128.0 / ALPHA, "mult")
     dma("y", R("cu1", 0, 2048, 1, 0, 128, 16), R("cub1", 0, 128))
     ms(R("ones", 0, 128), 1.0)
     i_id = add("g", "sel", (R("ident", 0, 128), R("ones", 0, 128)), [R("ones", 0, 128)], [R("ident", 0, 128)])
-    if PE0:
-        cp(R("identb", 0, 128), R("ident", 0, 128))
-        ts(R("identb", 128, 256), R("ident", 0, 128), -1.0, "mult")
-        ts(R("nident", 0, 128), R("ident", 0, 128), -1.0, "mult")
-        for s in range(NST):
-            act(R("s1%d" % s, 0, NW), R("own0", 4 * NW * s, 4 * NW * (s + 1) - 3, 4))
-            ms(R("q%d" % s, 512, 1024), 0.0)
-    else:
-        ops[i_id]["sdeps"].append(s_4)
-    ts(R("wt1", 256, 512), R("wt1", 0, 256), 2.0, "add")
-    ts(R("wt1", 512, 1024), R("wt1", 0, 512), 4.0, "add")
-    ts(R("wt1", 1024, 2048), R("wt1", 0, 1024), 8.0, "add")
-    ts(R("wt1", 2048, 2944), R("wt1", 0, 896), 16.0, "add")
-    ts(R("wt1", 2944, 3840), R("wt1", 896, 1792), 16.0, "add")
-    blocks = [(0, 256), (256, 1024), (1024, 2048), (2048, 2944), (2944, 3840)]
-    for a, b in blocks:
-        act(R("wt0", a, b), R("wt1", a, b), scale=R("misc", 1, 2))
-        if a < WT4_V:
-            ts(R("wt4", a, b), R("wt1", a, b), R("co4", 1, 2), "mult", R("co4", 0, 1), "add")
-        else:
-            act(R("wt4", a, b), R("wt1", a, b), scale=R("co4", 1, 2))
-            act(R("wt4", a, b), R("wt4", a, b), bias=R("co4", 0, 1))
-    for a, b in blocks:
-        act(R("wt0", a, b), R("wt0", a, b), bias=R("misc", 0, 1))
-    for a, b in blocks[:3]:
-        ts(R("wt1", a, b), R("wt1", a, b), R("misc1", 1, 2), "mult", R("misc1", 0, 1), "add")
-    for a in range(2048, 7680, 512):
-        act(R("wt1", a, a + 512), R("wt1", a, a + 512), scale=R("misc1", 1, 2))
-        act(R("wt1", a, a + 512), R("wt1", a, a + 512), bias=R("misc1", 0, 1))
+    if not O["pe_dt"][0]:
+        ops[i_id]["late"] = s_s
+    made = {("ident", 0)}
 
-    PP, VC0, C128, KQ, XI, HOME, DF, T1, T2, NL, N2, VX = range(12)
+    def unit(val, x):
+        name, k = ("identb", (1.0, 0.5).index(val)) if _two(x) else ("ident", (1.0, -1.0, 0.5, -0.5).index(val))
+        if (name, k) not in made:
+            made.add((name, k))
+            act(R(name, 128 * k, 128 * k + 128), R("ident", 0, 128), scale=val)
+        return R(name, 128 * k, 128 * k + 128)
+
+    def pe_sum(o, a, x, b, y, on=False):
+        add("t", "mm", [(o, unit(a, x), x, True, False)], [unit(a, x), x], [o])
+        parts = list(zip(halves(o, on), halves(y, on)))
+        for k, (p, q) in enumerate(parts):
+            add("t", "mm", [(p, unit(b, q), q, False, k == len(parts) - 1)], [unit(b, q), q], [p], goes_on=True)
+
+    for a, b in ((256, 512), (512, 1024), (1024, NX)):
+        act(R("xs", a, b), R("xs", 0, b - a), bias=float(2 * a))
+    for a, b in ((0, 512), (512, 1024), (1024, 1536), (1536, NX)):
+        ts(R("wt1", a, b), R("xs", a, b), R("misc1", 1, 2), "mult", R("misc1", 0, 1), "add")
+        for wt, co, off in (("wt0", "misc", 0), ("wt4", "co4", 0), ("wt1", "misc1", NX)):
+            if wt == "wt4" and O["wt4_v"]:
+                ts(R(wt, a, b), R("xs", a, b), R(co, 1, 2), "mult", R(co, 0, 1), "add")
+            else:
+                act(R(wt, off + a, off + b), R("xs", off + a, off + b), scale=R(co, 1, 2))
+                act(R(wt, off + a, off + b), R(wt, off + a, off + b), bias=R(co, 0, 1))
+
+    def lane(name, a, width, e, n=NM):
+        return R(name, a + e, a + width * (n - 1) + e + 1, width)
+
+    EDGE = 8.5 * ALPHA
+    ms(R("cs", 0, 28 * NM), BIG)
+    for e, val in ((0, -EDGE), (3, 0.0), (4, 126.0)):
+        ms(lane("cs", 0, 7, e, 4 * NM), val)
+    for j in range(4):
+        for e in (1, 2):
+            ms(lane("cs", 7 * NM * j, 7, e), float(8 >> j))
+    RA, RW = (0, 6 * NM, 12 * NM), (6, 6, 7)
+    ms(R("cr", 0, 19 * NM), BIG)
+    ms(R("tp", 0, 26 * NM), 0.0)
+    ms(lane("tp", 0, 7, 0), BIG)
+    for v in range(3):
+        ms(lane("cr", RA[v], RW[v], 0), -EDGE)
+        ms(lane("cr", RA[v], RW[v], 1), 0.0)
+        ms(lane("cr", RA[v], RW[v], 3), 0.5 / (1 << v))
+        for name, a, e in (("cr", RA[v], 2), ("tp", 7 * NM + RA[v], 3)):
+            ts(lane(name, a, RW[v], e), J, 2.0 * QH * (v + 1) + (0.125 if v else 0.0), "add")
+        if v != 1:
+            ms(lane("tp", 7 * NM + RA[v], RW[v], 0), BIG)
+    cp(lane("tp", 7 * NM, 6, 2), J)
+    ms(lane("tp", 7 * NM, 6, 4), 0.75)
+
+    NL, V1, DX, VX, T1, DF = range(6)
     OCOL, OXI, OCOL1, OKQ, OXR, OC0, OX0, OKF = range(8)
+    SW = {"ps": (0, 7), "p1": (7, 6), "p2": (13, 6), "p3": (19, 7)}
 
-    def st(s, i, n=1):
-        return R("st%d" % s, NC * i, NC * (i + n))
+    def st(s, i):
+        return R("st%d" % s, NWS[s] // 16 * i, NWS[s] // 16 * (i + 1))
 
-    def of(s, i, n=1):
-        return R("of%d" % s, NC * i, NC * (i + n))
+    def of(s, i):
+        return R("of%d" % s, 16 * i, 16 * i + NWS[s] // 16)
 
     def di(s, i):
-        return R("di%d" % s, NC * i, NC * (i + 1))
+        return R("di%d" % s, NWS[s] // 16 * i, NWS[s] // 16 * (i + 1))
 
     def B(name, s, h=0):
-        return R("%s%d" % (name, s), NW * h, NW * (h + 1))
+        return R("%s%d" % (name, s), NWS[s] * h, NWS[s] * (h + 1))
 
-    def slot(name, s, e, j=0):
-        return R("%s%d" % (name, s), 5 * NC * j + e, 5 * NC * (j + 1) - 4 + e, 5)
+    def PS(name, s):
+        b, a = PLACE[(name, s)]
+        return R(b, a, a + (SW[name][1] * NWS[s] // 16 if name in SW else NWS[s]))
 
-    def cnt(s):
-        return R("pc%d" % s, NW, NW + NC)
+    def pin(name, s, e):
+        b, a = PLACE[(name, s)]
+        return lane(b, a, SW[name][1], e, NWS[s] // 16)
 
-    def cast_of(s, table):
-        act(B("cug", s), IND(R(table, 0, 2048), of(s, OCOL)))
-        count(cst(s, C128), "cug%d" % s)
+    def res(name, s, e=None):
+        nc = NWS[s] // 16
+        a, w = SW[name]
+        return R("so%d" % s, a * nc, (a + w) * nc) if e is None else lane("so%d" % s, a * nc, w, e, nc)
 
-    def cst(s, c):
-        return R("pc%d" % s, NW + NC, NW + 2 * NC) if c == C128 else st(s, c)
-
-    def first_col(s, c, half=False):
-        tt(st(s, VC0), cst(s, c), slot("sa", s, 1), "subtract")
-        if half:
-            ts(of(s, OC0), st(s, VC0), 0.5, "mult")
-        else:
-            cp(of(s, OC0), st(s, VC0))
+    def wrapped(a, s):
+        return R("cf", a + I0[s] // 16, a + (I0[s] + NWS[s]) // 16)
 
     def Qs(s, h, k):
-        a = 2 * NW * (0, 1, 5, 6, 2, 3, 4)[k]
-        return R("q%d" % s, a, a + 2 * NW) if h == 2 else R("q%d" % s, a + NW * h, a + NW * h + NW)
+        a = QH * (2 * k + h)
+        return R("q%d" % s, a, a + NWS[s])
 
-    def PS(s, h, k):
-        return R("%s%d" % (("pb", "pd")[k], s), 0, 2 * NW) if h == 2 else B(("pb", "pd")[k], s, h)
+    def P1(s, h):
+        return PS(("t1", "s1")[h], s)
 
-    def both(bit):
-        return (2,) if MERGE & bit else (1, 0)
+    def PH(s, h):
+        return PS(("ht", "hs")[h], s)
 
-    def fslot(name, s, e):
-        return R("%s%d" % (name, s), e, 4 * NC - 3 + e, 4)
+    rnd = [0]
 
-    def vote(s, tv, sv, w, b0):
-        ds = Qs(s, 1, 3)
-        tt(ds, sv, B("s1", s, 1) if sv[0] == "ind" else B("pa", s, 1), "subtract")
-        act(B("wg", s), w)
-        act(B("rr", s), ds, scale=b0)
-        if _two(tv):
-            add("t", "mm", [(B("pc", s), R("nident", 0, 128), B("s1", s), True, False)], [R("nident", 0, 128), B("s1", s)], [B("pc", s)])
-            add("t", "mm", [(B("pc", s), R("identb", 0, 128), tv, False, True)], [R("identb", 0, 128), tv, B("pc", s)], [B("pc", s)])
-        else:
-            tt(B("pc", s), tv, B("pa", s), "subtract")
-        tt(B("pc", s), B("wg", s), B("pc", s), "mult")
-        tt(B("yes", s), B("pc", s), B("rr", s), "is_gt")
-        count(cnt(s), "yes%d" % s)
-
-    def levels(s, tab, half):
-        if PE0 & 2 and _two(R(tab, 0, 1)):
-            for h in (1, 0):
-                win, lo, hi = R(tab, 2048 * h, 2048 * h + 2048), B("lb", s, h), B("lb", s, 2 + h)
-                act(lo, IND(win, of(s, OCOL)))
-                act(hi, IND(win, of(s, OCOL1)))
-            lo, hi, p, m = R("lb%d" % s, 0, 512), R("lb%d" % s, 512, 1024), R("identb", 0, 128), R("identb", 128, 256)
-            add("t", "mm", [(PS(s, 2, 0), p, lo, True, True)], [p, lo], [PS(s, 2, 0)])
-            add("t", "mm", [(PS(s, 2, 1), m, lo, True, False), (PS(s, 2, 1), p, hi, False, True)], [p, m, lo, hi], [PS(s, 2, 1)])
-            act(Qs(s, 2, 2), PS(s, 2, 1), scale=0.5)
-            tt(Qs(s, 2, 4), Qs(s, 2, 2), PS(s, 2, 0), "add")
-            act(Qs(s, 2, 0), lo)
+    def to_psum(s, h):
+        if h and O["pe_ds"][rnd[0]]:
             return
-        for h in (1, 0):
-            act(Qs(s, h, 0), IND(R(tab, 2048 * h, 2048 * h + 2048), of(s, OCOL)))
-        for h in both(1):
-            act(PS(s, h, 0), Qs(s, h, 0))
-        if FUSE_N:
-            for h in (1, 0):
-                tt(Qs(s, h, 1), IND(R(tab, 2048 * h, 2048 * h + 2048), of(s, OCOL1)), Qs(s, h, 0), "subtract")
+        if O["pe_copy"][h]:
+            g = [(P1(s, h), R("ident", 0, 128), B("s1", s, h), True, True)]
+            add("t", "mm", g, [R("ident", 0, 128), B("s1", s, h)], [P1(s, h)])
         else:
-            for h in (1, 0):
-                act(Qs(s, h, 1), IND(R(tab, 2048 * h, 2048 * h + 2048), of(s, OCOL1)))
-            tt(PS(s, 2, 1), Qs(s, 2, 1), PS(s, 2, 0), "subtract")
-        if half:
-            for h in both(2):
-                act(Qs(s, h, 2), Qs(s, h, 1) if FUSE_N else PS(s, h, 1), scale=0.5)
-            for h in both(4):
-                tt(Qs(s, h, 4), Qs(s, h, 2), PS(s, h, 0), "add")
-        if FUSE_N:
-            for h in both(1):
-                act(PS(s, h, 1), Qs(s, h, 1))
+            act(P1(s, h), B("s1", s, h))
 
-    def at_depth(s, off, start, out):
-        act(Qs(s, 0, 3), IND(R("ktab", start, 2048), off), scale=0.0625)
+    def vote(s, tv, sv, w, b0, z, sp, pe_s=False, pe_t=False):
+        ds, m = B("ds", s), PS("m0", s)
+        if sv[0] == "ind":
+            tt(ds, sv, B("s1", s, 1), "subtract")
+        elif pe_s:
+            ds = P1(s, 1)
+            pe_sum(ds, -1.0, B("s1", s, 1), 1.0, sv, "ds" in sp)
+        else:
+            for o, x, y in zip(*[halves(r, "ds" in sp) for r in (ds, sv, P1(s, 1))]):
+                tt(o, x, y, "subtract")
+        act(B("wg", s), w)
+        for o, x in zip(*[halves(r, "rr" in sp) for r in (B("rr", s), ds)]):
+            act(o, x, scale=b0)
+        if pe_t:
+            pe_sum(m, -1.0, B("s1", s, 0), 1.0, tv)
+        else:
+            for o, x, y in zip(*[halves(r, "sub" in sp) for r in (m, tv, P1(s, 0))]):
+                tt(o, x, y, "subtract")
+        for o, x in zip(*[halves(r, "mul" in sp) for r in (m, B("wg", s))]):
+            tt(o, x, o, "mult")
+        for o, x, y in zip(*[halves(r, "yes" in sp) for r in (B("yes", s), m, B("rr", s))]):
+            tt(o, x, y, "is_gt")
+        count(s, z, "yes%d" % s, "yes" in sp)
+
+    def vote_turned(s, w, b0, z, sp):
+        tt(B("ds", s), chosen(s, 1), B("sg", s), "subtract")
+        tt(B("dt", s), chosen(s, 0), B("tg", s), "subtract")
+        act(PH(s, 0), B("ds", s), scale=b0)
+        tt(B("aa", s), w, B("dt", s), "mult")
+        for o, x, y in zip(*[halves(r, "yes" in sp) for r in (B("yes", s), B("aa", s), PH(s, 0))]):
+            tt(o, x, y, "is_lt")
+        count(s, z, "yes%d" % s, "yes" in sp)
+
+    def levels(s, tab, a=0, b=2048):
         for h in (1, 0):
-            tt(Qs(s, h, 2), Qs(s, 0, 3), PS(s, h, 1), "mult")
-        for h in (both(8) if len(out) == 3 else (1, 0)):
-            tt(out[h], Qs(s, h, 2), PS(s, h, 0), "add")
+            win = R(tab, 2048 * h + a, 2048 * h + b)
+            act(Qs(s, h, 0), IND(win, of(s, OCOL)))
+            if O["pe_h"][rnd[0]][h]:
+                hi = B("hb" if _two(win) else "dd", s, h)
+                act(hi, IND(win, of(s, OCOL1)))
+                pe_sum(PH(s, h), -0.5, Qs(s, h, 0), 0.5, hi)
+            elif O["fuse_n"][h]:
+                tt(B("dd", s, h), IND(win, of(s, OCOL1)), Qs(s, h, 0), "subtract")
+                act(PH(s, h), B("dd", s, h), scale=0.5)
+            else:
+                act(PH(s, h), Qs(s, h, 0), scale=0.5)
+                act(B("dd", s, h), IND(win, of(s, OCOL1)), scale=0.5)
+                tt(PH(s, h), B("dd", s, h), PH(s, h), "subtract")
+
+    def at_depth(s, off, out):
+        act(B("kk", s), IND(R("cf", 16, 32), off), scale=0.125)
+        for h in (1, 0):
+            tt(PS("m%d" % h, s), B("kk", s), PH(s, h), "mult")
+        for h in (1, 0):
+            tt(out[h], PS("m%d" % h, s), Qs(s, h, 0), "add")
 
     def chosen(s, h):
-        return IND(R("q%d" % s, NW * h, 10 * NW), of(s, OKF))
+        return IND(R("q%d" % s, QH * h, QH * (7 + h)), of(s, OKF))
 
-    def small(o, x, scale, bias=None):
-        if SLIM & 4:
-            return ts(o, x, scale, "mult", bias, None if bias is None else "add")
-        return act(o, x, scale=scale, bias=bias)
+    def first_col(s, low, half):
+        tt(pin("p3", s, 6), pin("ps", s, 5), low, "subtract")
+        ts(of(s, OC0), pin("p3", s, 6), -0.5 if half else -1.0, "mult")
 
-    def hop(s, tab, wt, wend, co, c, nxt, even=None):
+    def hop(s, tab, wt, wend, co, nxt, even=None, turned=False):
         phase(s, "")
+        nc = NWS[s] // 16
         b0 = R(co, 2, 3)
+        win = R(wt, 0, wend)
         for j in range(4):
-            step = 8 >> j
             oc, ox = (OC0, OX0) if j == 0 else (OCOL, OXI)
             wt_, ws_ = (R(even, 0, 1024), R(even, 1024, 2048)) if even else (R(tab, 0, 2048), R(tab, 2048, 4096))
-            tg = B("tb" if PE0 & 1 and _two(wt_) else "tg", s)
+            pe_t = O["pe_dt"][rnd[0]]
+            tg = B("tb" if pe_t and _two(wt_) else "tg", s)
             act(tg, IND(wt_, of(s, oc)))
             sv = IND(ws_, of(s, oc))
-            if not FUSE_S[j]:
-                act(Qs(s, 1, 1), sv)
-                sv = Qs(s, 1, 1)
-            vote(s, tg, sv, IND(R(wt, 0, wend[0]), of(s, ox)), b0)
-            ts(slot("sb", s, 0, j), cnt(s), 8.5, "is_ge", 2.0 * step, "mult")
-            o, x, y = R("so%d" % s, 0, 5 * NC), R("sa%d" % s, 0, 5 * NC), R("sb%d" % s, 5 * NC * j, 5 * NC * (j + 1))
-            add("v", "scan", (o, x, y, "subtract", "min"), [x, y], [o])
-            if even and j < 3:
-                ts(of(s, OCOL), slot("so", s, 4), float(step), "subtract", 0.5, "mult")
+            if j == 0 and turned:
+                act(B("sg", s), sv)
+                vote_turned(s, IND(win, of(s, ox)), b0, pin("ps", s, 1), O["split"])
+                for h in (0, 1):
+                    act(B("s1", s, h), chosen(s, h))
+                    to_psum(s, h)
             else:
-                ts(of(s, OCOL), slot("so", s, 4), float(step), "subtract")
+                if not O["fuse_s"][j]:
+                    act(B("sg", s), sv)
+                    sv = B("sg", s)
+                vote(s, tg, sv, IND(win, of(s, ox)), b0, pin("ps", s, 1), O["split"], False, pe_t)
+            scan(res("ps", s), PS("ps", s), R("cs", 7 * NM * j, 7 * NM * j + 7 * nc))
+            ts(of(s, OCOL), res("ps", s, 5), -0.5 if even and j < 3 else -1.0, "mult")
             if j == 3:
-                cp(of(s, OCOL1), slot("so", s, 4))
-            ts(of(s, OXI), slot("so", s, 3), step - 1.0, "add")
-            small(slot("sa", s, 1), slot("so", s, 2), -1.0, R("cf", 16 + step, 17 + step))
-        if nxt is not None:
-            small(st(s, NL), slot("so", s, 2), -1.0, R("cf", 9, 10))
-            small(st(s, N2), slot("so", s, 2), -2.0, R("cf", 9, 10))
-        levels(s, tab, True)
-        vote(s, Qs(s, 0, 4), Qs(s, 1, 4), IND(R(wt, 1024, wend[1]), of(s, OXI)), b0)
-        if SLIM & 1:
-            ts(st(s, KQ), cnt(s), 8.5, "is_ge", 1024.0, "mult")
-            tt(st(s, XI), slot("so", s, 3), st(s, KQ), "add")
-            cp(of(s, OKQ, 2), st(s, KQ, 2))
-            kq = st(s, KQ)
-            act(fslot("fb", s, 0), kq, scale=NW / 256)
-        else:
-            kq = fslot("fb", s, 0) if NW == 256 else st(s, KQ)
-            ts(of(s, OKQ), cnt(s), 8.5, "is_ge", 1024.0, "mult")
-            ts(kq, cnt(s), 8.5, "is_ge", 1024.0, "mult")
-            tt(st(s, XI), slot("so", s, 3), kq, "add")
-            cp(of(s, OXR), st(s, XI))
-            if NW != 256:
-                act(fslot("fb", s, 0), kq, scale=NW / 256)
+                ts(of(s, OCOL1), res("ps", s, 5), -1.0, "mult", 1.0, "add")
+                ts(of(s, OXI), res("ps", s, 6), 0.5, "add", 8.0, "mult")
+            else:
+                ts(of(s, OXI), res("ps", s, 6), 8.0, "mult")
+            if j < 3 or nxt is not None:
+                act(pin("ps", s, 3), res("ps", s, 4), scale=-1.0)
+        act(pin("p3", s, 5), res("ps", s, 4), scale=-1.0 if nxt is None else -2.0)
+        for p in ("p1", "p2"):
+            act(pin(p, s, 5), res("ps", s, 6), scale=-1.0)
         if nxt == "home":
-            first_col(s, HOME)
-        elif nxt is not None:
-            cast_of(s, nxt)
-            first_col(s, C128)
-        for j, h in ((1, 4), (2, 2)):
-            at_depth(s, of(s, OKQ), 128 * h, [Qs(s, x, 4 + j) for x in range(3)])
-            vote(s, Qs(s, 0, 4 + j), Qs(s, 1, 4 + j), IND(R(wt, 128 * h, wend[1]), of(s, OXR)), b0)
-            if j == 1:
-                ts(st(s, PP), cnt(s), 8.5, "is_ge", 128.0 * h, "mult")
-                tt(st(s, KQ), kq, st(s, PP), "add")
-                tt(st(s, XI), st(s, XI), st(s, PP), "add")
-                cp(of(s, OKQ, 2), st(s, KQ, 2))
-                small(fslot("fb", s, 1), st(s, PP), 6.0 * NW / 512)
-            else:
-                ts(fslot("fb", s, 2), cnt(s), 8.5, "is_ge", 8.0 * NW, "mult")
-                if SLIM & 2:
-                    act(st(s, PP), fslot("fb", s, 2), scale=32.0 / NW)
-                else:
-                    ts(st(s, PP), cnt(s), 8.5, "is_ge", 128.0 * h, "mult")
-                tt(st(s, KQ), st(s, KQ), st(s, PP), "add")
-        o, x, y = R("fo%d" % s, 0, 4 * NC), R("fa%d" % s, 0, 4 * NC), R("fb%d" % s, 0, 4 * NC)
-        add("v", "scan", (o, x, y, "add", "max"), [x, y], [o])
-        cp(of(s, OKF), fslot("fo", s, 3))
+            act(pin("ps", s, 5), wrapped(64, s))
+        levels(s, tab)
+        for h in (1, 0):
+            tt(Qs(s, h, 1), PH(s, h), Qs(s, h, 0), "add")
+        for v, p in enumerate(("p1", "p2", "p3")):
+            if v:
+                at_depth(s, of(s, OKQ), [Qs(s, h, v + 1) for h in (0, 1)])
+            vote(s, Qs(s, 0, v + 1), Qs(s, 1, v + 1), IND(win, of(s, OXR if v else OXI)), b0, pin(p, s, 1), O["rsplit"], O["pe_ds"][rnd[0]])
+            scan(res(p, s), PS(p, s), R("cr", RA[v], RA[v] + RW[v] * nc))
+            if v < 2:
+                ts(of(s, OKQ), res(p, s, 4), 16.0, "mult")
+                ts(of(s, OXR), res(p, s, 5), -8.0, "mult")
+            if v == 0:
+                x, o = res("p1", s), PS("p2", s)
+                act(R(o[0], o[1], o[2] - 1, 2), R(x[0], x[1], x[2] - 1, 2), bias=R("cf", 10, 11))
+                if nxt not in (None, "home"):
+                    act(B("cug", s), IND(R(nxt, 0, 2048), of(s, OCOL)))
+                    count(s, pin("ps", s, 5), "cug%d" % s, False)
+                if nxt is not None:
+                    first_col(s, res("ps", s, 4), False)
+            elif v == 1:
+                for e in (2, 4):
+                    act(pin("p3", s, e), res("p2", s, e))
+        ts(of(s, OKF), res("p3", s, 2), 0.125, "subtract")
         if nxt is not None:
-            tt(st(s, VX), st(s, KQ), st(s, N2), "add")
-            cp(of(s, OX0), st(s, VX))
-            tt(slot("sa", s, 3), st(s, KQ), st(s, NL), "add")
-            tt(slot("sa", s, 4), slot("sa", s, 3), cst(s, HOME if nxt == "home" else C128), "add")
-            act(B("s1", s, 1), chosen(s, 1))
-            act(B("s1", s), chosen(s, 0))
-            if MERGE & 16:
-                act(R("pa%d" % s, 0, 2 * NW), R("s1%d" % s, 0, 2 * NW))
-            else:
-                act(B("pa", s), B("s1", s))
-                act(B("pa", s, 1), B("s1", s, 1))
+            ts(of(s, OX0), res("p3", s, 5), -8.0, "mult")
+            act(pin("ps", s, 6), res("p3", s, 6))
+            if not O["first"]:
+                for h in (1, 0):
+                    act(B("s1", s, h), chosen(s, h))
+                for h in (0, 1):
+                    to_psum(s, h)
 
     def finish(s, rnd, out):
         for h in (1, 0):
-            a = 2048 * h + 4 * NW * s + rnd
-            old = R("own0", a, a + 4 * NW - 3, 4)
+            a = 2048 * h + 4 * I0[s] + rnd
+            old = R("own0", a, a + 4 * NWS[s] - 3, 4)
             df = B(("tg", "wg")[h], s)
             tt(df, chosen(s, h), old, "subtract")
-            if FIN_V >> h & 1:
-                ts(PS(s, h, 0), df, 0.25, "mult")
-            else:
-                act(PS(s, h, 0), df, scale=0.25)
-            tt(R(out, 512 * h + NW * s, 512 * h + NW * (s + 1)), PS(s, h, 0), old, "add")
+            act(PH(s, h), df, scale=0.25)
+            tt(R(out, 512 * h + I0[s], 512 * h + I0[s] + NWS[s]), PH(s, h), old, "add")
 
-    def depart(s):
-        ts(st(s, T1), slot("sa", s, 1), -16.0, "mult")
-        tt(st(s, T1), st(s, T1), di(s, 0), "subtract")
-        ts(st(s, T2), st(s, KQ), 1.0 / 128, "mult")
-        tt(di(s, 1), st(s, T1), st(s, T2), "add")
+    def depart(s, out):
+        ts(st(s, T1), res("p3", s, 5), -16.0, "mult")
+        tt(di(s, 1), st(s, T1), di(s, 0), "subtract")
         ts(di(s, 2), di(s, 1), 1, "arith_shift_right")
-        tt(di(s, 0), di(s, 0), di(s, 2), "add")
+        tt(out, di(s, 0), di(s, 2), "add")
 
     def spread(f, src, s, h, on):
-        a = 2048 * h + 1024 * s
-        (cp if on == "v" else act)(R(f, a, a + 1024 - 3, 4), R(src, 512 * h + 256 * s, 512 * h + 256 * (s + 1)))
+        a = 2048 * h + 4 * I0[s]
+        (cp if on == "v" else act)(R(f, a, a + 4 * NWS[s] - 3, 4), R(src, 512 * h + I0[s], 512 * h + I0[s] + NWS[s]))
+
+    def casts(s):
+        return 128 * (I0[s] // 32), 128 * -(-(I0[s] + NWS[s]) // 32)
 
     def start(s, half):
-        tt(slot("sa", s, 3), st(s, T1), slot("sa", s, 1), "add")
-        tt(st(s, VX), slot("sa", s, 3), slot("sa", s, 1), "add")
-        ts(of(s, OX0), st(s, VX), 1.0, "subtract")
-        tt(st(s, VC0), st(s, HOME), slot("sa", s, 1), "subtract")
-        cp(of(s, OCOL), st(s, VC0))
-        ts(of(s, OCOL1), st(s, VC0), 1.0, "add")
-        cast_of(s, "cu0")
-        first_col(s, C128, half)
-        tt(slot("sa", s, 4), slot("sa", s, 3), cst(s, C128), "add")
+        a, b = casts(s)
+        act(pin("ps", s, 3), st(s, NL), scale=-1.0)
+        tt(st(s, V1), st(s, NL), wrapped(64, s), "subtract")
+        ts(of(s, OCOL), st(s, V1), float(a), "subtract")
+        if not half:
+            ts(of(s, OCOL1), st(s, V1), a - 1.0, "subtract")
+        tt(st(s, VX), st(s, DX), st(s, NL), "add")
+        ts(of(s, OX0), st(s, VX), 8.0, "mult")
+        act(B("cug", s), IND(R("cu0", a, b), of(s, OCOL)))
+        count(s, pin("ps", s, 5), "cug%d" % s, False)
+        first_col(s, st(s, NL), half)
+        tt(pin("ps", s, 6), pin("ps", s, 5), st(s, DX), "add")
 
     for s in range(NST):
         cur[0] = s
-        ms(R("sa%d" % s, 0, 5 * NC), BIG)
-        ms(slot("sa", s, 2), 0.0)
-        if s == 0:
-            ms(R("sb0", 0, 20 * NC), BIG)
-            for j in range(4):
-                ms(slot("sb", s, 1, j), -float(8 >> j))
-                ms(slot("sb", s, 2, j), 126.0 + (8 >> j))
-            for x in range(1, NST):
-                act(R("sb%d" % x, 0, 20 * NC), R("sb0", 0, 20 * NC))
-        iota(st(s, HOME), [[128, NC // 2], [0, 2]], 4 * NW * s, 0)
-        ts(slot("sa", s, 1), R("cf", 32, 32 + NC), R("cf", 8, 9), "add")
-        ts(di(s, 0), slot("sa", s, 1), -16.0, "mult")
-        ms(st(s, T1), 256.0)
+        nc = NWS[s] // 16
+        for p, (a, w) in SW.items():
+            act(PS(p, s), R("tp", a * NM, a * NM + w * nc))
+        ts(di(s, 0), wrapped(32, s), R("cf", 8, 9), "add")
+        ts(st(s, NL), di(s, 0), 0.0625, "mult")
+        ts(st(s, DX), di(s, 0), 0.0625, "mult")
         start(s, True)
-        act(B("pa", s), R("own0", 4 * NW * s, 4 * NW * (s + 1) - 3, 4))
-        act(B("s1", s, 1), R("own0", 2048 + 4 * NW * s, 2048 + 4 * NW * (s + 1) - 3, 4))
-        act(B("pa", s, 1), B("s1", s, 1))
-        ms(R("fa%d" % s, 0, 4 * NC), 0.0)
-        ms(fslot("fa", s, 0), -BIG)
-        ts(fslot("fa", s, 3), R("cf", 48, 48 + NC), R("cf", 10, 11), "add")
-        ms(R("fb%d" % s, 0, 4 * NC), -BIG)
+        act(P1(s, 0), R("own0", 4 * I0[s], 4 * (I0[s] + NWS[s]) - 3, 4))
+        if O["pe_dt"][0]:
+            act(B("s1", s, 0), R("own0", 4 * I0[s], 4 * (I0[s] + NWS[s]) - 3, 4))
+        act(B("s1", s, 1), R("own0", 2048 + 4 * I0[s], 2048 + 4 * (I0[s] + NWS[s]) - 3, 4))
+        to_psum(s, 1)
     for s in range(NST):
-        hop(s, "w1b", "wt1", (256, 2048), "misc1", C128, "cu1", "we1")
-        hop(s, "w4b", "wt4", (3840, 3840), "co4", C128, "home")
-        hop(s, "own0", "wt0", (3840, 3840), "misc", HOME, None)
+        hop(s, "w1b", "wt1", NX, "misc1", "cu1", "we1")
+        hop(s, "w4b", "wt4", NX, "co4", "home", turned=O["first"])
+        hop(s, "own0", "wt0", NX, "misc", None, turned=O["first"])
         finish(s, 0, "newb")
     phase(None, "m")
     arr = []
-    for s in range(2):
+    for s in range(NST):
         for h in (1, 0):
-            sn = send("mid%d" % (2 * s + h), [R("newb", 512 * h + 256 * s, 512 * h + 256 * (s + 1))], 1 << 17)
+            a, b = 512 * h + I0[s], 512 * h + I0[s] + NWS[s]
+            sn = send("mid%d" % (2 * s + h), [R("newb", a, b)], 512 * NWS[s])
             if arr:
                 ops[sn]["late"] = last_sn
             last_sn = sn
-            arr.append(arrive("an%d" % (2 * s + h), (2, 0), [R("new1", 512 * h + 256 * s, 512 * h + 256 * (s + 1))], [sn], 1, 1 << 16))
-    s_n = send("mid4", [R("newb", 0, 1024)], 0, arr)
-    arrive("an4", (0, 1), [R("new4", 0, 1024)], [s_n], 0, 1 << 19)
+            arr.append(arrive("an%d" % (2 * s + h), (2, 0), [R("new1", a, b)], [sn], 1, 256 * NWS[s], (R("newb", a, b), 1)))
+    s_n = send("far", [R("newb", 0, 1024)], 0, arr)
+    arrive("af", (0, 1), [R("new4", 0, 1024)], [s_n], 0, 1 << 19, (R("newb", 0, 1024), 4))
     dma("y", R("new4s", 0, 1024, 1, 0, 112), R("new4", 0, 1024, 1, 16, 128))
     dma("y", R("new4s", 0, 1024, 1, 112, 128), R("new4", 0, 1024, 1, 0, 16))
-    for s in range(2):
+    for s in range(NST):
         for h in (0, 1):
             spread("f0", "newb", s, h, "s")
             spread("f1", "new1", s, h, "s" if h else "v")
             spread("f4", "new4s", s, h, "s")
+    rnd[0] = 1
     for s in range(NST):
         cur[0] = s
-        depart(s)
+        depart(s, di(s, 0))
         ts(di(s, 1), di(s, 0), 4, "arith_shift_right")
-        ts(slot("sa", s, 1), di(s, 1), -1.0, "mult")
+        cp(st(s, NL), di(s, 1))
         ts(di(s, 2), di(s, 0), 15, "bitwise_and")
-        ts(st(s, KQ), di(s, 2), 128.0, "mult")
-        cp(of(s, OKF), st(s, KQ))
+        cp(of(s, OKF), di(s, 2))
         ts(di(s, 3), di(s, 0), 1, "bitwise_and")
-        ts(st(s, T2), di(s, 3), 3712.0, "mult", 256.0, "add")
-        tt(st(s, T1), st(s, KQ), st(s, T2), "add")
+        ts(st(s, T1), di(s, 3), (2 * NX - 1) / 16.0, "mult")
+        ts(st(s, DX), di(s, 0), 0.0625, "mult")
+        tt(st(s, DX), st(s, DX), st(s, T1), "add")
         start(s, False)
-        levels(s, "f0", False)
-        at_depth(s, of(s, OKF), 0, [B("pa", s), B("s1", s, 1)])
-        act(B("pa", s, 1), B("s1", s, 1))
+        levels(s, "f0", *casts(s))
+        at_depth(s, of(s, OKF), [P1(s, 0), B("s1", s, 1)])
+        to_psum(s, 1)
+        if O["pe_dt"][1]:
+            act(B("s1", s, 0), P1(s, 0))
     for s in range(NST):
-        hop(s, "f1", "wt1", (7680, 7680), "misc1", C128, "cu1")
-        hop(s, "f4", "wt4", (3840, 3840), "co4", C128, "home")
-        hop(s, "f0", "wt0", (3840, 3840), "misc", HOME, None)
+        hop(s, "f1", "wt1", 2 * NX, "misc1", "cu1")
+        hop(s, "f4", "wt4", NX, "co4", "home", turned=O["first"])
+        hop(s, "f0", "wt0", NX, "misc", None, turned=O["first"])
         finish(s, 1, "new1")
-        a, b = NW * (s + 1) - 256, NW * (s + 1)
-        for h, y in enumerate(("yt", "ys")):
-            if b % 256 == 0:
-                dma("y", R(y, a, b), R("new1", 512 * h + a, 512 * h + b))
-        depart(s)
-        cp(st(s, DF), di(s, 0))
-        g = [(R("pa%d" % s, b, NW, 16, 0, 8), R("ident", b, 128, 16), st(s, DF), True, True) for b in range(16)]
-        add("t", "mm", g, [R("ident", 0, 128), st(s, DF)], [B("pa", s)])
-        act(R("new4s", NW * s, NW * s + NW, 1, 0, 8), R("pa%d" % s, 0, NW, 1, 0, 8))
-        if NW * (s + 1) % 256 == 0:
-            dma("s", R("yd", a, NW * s + NW, 1, 0, 8), R("new4s", a, NW * s + NW, 1, 0, 8))
+        a, b = I0[s], I0[s] + NWS[s]
+        for h, y in ((1, "ys"), (0, "yt")):
+            dma("y", R(y, a, b), R("new1", 512 * h + a, 512 * h + b))
+        depart(s, st(s, DF))
+        o = P1(s, 0)
+        g = [(R(o[0], o[1] + e, o[2], 16, 0, 8), R("ident", e, 128, 16), st(s, DF), True, True) for e in range(16)]
+        add("t", "mm", g, [R("ident", 0, 128), st(s, DF)], [o])
+        act(R("new4s", a, b, 1, 0, 8), R(o[0], o[1], o[2], 1, 0, 8))
+        dma("s", R("yd", a, b, 1, 0, 8), R("new4s", a, b, 1, 0, 8))
     return ops
 
 
@@ -622,7 +675,7 @@ def order(ops, P, U):
     x = U["seed"]
     for i, o in enumerate(ops):
         x = (x * 1103515245 + 12345) % 2147483648
-        pri[i] += U["noise"] * x / 2147483648 + (U["lead"] * (NST - 1 - o["s"]) if o["s"] is not None else 0.0) + 1e9 * o.get("first", 0) + U["role"].get(o["role"], 0)
+        pri[i] += U["noise"] * x / 2147483648 - (U["lead"] * o["s"] if o["s"] is not None else 0.0) + 1e9 * o.get("first", 0) + U["role"].get(o["role"], 0)
     ready = [0.0] * n
     pool = {e: [] for e in "vstgy"}
     free = {e: 0.0 for e in "vstgy"}
@@ -667,13 +720,139 @@ def order(ops, P, U):
     return seq, end
 
 
-INORDER = 1
-POOL = {"v": 1, "s": 1, "t": 1, "g": 1} if INORDER else {"v": 32, "s": 32, "t": 8, "g": 6}
+def lags(ops, P):
+    cs = [cost(o, P) for o in ops]
+    pred = []
+    for o in ops:
+        p = {}
+        for d in o["soft"] + ([o["late"]] if "late" in o else []):
+            p[d] = cs[d][0]
+        for d in o["deps"] + o["sdeps"]:
+            same = ops[d]["e"] == o["e"] and ops[d]["k"] not in ("dma", "send")
+            p[d] = cs[d][1] + (P["same"] if same else P["wake"])
+        pred.append(list(p.items()))
+    return cs, pred
 
 
-def plan(U):
-    ops = build()
-    seq, end = order(ops, PAR, U)
+def place(seq, eng, hold, pred):
+    st = [0.0] * len(eng)
+    A, Z = {e: [] for e in "vstgy"}, {e: [] for e in "vstgy"}
+    for i in seq:
+        t = max([st[d] + l for d, l in pred[i]] + [0.0])
+        if eng[i] is not None:
+            a, z = A[eng[i]], Z[eng[i]]
+            k = len(z)
+            while k and z[k - 1] > t:
+                k -= 1
+            while k < len(a) and a[k] < t + hold[i]:
+                t = z[k]
+                k += 1
+            a.insert(k, t)
+            z.insert(k, t + hold[i])
+        st[i] = t
+    return st
+
+
+def squeeze(ops, P, end, rounds):
+    cs, pred = lags(ops, P)
+    n = len(ops)
+    hold, eng = [c[0] for c in cs], [o["e"] for o in ops]
+    back = [[] for _ in ops]
+    for j in range(n):
+        for d, l in pred[j]:
+            back[d].append((j, l + hold[j] - hold[d]))
+    back = [b or [(n, cs[i][1] - hold[i])] for i, b in enumerate(back)] + [[]]
+    st = [end[i] - cs[i][1] for i in range(n)]
+    best = (max(end), st)
+    for _ in range(rounds):
+        rs = place([n] + sorted(range(n), key=lambda i: -st[i] - hold[i]), eng + [None], hold + [0], back)
+        st = place(sorted(range(n), key=lambda i: -rs[i] - hold[i]), eng, hold, pred)
+        best = min(best, (max(st[i] + cs[i][1] for i in range(n)), st))
+    return best[0], sorted(range(n), key=lambda i: best[1][i])
+
+
+def swaps(ops, P, seq, turns):
+    cs, pred = lags(ops, P)
+    n = len(ops)
+    hold, lat = [c[0] for c in cs], [c[1] for c in cs]
+    succ = [[] for _ in ops]
+    for j in range(n):
+        for d, l in pred[j]:
+            succ[d].append((j, l))
+    direct = [set(d for d, _ in p) for p in pred]
+    mp, mn, last, seq = [-1] * n, [-1] * n, {}, list(seq)
+    for i in seq:
+        e = ops[i]["e"]
+        if e in last and e is not None:
+            mp[i], mn[last[e]] = last[e], i
+        last[e] = i
+    pos = {i: k for k, i in enumerate(seq)}
+    head, tail = [0.0] * n, [0.0] * n
+
+    def early(i, t):
+        for d, l in pred[i]:
+            if head[d] + l > t:
+                t = head[d] + l
+        return t
+
+    def late(i, t):
+        for d, l in succ[i]:
+            if tail[d] + l > t:
+                t = tail[d] + l
+        return t
+
+    def mend(a, b):
+        for i in seq[a:]:
+            head[i] = early(i, head[mp[i]] + hold[mp[i]] if mp[i] >= 0 else 0.0)
+        for i in seq[b::-1]:
+            tail[i] = late(i, max(lat[i], tail[mn[i]] + hold[i]) if mn[i] >= 0 else lat[i])
+        return max(head[i] + lat[i] for i in range(n))
+
+    now = mend(0, n - 1)
+    best, barred, x = (now, list(seq), list(head)), {}, 1
+    for turn in range(turns):
+        cand = []
+        for v in range(n):
+            u = mp[v]
+            if head[v] + tail[v] > now - 1e-6 and u >= 0 and head[u] + hold[u] > head[v] - 1e-6 and u not in direct[v]:
+                hv = early(v, head[mp[u]] + hold[mp[u]] if mp[u] >= 0 else 0.0)
+                tu = late(u, max(lat[u], tail[mn[v]] + hold[u]) if mn[v] >= 0 else lat[u])
+                est = max(hv + late(v, max(lat[v], tu + hold[v])), early(u, hv + hold[v]) + tu)
+                x = (x * 1103515245 + 12345) % 2147483648
+                if barred.get((v, u), 0) <= turn or est < best[0] - 1e-6:
+                    cand.append((est + 30.0 * x / 2147483648, u, v))
+        if not cand:
+            barred.clear()
+            continue
+        _, u, v = min(cand)
+        a, b = mp[u], mn[v]
+        if a >= 0:
+            mn[a] = v
+        if b >= 0:
+            mp[b] = u
+        mp[v], mn[v], mp[u], mn[u] = a, u, v, b
+        barred[(u, v)] = turn + 8 + (x >> 8) % 13
+        pu, pv = pos[u], pos[v]
+        behind, lo, hi = {u}, [], [u]
+        for i in seq[pu + 1:pv + 1]:
+            if i != v and (direct[i] & behind or mp[i] in behind):
+                behind.add(i)
+                hi.append(i)
+            else:
+                lo.append(i)
+        seq[pu:pv + 1] = lo + hi
+        for k in range(pu, pv + 1):
+            pos[seq[k]] = k
+        now = mend(pu, pv)
+        if now < best[0] - 1e-6:
+            best = (now, list(seq), list(head))
+    return best[1], [best[2][i] + lat[i] for i in range(n)]
+
+
+def plan(O, U):
+    ops = build(O)
+    tries = [squeeze(ops, PAR, order(ops, PAR, dict(U, lead=lead, look=look))[1], U["rounds"]) for lead in U["leads"] for look in U["looks"]]
+    seq, end = swaps(ops, PAR, min(tries)[1], U["turns"])
     known = {e: 0 for e in "vstgy"}
     K, waits, raised, before, pre = {}, {}, set(), {}, {e: 0 for e in "vstgy"}
     for i in seq:
@@ -688,10 +867,10 @@ def plan(U):
                 raised.add(d)
                 known[e] |= K[d] | (1 << d) | before.get(d, 0)
         K[i], waits[i] = known[e], w
-        if INORDER and ops[i]["k"] not in ("dma", "send"):
+        if ops[i]["k"] not in ("dma", "send"):
             before[i] = pre[e]
             pre[e] |= (1 << i) | K[i]
-    sem, names, turn, last, tail = {}, [], {e: 0 for e in POOL}, {}, []
+    sem, names, turn, tail = {}, [], {e: 0 for e in "vstg"}, []
     for i in seq:
         o = ops[i]
         if o["k"] == "dma":
@@ -700,20 +879,16 @@ def plan(U):
             if i not in raised:
                 tail.append(i)
         elif o["k"] not in ("arr", "send") and i in raised:
-            e = o["e"]
-            nm = "%s%d" % (e, turn[e] % POOL[e])
-            sem[i] = (nm, turn[e] // POOL[e] + 1)
-            turn[e] += 1
-            if not INORDER and nm in last and not K[i] >> last[nm] & 1:
-                waits[i].append(last[nm])
-            last[nm] = i
-    names += ["%s%d" % (e, k) for e in POOL for k in range(POOL[e])]
+            turn[o["e"]] += 1
+            sem[i] = (o["e"] + "0", turn[o["e"]])
+    names += [e + "0" for e in "vstg"]
     return ops, seq, waits, sem, names, tail, end
 
 
-OPS, SEQ, WAITS, SEM, _NAMES, TAIL, END = plan(TUNE)
-SEMAPHORES = _NAMES + ["am0", "am1", "am4", "ae0", "ae1", "ab0", "ab1", "ab4", "an0", "an1", "an2", "an3", "an4",
-                       "sent", "rm", "re0", "re1", "rb0", "rf", "rn0", "rn1"]
+OPS, SEQ, WAITS, SEM, _NAMES, TAIL, END = plan(OPT, TUNE)
+NST = len(OPT["nw"])
+SEMAPHORES = (_NAMES + ["am0", "am1", "am4", "ae0", "ae1", "ab0", "ab1", "ab4", "af", "sent", "rm", "re0", "re1", "rb0", "rf"]
+              + ["an%d" % k for k in range(2 * NST)] + ["rn%d" % k for k in range(NST)])
 
 
 def bits(es):
@@ -736,8 +911,9 @@ def piece(T, kind, k, landed):
         return T["w1b" if landed else "own0"][:, 1024 * k:1024 * k + 1024]
     if kind == "f":
         return T["w4b" if landed else "stage4"][:, 2048 * k:2048 * k + 2048]
-    a = 512 * (k // 2 % 2) + 256 * (k // 4) + 128 * (k % 2)
-    return T["new1" if landed else "newb"][:, a:a + 128]
+    w = OPT["nw"][k // 4] // 2
+    a = 512 * (k // 2 % 2) + sum(OPT["nw"][:k // 4]) + w * (k % 2)
+    return T["new1" if landed else "newb"][:, a:a + w]
 
 
 def relay_program(g, core, T, topo, src, down, far, k):
@@ -748,7 +924,7 @@ def relay_program(g, core, T, topo, src, down, far, k):
              ("e", k + 4, half, down, "ae1", "re1"), ("b", k, half, down, "ab%d" % (k // 2), "rb0")]
     if k == 1:
         steps.append(("f", 1, rest, far, "ab4", "rf"))
-    steps += [("n", k, half, down, "an%d" % (k // 2), "rn0"), ("n", k + 4, half, down, "an%d" % (k // 2 + 2), "rn1")]
+    steps += [("n", k + 4 * s, half, down, "an%d" % (k // 2 + 2 * s), "rn%d" % s) for s in range(NST)]
     total = 0
     for kind, j, n, dst, sem, got in steps:
         rid, pid = topo.addr(dst, core)
@@ -780,7 +956,7 @@ def rank_program(g, core, T, topo):
     Q = {"v": g.vector, "s": g.scalar, "t": g.tensor, "g": g, "y": g.sync}
     A, F = AluOpType, ActivationFunctionType
     alu = {"add": A.add, "subtract": A.subtract, "mult": A.mult, "max": A.max, "min": A.min, "is_ge": A.is_ge, "is_gt": A.is_gt,
-           "is_equal": A.is_equal, "arith_shift_right": A.arith_shift_right, "bitwise_and": A.bitwise_and}
+           "is_lt": A.is_lt, "is_equal": A.is_equal, "arith_shift_right": A.arith_shift_right, "bitwise_and": A.bitwise_and}
     sent = [0]
 
     def ap(r):
@@ -805,8 +981,8 @@ def rank_program(g, core, T, topo):
         elif what == "bulk4":
             ts_ = [tr(far, piece(T, "f", 0, False), piece(T, "f", 0, True), "ab4", off),
                    tr(rel[1], piece(T, "f", 1, False), piece(T, "f", 1, True), "rf", only_on)]
-        elif what == "mid4":
-            ts_ = [tr(far, T.newb[:], T.new4[:], "an4", off)]
+        elif what == "far":
+            ts_ = [tr(far, T.newb[:], T.new4[:], "af", off)]
         else:
             kind, h = {"b": "b", "e": "e", "m": "n"}[what[0]], int(what[-1])
             ts_ = [tr(rel[(2 * h + j) % NREL], piece(T, kind, 2 * h + j, False), piece(T, kind, 2 * h + j, True), "r%s%d" % (kind, h // 2), on[j::2])
@@ -842,10 +1018,8 @@ def rank_program(g, core, T, topo):
         elif k == "ms":
             ins = q.memset(ap(a[0]), a[1])
         elif k == "act":
-            if a[2] == "relu":
-                ins = q.activation(ap(a[0]), ap(a[1]), F.Relu, bias=ap(a[3]))
-            elif a[3] is not None:
-                ins = q.activation(ap(a[0]), ap(a[1]), F.Identity, bias=ap(a[3]), scale=1.0 if a[2] is None else a[2])
+            if a[3] is not None:
+                ins = q.activation(ap(a[0]), ap(a[1]), F.Identity, bias=ap(a[3]))
             elif a[2] is not None:
                 ins = q.activation(ap(a[0]), ap(a[1]), F.Copy, scale=ap(a[2]))
             else:

@@ -2,17 +2,17 @@ import math
 from concourse.bass import DstId, RemoteDMATransfer
 from concourse.mybir import AluOpType, ActivationFunctionType
 
-OPT = dict(nw=(256, 256),
+OPT = dict(nw=(176, 176, 160),
            fuse_s=(1, 1, 1, 1),
            fuse_n=(1, 1),
            first=0,
-           pe_copy=(0, 0),
+           pe_copy=(0, 1),
            pe_ds=(0, 0),
            pe_dt=(0, 0),
            pe_h=((0, 0), (0, 0)),
            split=("mul", "yes", "sub", "rr"), rsplit=("yes", "mul", "rr", "sub", "ds"), wt4_v=0)
 NREL = 4
-TUNE = dict(lead=2000.0, look=100.0, noise=0.0, seed=1, role={}, leads=(1000.0, 2000.0), looks=(0.0, 100.0), rounds=15, turns=3000)
+TUNE = dict(lead=600.0, look=0.0, noise=0.0, seed=1, role={}, leads=(600.0, 1400.0, 2000.0), widths=(120, 80, 160, 100), turns=300)
 PAR = dict(fix=0.0, fixs=0.0, fuse=0.0, cyc=0.95, g=1.56, wake=200.0, same=180.0, pe=0.5, dma=2000.0, bw=160.0, call=900.0, leg=2500.0, link=45.0)
 BIG = 1.0e6
 ALPHA = 4096.0
@@ -37,6 +37,7 @@ def layout(O):
         "misc4": ("sbuf", [128, 33], "float32"), "co4": ("sbuf", [128, 4], "float32"),
         "newb": ("sbuf", [128, 1024], "float32"), "new1": ("sbuf", [128, 1024], "float32"),
         "new4": ("sbuf", [128, 1024], "float32"), "new4s": ("sbuf", [128, 1024], "float32"),
+        "st": ("sbuf", [128, 6 * 32], "float32"), "di": ("sbuf", [128, 4 * 32], "int32"),
         "ci": ("sbuf", [128, 32], "int32"), "cf": ("sbuf", [128, 128], "float32"),
         "cs": ("sbuf", [128, 28 * 16], "float32"), "cr": ("sbuf", [128, 19 * 16], "float32"), "tp": ("sbuf", [128, 26 * 16], "float32"),
     }
@@ -52,9 +53,7 @@ def layout(O):
         S["cug%d" % s] = ("sbuf", [128, nw], "bfloat16")
         S["tb%d" % s] = ("sbuf", [128, nw], "bfloat16")
         S["hb%d" % s] = ("sbuf", [128, 2 * nw], "bfloat16")
-        S["st%d" % s] = ("sbuf", [128, 8 * nc], "float32")
         S["so%d" % s] = ("sbuf", [128, 26 * nc], "float32")
-        S["di%d" % s] = ("sbuf", [128, 4 * nc], "int32")
         S["of%d" % s] = ("sbuf", [128, 8 * 16], "uint16")
     for b in range(8):
         S["bank%d" % b] = ("psum", [128, 512], "float32")
@@ -366,14 +365,15 @@ def build(O):
     OCOL, OXI, OCOL1, OKQ, OXR, OC0, OX0, OKF = range(8)
     SW = {"ps": (0, 7), "p1": (7, 6), "p2": (13, 6), "p3": (19, 7)}
 
-    def st(s, i):
-        return R("st%d" % s, NWS[s] // 16 * i, NWS[s] // 16 * (i + 1))
+    def st(s, i, name="st"):
+        a, b = (0, 32) if s is None else (I0[s] // 16, (I0[s] + NWS[s]) // 16)
+        return R(name, 32 * i + a, 32 * i + b)
 
     def of(s, i):
         return R("of%d" % s, 16 * i, 16 * i + NWS[s] // 16)
 
-    def di(s, i):
-        return R("di%d" % s, NWS[s] // 16 * i, NWS[s] // 16 * (i + 1))
+    def di(i, s=None):
+        return st(s, i, "di")
 
     def B(name, s, h=0):
         return R("%s%d" % (name, s), NWS[s] * h, NWS[s] * (h + 1))
@@ -416,7 +416,7 @@ def build(O):
             act(P1(s, h), B("s1", s, h))
 
     def vote(s, tv, sv, w, b0, z, sp, pe_s=False, pe_t=False):
-        ds, m = B("ds", s), PS("m0", s)
+        ds, m = B("ds", s), PS("ht" if pe_t else "m0", s)
         if sv[0] == "ind":
             tt(ds, sv, B("s1", s, 1), "subtract")
         elif pe_s:
@@ -486,7 +486,7 @@ def build(O):
         for j in range(4):
             oc, ox = (OC0, OX0) if j == 0 else (OCOL, OXI)
             wt_, ws_ = (R(even, 0, 1024), R(even, 1024, 2048)) if even else (R(tab, 0, 2048), R(tab, 2048, 4096))
-            pe_t = O["pe_dt"][rnd[0]]
+            pe_t = O["pe_dt"][rnd[0]] >> j & 1
             tg = B("tb" if pe_t and _two(wt_) else "tg", s)
             act(tg, IND(wt_, of(s, oc)))
             sv = IND(ws_, of(s, oc))
@@ -556,11 +556,12 @@ def build(O):
             act(PH(s, h), df, scale=0.25)
             tt(R(out, 512 * h + I0[s], 512 * h + I0[s] + NWS[s]), PH(s, h), old, "add")
 
-    def depart(s, out):
-        ts(st(s, T1), res("p3", s, 5), -16.0, "mult")
-        tt(di(s, 1), st(s, T1), di(s, 0), "subtract")
-        ts(di(s, 2), di(s, 1), 1, "arith_shift_right")
-        tt(out, di(s, 0), di(s, 2), "add")
+    def depart(out):
+        for s in range(NST):
+            act(st(s, T1), res("p3", s, 5), scale=-16.0)
+        tt(di(1), st(None, T1), di(0), "subtract")
+        ts(di(2), di(1), 1, "arith_shift_right")
+        tt(out, di(0), di(2), "add")
 
     def spread(f, src, s, h, on):
         a = 2048 * h + 4 * I0[s]
@@ -569,29 +570,31 @@ def build(O):
     def casts(s):
         return 128 * (I0[s] // 32), 128 * -(-(I0[s] + NWS[s]) // 32)
 
-    def start(s, half):
+    def start(s, half, dx):
         a, b = casts(s)
+        if s == 0:
+            tt(st(None, V1), st(None, NL), R("cf", 64, 96), "subtract")
+            tt(st(None, VX), st(None, dx), st(None, NL), "add")
         act(pin("ps", s, 3), st(s, NL), scale=-1.0)
-        tt(st(s, V1), st(s, NL), wrapped(64, s), "subtract")
         ts(of(s, OCOL), st(s, V1), float(a), "subtract")
         if not half:
             ts(of(s, OCOL1), st(s, V1), a - 1.0, "subtract")
-        tt(st(s, VX), st(s, DX), st(s, NL), "add")
         ts(of(s, OX0), st(s, VX), 8.0, "mult")
         act(B("cug", s), IND(R("cu0", a, b), of(s, OCOL)))
         count(s, pin("ps", s, 5), "cug%d" % s, False)
         first_col(s, st(s, NL), half)
-        tt(pin("ps", s, 6), pin("ps", s, 5), st(s, DX), "add")
+        tt(pin("ps", s, 6), pin("ps", s, 5), st(s, dx), "add")
 
+    ts(di(0), R("cf", 32, 64), R("cf", 8, 9), "add")
+    ts(st(None, NL), di(0), 0.0625, "mult")
     for s in range(NST):
         cur[0] = s
         nc = NWS[s] // 16
         for p, (a, w) in SW.items():
             act(PS(p, s), R("tp", a * NM, a * NM + w * nc))
-        ts(di(s, 0), wrapped(32, s), R("cf", 8, 9), "add")
-        ts(st(s, NL), di(s, 0), 0.0625, "mult")
-        ts(st(s, DX), di(s, 0), 0.0625, "mult")
-        start(s, True)
+        if NWS[s] < QH:
+            ms(R("q%d" % s, NWS[s], 8 * QH), 0.0)
+        start(s, True, NL)
         act(P1(s, 0), R("own0", 4 * I0[s], 4 * (I0[s] + NWS[s]) - 3, 4))
         if O["pe_dt"][0]:
             act(B("s1", s, 0), R("own0", 4 * I0[s], 4 * (I0[s] + NWS[s]) - 3, 4))
@@ -605,13 +608,13 @@ def build(O):
     phase(None, "m")
     arr = []
     for s in range(NST):
+        new = [R("newb", 512 * h + I0[s], 512 * h + I0[s] + NWS[s]) for h in (0, 1)]
+        sn = send("mid%d" % s, new, 1024 * NWS[s])
+        if arr:
+            ops[sn]["late"] = last_sn
+        last_sn = sn
         for h in (1, 0):
-            a, b = 512 * h + I0[s], 512 * h + I0[s] + NWS[s]
-            sn = send("mid%d" % (2 * s + h), [R("newb", a, b)], 512 * NWS[s])
-            if arr:
-                ops[sn]["late"] = last_sn
-            last_sn = sn
-            arr.append(arrive("an%d" % (2 * s + h), (2, 0), [R("new1", a, b)], [sn], 1, 256 * NWS[s], (R("newb", a, b), 1)))
+            arr.append(arrive("an%d" % (2 * s + h), (2, 0), [("new1",) + new[h][1:]], [sn], 1, 256 * NWS[s], (new[h], 1)))
     s_n = send("far", [R("newb", 0, 1024)], 0, arr)
     arrive("af", (0, 1), [R("new4", 0, 1024)], [s_n], 0, 1 << 19, (R("newb", 0, 1024), 4))
     dma("y", R("new4s", 0, 1024, 1, 0, 112), R("new4", 0, 1024, 1, 16, 128))
@@ -619,23 +622,23 @@ def build(O):
     for s in range(NST):
         for h in (0, 1):
             spread("f0", "newb", s, h, "s")
-            spread("f1", "new1", s, h, "s" if h else "v")
+            spread("f1", "new1", s, h, "v" if h and s == NST - 1 else "s")
             spread("f4", "new4s", s, h, "s")
     rnd[0] = 1
+    depart(di(0))
+    ts(di(1), di(0), 4, "arith_shift_right")
+    cp(st(None, NL), di(1))
+    ts(di(2), di(0), 15, "bitwise_and")
+    ts(di(3), di(0), 1, "bitwise_and")
+    ts(st(None, T1), di(3), 2.0 * NX - 1, "mult")
+    tt(st(None, T1), st(None, T1), di(0), "add")
+    act(st(None, DX), st(None, T1), scale=0.0625)
     for s in range(NST):
         cur[0] = s
-        depart(s, di(s, 0))
-        ts(di(s, 1), di(s, 0), 4, "arith_shift_right")
-        cp(st(s, NL), di(s, 1))
-        ts(di(s, 2), di(s, 0), 15, "bitwise_and")
-        cp(of(s, OKF), di(s, 2))
-        ts(di(s, 3), di(s, 0), 1, "bitwise_and")
-        ts(st(s, T1), di(s, 3), (2 * NX - 1) / 16.0, "mult")
-        ts(st(s, DX), di(s, 0), 0.0625, "mult")
-        tt(st(s, DX), st(s, DX), st(s, T1), "add")
-        start(s, False)
+        cp(of(s, OKQ), di(2, s))
+        start(s, False, DX)
         levels(s, "f0", *casts(s))
-        at_depth(s, of(s, OKF), [P1(s, 0), B("s1", s, 1)])
+        at_depth(s, of(s, OKQ), [P1(s, 0), B("s1", s, 1)])
         to_psum(s, 1)
         if O["pe_dt"][1]:
             act(B("s1", s, 0), P1(s, 0))
@@ -647,12 +650,13 @@ def build(O):
         a, b = I0[s], I0[s] + NWS[s]
         for h, y in ((1, "ys"), (0, "yt")):
             dma("y", R(y, a, b), R("new1", 512 * h + a, 512 * h + b))
-        depart(s, st(s, DF))
-        o = P1(s, 0)
-        g = [(R(o[0], o[1] + e, o[2], 16, 0, 8), R("ident", e, 128, 16), st(s, DF), True, True) for e in range(16)]
-        add("t", "mm", g, [R("ident", 0, 128), st(s, DF)], [o])
-        act(R("new4s", a, b, 1, 0, 8), R(o[0], o[1], o[2], 1, 0, 8))
-        dma("s", R("yd", a, b, 1, 0, 8), R("new4s", a, b, 1, 0, 8))
+    phase(None, "z")
+    depart(st(None, DF))
+    o = PS("m1", 0)[0]
+    g = [(R(o, e, 512, 16, 0, 8), R("ident", e, 128, 16), st(None, DF), True, True) for e in range(16)]
+    add("t", "mm", g, [R("ident", 0, 128), st(None, DF)], [R(o, 0, 512)])
+    act(R("new4s", 0, 512, 1, 0, 8), R(o, 0, 512, 1, 0, 8))
+    dma("s", R("yd", 0, 512, 1, 0, 8), R("new4s", 0, 512, 1, 0, 8))
     return ops
 
 
@@ -771,7 +775,7 @@ def squeeze(ops, P, end, rounds):
     return best[0], sorted(range(n), key=lambda i: best[1][i])
 
 
-def swaps(ops, P, seq, turns):
+def swaps(ops, P, seq, turns, width, x):
     cs, pred = lags(ops, P)
     n = len(ops)
     hold, lat = [c[0] for c in cs], [c[1] for c in cs]
@@ -780,14 +784,17 @@ def swaps(ops, P, seq, turns):
         for d, l in pred[j]:
             succ[d].append((j, l))
     direct = [set(d for d, _ in p) for p in pred]
-    mp, mn, last, seq = [-1] * n, [-1] * n, {}, list(seq)
-    for i in seq:
-        e = ops[i]["e"]
-        if e in last and e is not None:
-            mp[i], mn[last[e]] = last[e], i
-        last[e] = i
-    pos = {i: k for k, i in enumerate(seq)}
+    mp, mn, seq = [-1] * n, [-1] * n, list(seq)
     head, tail = [0.0] * n, [0.0] * n
+
+    def link():
+        last = {}
+        for i in seq:
+            e = ops[i]["e"]
+            mp[i], mn[i] = -1, -1
+            if e in last and e is not None:
+                mp[i], mn[last[e]] = last[e], i
+            last[e] = i
 
     def early(i, t):
         for d, l in pred[i]:
@@ -801,58 +808,72 @@ def swaps(ops, P, seq, turns):
                 t = tail[d] + l
         return t
 
-    def mend(a, b):
-        for i in seq[a:]:
+    def mend(a, b, lo, hi):
+        for i in seq[a:hi]:
             head[i] = early(i, head[mp[i]] + hold[mp[i]] if mp[i] >= 0 else 0.0)
-        for i in seq[b::-1]:
+        for i in reversed(seq[lo:b + 1]):
             tail[i] = late(i, max(lat[i], tail[mn[i]] + hold[i]) if mn[i] >= 0 else lat[i])
-        return max(head[i] + lat[i] for i in range(n))
+        return max(head[i] + tail[i] for i in seq[lo:hi])
 
-    now = mend(0, n - 1)
-    best, barred, x = (now, list(seq), list(head)), {}, 1
-    for turn in range(turns):
-        cand = []
-        for v in range(n):
-            u = mp[v]
-            if head[v] + tail[v] > now - 1e-6 and u >= 0 and head[u] + hold[u] > head[v] - 1e-6 and u not in direct[v]:
-                hv = early(v, head[mp[u]] + hold[mp[u]] if mp[u] >= 0 else 0.0)
-                tu = late(u, max(lat[u], tail[mn[v]] + hold[u]) if mn[v] >= 0 else lat[u])
-                est = max(hv + late(v, max(lat[v], tu + hold[v])), early(u, hv + hold[v]) + tu)
-                x = (x * 1103515245 + 12345) % 2147483648
-                if barred.get((v, u), 0) <= turn or est < best[0] - 1e-6:
-                    cand.append((est + 30.0 * x / 2147483648, u, v))
-        if not cand:
-            barred.clear()
-            continue
-        _, u, v = min(cand)
-        a, b = mp[u], mn[v]
-        if a >= 0:
-            mn[a] = v
-        if b >= 0:
-            mp[b] = u
-        mp[v], mn[v], mp[u], mn[u] = a, u, v, b
-        barred[(u, v)] = turn + 8 + (x >> 8) % 13
-        pu, pv = pos[u], pos[v]
-        behind, lo, hi = {u}, [], [u]
-        for i in seq[pu + 1:pv + 1]:
-            if i != v and (direct[i] & behind or mp[i] in behind):
-                behind.add(i)
-                hi.append(i)
-            else:
-                lo.append(i)
-        seq[pu:pv + 1] = lo + hi
-        for k in range(pu, pv + 1):
-            pos[seq[k]] = k
-        now = mend(pu, pv)
-        if now < best[0] - 1e-6:
-            best = (now, list(seq), list(head))
-    return best[1], [best[2][i] + lat[i] for i in range(n)]
+    for lo in list(range(0, n, width // 2)) + list(range(width // 4, n, width // 2)):
+        link()
+        mend(0, n - 1, 0, n)
+        seq.sort(key=lambda i: head[i])
+        hi = min(lo + width, n)
+        pos = {seq[k]: k for k in range(lo, hi)}
+        now = max(head[i] + tail[i] for i in seq[lo:hi])
+        best, barred = (now, seq[lo:hi]), {}
+        for turn in range(turns):
+            cand = []
+            for v in seq[lo:hi]:
+                u = mp[v]
+                if head[v] + tail[v] > now - 1e-6 and u in pos and head[u] + hold[u] > head[v] - 1e-6 and u not in direct[v]:
+                    hv = early(v, head[mp[u]] + hold[mp[u]] if mp[u] >= 0 else 0.0)
+                    tu = late(u, max(lat[u], tail[mn[v]] + hold[u]) if mn[v] >= 0 else lat[u])
+                    est = max(hv + late(v, max(lat[v], tu + hold[v])), early(u, hv + hold[v]) + tu)
+                    x = (x * 1103515245 + 12345) % 2147483648
+                    if barred.get((v, u), 0) <= turn or est < best[0] - 1e-6:
+                        cand.append((est + 30.0 * x / 2147483648, u, v))
+            if not cand:
+                if not barred:
+                    break
+                barred.clear()
+                continue
+            _, u, v = min(cand)
+            a, b = mp[u], mn[v]
+            if a >= 0:
+                mn[a] = v
+            if b >= 0:
+                mp[b] = u
+            mp[v], mn[v], mp[u], mn[u] = a, u, v, b
+            barred[(u, v)] = turn + 8 + (x >> 8) % 13
+            pu, pv = pos[u], pos[v]
+            behind, ahead, after = {u}, [], [u]
+            for i in seq[pu + 1:pv + 1]:
+                if i != v and (direct[i] & behind or mp[i] in behind):
+                    behind.add(i)
+                    after.append(i)
+                else:
+                    ahead.append(i)
+            seq[pu:pv + 1] = ahead + after
+            for k in range(pu, pv + 1):
+                pos[seq[k]] = k
+            now = mend(pu, pv, lo, hi)
+            if now < best[0] - 1e-6:
+                best = (now, seq[lo:hi])
+        seq[lo:hi] = best[1]
+    link()
+    mend(0, n - 1, 0, n)
+    return seq, [head[i] + lat[i] for i in range(n)]
 
 
 def plan(O, U):
     ops = build(O)
-    tries = [squeeze(ops, PAR, order(ops, PAR, dict(U, lead=lead, look=look))[1], U["rounds"]) for lead in U["leads"] for look in U["looks"]]
-    seq, end = swaps(ops, PAR, min(tries)[1], U["turns"])
+    seq = min(squeeze(ops, PAR, order(ops, PAR, dict(U, lead=lead))[1], 6) for lead in U["leads"])[1]
+    for k, width in enumerate(U["widths"]):
+        seq, end = swaps(ops, PAR, seq, U["turns"], width, k + 1)
+        seq = squeeze(ops, PAR, end, 2)[1]
+    seq, end = swaps(ops, PAR, seq, 0, len(ops), 1)
     known = {e: 0 for e in "vstgy"}
     K, waits, raised, before, pre = {}, {}, set(), {}, {e: 0 for e in "vstgy"}
     for i in seq:
@@ -924,7 +945,7 @@ def relay_program(g, core, T, topo, src, down, far, k):
              ("e", k + 4, half, down, "ae1", "re1"), ("b", k, half, down, "ab%d" % (k // 2), "rb0")]
     if k == 1:
         steps.append(("f", 1, rest, far, "ab4", "rf"))
-    steps += [("n", k + 4 * s, half, down, "an%d" % (k // 2 + 2 * s), "rn%d" % s) for s in range(NST)]
+    steps += [("n", k + NREL * s, len(on) // NREL, down, "an%d" % (k // 2 + 2 * s), "rn%d" % s) for s in range(NST)]
     total = 0
     for kind, j, n, dst, sem, got in steps:
         rid, pid = topo.addr(dst, core)
@@ -983,8 +1004,11 @@ def rank_program(g, core, T, topo):
                    tr(rel[1], piece(T, "f", 1, False), piece(T, "f", 1, True), "rf", only_on)]
         elif what == "far":
             ts_ = [tr(far, T.newb[:], T.new4[:], "af", off)]
+        elif what[0] == "m":
+            s = int(what[-1])
+            ts_ = [tr(rel[k], piece(T, "n", NREL * s + k, False), piece(T, "n", NREL * s + k, True), "rn%d" % s, on[k::NREL]) for k in range(NREL)]
         else:
-            kind, h = {"b": "b", "e": "e", "m": "n"}[what[0]], int(what[-1])
+            kind, h = what[0], int(what[-1])
             ts_ = [tr(rel[(2 * h + j) % NREL], piece(T, kind, 2 * h + j, False), piece(T, kind, 2 * h + j, True), "r%s%d" % (kind, h // 2), on[j::2])
                    for j in range(2)]
         g.remote_dma_fused(ts_, local_sem=T.sem.sent)

@@ -3,20 +3,24 @@ from concourse.bass import DstId, RemoteDMATransfer
 from concourse.mybir import AluOpType, ActivationFunctionType
 
 OPT = dict(nw=(176, 176, 160),
-           fuse_s=(1, 1, 1, 1),
+           fuse_s=(15, 15),
            fuse_n=(1, 1),
            first=0,
            pe_copy=(0, 1),
-           pe_ds=(0, 0),
+           pe_ds=(2, 2),
+           pe_ss=(0, 0),
+           one_act=0, keep=0, on_g=("xi", "xr", "kf", "x0", "x3"),
            pe_dt=(0, 0),
            pe_h=((0, 0), (0, 0)),
            split=("mul", "yes", "sub", "rr"), rsplit=("yes", "mul", "rr", "sub", "ds"), wt4_v=0)
 NREL = 4
 TUNE = dict(lead=600.0, look=0.0, noise=0.0, seed=1, role={}, leads=(600.0, 1400.0, 2000.0), widths=(120, 80, 160, 100), turns=300)
 PAR = dict(fix=0.0, fixs=0.0, fuse=0.0, cyc=0.95, g=1.56, wake=200.0, same=180.0, pe=0.5, dma=2000.0, bw=160.0, call=900.0, leg=2500.0, link=45.0)
-BIG = 1.0e6
-ALPHA = 4096.0
+BIG = 2.0 ** 23
+ALPHA = 65536.0
 NX = 2032
+M1 = 2.0 ** 22
+EPS = 15.0 / 512
 
 
 def layout(O):
@@ -37,8 +41,10 @@ def layout(O):
         "misc4": ("sbuf", [128, 33], "float32"), "co4": ("sbuf", [128, 4], "float32"),
         "newb": ("sbuf", [128, 1024], "float32"), "new1": ("sbuf", [128, 1024], "float32"),
         "new4": ("sbuf", [128, 1024], "float32"), "new4s": ("sbuf", [128, 1024], "float32"),
-        "st": ("sbuf", [128, 6 * 32], "float32"), "di": ("sbuf", [128, 4 * 32], "int32"),
-        "ci": ("sbuf", [128, 32], "int32"), "cf": ("sbuf", [128, 128], "float32"),
+        "st": ("sbuf", [128, 8 * 32], "float32"), "di": ("sbuf", [128, 4 * 32], "int32"),
+        "ci": ("sbuf", [128, 32], "int32"), "cf": ("sbuf", [128, 160], "float32"),
+        "gi": ("sbuf", [128, 256], "int32"), "eb": ("sbuf", [128, 256], "bfloat16"), "mc": ("sbuf", [128, 512], "bfloat16"),
+        "oneb": ("sbuf", [128, max(nws)], "bfloat16"),
         "cs": ("sbuf", [128, 28 * 16], "float32"), "cr": ("sbuf", [128, 19 * 16], "float32"), "tp": ("sbuf", [128, 26 * 16], "float32"),
     }
     qh = max(nws)
@@ -50,7 +56,7 @@ def layout(O):
             S["%s%d" % (n, s)] = ("sbuf", [128, 2 * nw], "float32")
         S["q%d" % s] = ("sbuf", [128, 8 * qh], "float32")
         S["yes%d" % s] = ("sbuf", [128, nw], "bfloat16")
-        S["cug%d" % s] = ("sbuf", [128, nw], "bfloat16")
+        S["yez%d" % s] = ("sbuf", [128, 2 * nw], "bfloat16")
         S["tb%d" % s] = ("sbuf", [128, nw], "bfloat16")
         S["hb%d" % s] = ("sbuf", [128, 2 * nw], "bfloat16")
         S["so%d" % s] = ("sbuf", [128, 26 * nc], "float32")
@@ -60,16 +66,9 @@ def layout(O):
     P = {}
     for s, nw in enumerate(nws):
         nc = nw // 16
-        if len(nws) == 2:
-            rows = [("t1", "s1"), ("ht", "hs"), ("m0", "m1"), ("ps", "p1", "p2", "p3")]
-            if O["pe_ds"][0] or O["pe_ds"][1]:
-                rows = [("t1", "m0"), ("ht", "hs"), ("m1", "s1"), ("ps", "p1", "p2", "p3")]
-            banks = [4 * s + k for k in range(4)]
-            base = [0, 0, 0, 0]
-        else:
-            rows = [("t1", "s1", "ps", "p1"), ("ht", "hs", "p2", "p3"), ("m0",), ("m1",)]
-            banks = [2 * s, 2 * s + 1, 6, 7]
-            base = [0, 0, sum(nws[:s]), sum(nws[:s])]
+        rows = [("t1", "ht", "ps", "p3"), ("hs", "s1", "p1", "p2"), ("m0",), ("m1",)]
+        banks = [2 * s, 2 * s + 1, 6, 7]
+        base = [0, 0, sum(nws[:s]), sum(nws[:s])]
         for names, b, a in zip(rows, banks, base):
             for n in names:
                 P[(n, s)] = ("bank%d" % b, a)
@@ -137,7 +136,7 @@ def cost(op, P):
     if k == "mm":
         t = sum(P["pe"] * max(min(64, _n(m[1])), _n(m[2])) * (1 if _two(m[1]) else 4) for m in a)
         return t, t + 60
-    if k in ("iota", "sel"):
+    if k in ("iota", "sel", "gcp"):
         t = 150 + 2 * c * _n(a[0])
         return t, t
     if k == "dma":
@@ -214,8 +213,8 @@ def build(O):
     def act(o, x, scale=None, bias=None):
         return add("s", "act", (o, x, scale, bias), refs(x, scale, bias), [o])
 
-    def scan(o, x, y):
-        return add("v", "scan", (o, x, y, "subtract", "min"), [x, y], [o])
+    def scan(o, x, y, first=0.0):
+        return add("v", "scan", (o, x, y, "subtract", "min", first), [x, y], [o])
 
     def iota(o, pat, base, cm):
         return add("g", "iota", (o, pat, base, cm), [], [o])
@@ -229,18 +228,21 @@ def build(O):
         return i
 
     def arrive(sem, n, wr, mirror, legs, nbytes, src):
-        i = add(None, "arr", (sem, n, legs, nbytes), [], wr, src=src)
+        i = add(None, "arr", (sem, n, legs, nbytes, wr), [], wr, src=src)
         ops[i]["sdeps"] += list(mirror)
         return i
 
     def halves(r, on):
         return [(r[0], r[1] + e, r[2], 2) + r[4:] for e in (0, 1)] if on else [r]
 
-    def count(s, o, src, on):
-        nw = NWS[s]
+    def count(o, src, on):
+        n, a, b = src[:3]
         for es in ([range(0, 16, 2), range(1, 16, 2)] if on else [range(16)]):
-            g = [(o, R("mm", 128 * e, 128 * e + 128), R(src, e, nw, 16), e == 0, e == 15) for e in es]
-            add("t", "mm", g, [R("mm", 0, 2048), R(src, es[0], nw, es.step)], [o], goes_on=es[0] == 1)
+            g = [(o, R("mm", 128 * e, 128 * e + 128), R(n, a + e, b, 16), e == 0, e == 15) for e in es]
+            add("t", "mm", g, [R("mm", 0, 2048), R(n, a + es[0], b, es.step)], [o], goes_on=es[0] == 1)
+
+    def to_list(name, o, x):
+        return add("g", "gcp", (o, x), [x], [o]) if name in O["on_g"] else cp(o, x)
 
     ms(R("misc", 0, 4), 0.0)
     d0 = dma("y", R("cui", 0, 128), R("cu", 0, 2048, 1, 0, 8))
@@ -285,12 +287,14 @@ def build(O):
     iota(R("cf", 32, 64), [[0, 16], [1024, 2]], 0, 0)
     iota(R("cf", 64, 96), [[-128, 16], [0, 2]], 0, 0)
     iota(R("cf", 96, 112), [[16, 16]], 0, 0)
+    iota(R("cf", 128, 160), [[-1024, 16], [0, 2]], 0, 0)
     ts(R("ci", 16, 24), R("ci", 0, 8), 4, "arith_shift_right")
     ts(R("cf", 0, 8), R("ci", 16, 24), 0.0, "is_equal", -ALPHA, "mult")
     ts(R("ci", 9, 10), R("ci", 8, 9), 15, "bitwise_and")
     ts(R("cf", 8, 9), R("ci", 9, 10), 64.0, "mult")
     cp(R("cf", 9, 10), R("ci", 9, 10))
-    ms(R("cf", 10, 11), 0.125)
+    for k, val in enumerate((1.0, -8.5 * ALPHA, 2.0 if "x3" in O["on_g"] else 6.0, 4.0)):
+        ms(R("cf", 10 + k, 11 + k), val)
     ts(R("cf", 96, 112), R("cf", 96, 112), R("cf", 9, 10), "add")
     J = R("cf", 96, 96 + NM)
     ms(R("mm", 0, 2048), 0.0)
@@ -302,9 +306,9 @@ def build(O):
     for i in later:
         ops[i]["late"] = s_s
     ms(R("cu0", 0, 2048), 0.0)
-    ts(R("cub0", 0, 128), R("misc", 4, 132), 128.0 / ALPHA, "mult")
+    ts(R("cub0", 0, 128), R("misc", 4, 132), 1024.0 / ALPHA, "mult")
     dma("y", R("cu0", 0, 2048, 1, 0, 128, 16), R("cub0", 0, 128))
-    ts(R("cub1", 0, 128), R("misc1", 4, 132), 128.0 / ALPHA, "mult")
+    ts(R("cub1", 0, 128), R("misc1", 4, 132), 1024.0 / ALPHA, "mult")
     dma("y", R("cu1", 0, 2048, 1, 0, 128, 16), R("cub1", 0, 128))
     ms(R("ones", 0, 128), 1.0)
     i_id = add("g", "sel", (R("ident", 0, 128), R("ones", 0, 128)), [R("ones", 0, 128)], [R("ident", 0, 128)])
@@ -332,6 +336,8 @@ def build(O):
         for wt, co, off in (("wt0", "misc", 0), ("wt4", "co4", 0), ("wt1", "misc1", NX)):
             if wt == "wt4" and O["wt4_v"]:
                 ts(R(wt, a, b), R("xs", a, b), R(co, 1, 2), "mult", R(co, 0, 1), "add")
+            elif O["one_act"]:
+                act(R(wt, off + a, off + b), R("xs", off + a, off + b), scale=R(co, 1, 2), bias=R(co, 0, 1))
             else:
                 act(R(wt, off + a, off + b), R("xs", off + a, off + b), scale=R(co, 1, 2))
                 act(R(wt, off + a, off + b), R(wt, off + a, off + b), bias=R(co, 0, 1))
@@ -341,27 +347,37 @@ def build(O):
 
     EDGE = 8.5 * ALPHA
     ms(R("cs", 0, 28 * NM), BIG)
-    for e, val in ((0, -EDGE), (3, 0.0), (4, 126.0)):
+    for e, val in ((0, -EDGE), (3, 0.0), (4, 8 * 126.0)):
         ms(lane("cs", 0, 7, e, 4 * NM), val)
     for j in range(4):
         for e in (1, 2):
-            ms(lane("cs", 7 * NM * j, 7, e), float(8 >> j))
+            ms(lane("cs", 7 * NM * j, 7, e), float(64 >> j))
+    iota(R("gi", 0, 128), [[-16, 8], [0, 16]], 0, 1)
+    ts(R("gi", 128, 256), R("gi", 0, 128), 4, "arith_shift_right")
+    for k in (0, 1):
+        ts(R("eb", 128 * k, 128 * k + 128), R("gi", 128, 256), 0.0, "is_equal", EPS / (1 << k), "mult")
+    ms(R("mc", 0, 512, 1, 0, 64), 0.0)
+    for k, (big, half) in enumerate(((M1, 0.0), (-M1, 0.25), (M1 / 2, -0.25) if O["keep"] else (-M1 / 2, 0.0), (-M1 / 2, 0.125))):
+        ms(R("mc", 128 * k, 128 * k + 128, 1, 0, 1), big)
+        if half:
+            ms(R("mc", 128 * k, 128 * k + 128, 1, 32, 33), half)
+    ms(R("oneb", 0, QH), 1.0)
     RA, RW = (0, 6 * NM, 12 * NM), (6, 6, 7)
     ms(R("cr", 0, 19 * NM), BIG)
     ms(R("tp", 0, 26 * NM), 0.0)
-    ms(lane("tp", 0, 7, 0), BIG)
     for v in range(3):
-        ms(lane("cr", RA[v], RW[v], 0), -EDGE)
-        ms(lane("cr", RA[v], RW[v], 1), 0.0)
-        ms(lane("cr", RA[v], RW[v], 3), 0.5 / (1 << v))
-        for name, a, e in (("cr", RA[v], 2), ("tp", 7 * NM + RA[v], 3)):
-            ts(lane(name, a, RW[v], e), J, 2.0 * QH * (v + 1) + (0.125 if v else 0.0), "add")
-        if v != 1:
-            ms(lane("tp", 7 * NM + RA[v], RW[v], 0), BIG)
-    cp(lane("tp", 7 * NM, 6, 2), J)
-    ms(lane("tp", 7 * NM, 6, 4), 0.75)
+        z = 1 if v < 2 else 0
+        if z:
+            ms(lane("cr", RA[v], RW[v], 0), -EDGE)
+        ms(lane("cr", RA[v], RW[v], z), 0.0)
+        ms(lane("cr", RA[v], RW[v], z + 2), float(4 >> v))
+        for name, a, e in (("cr", RA[v], z + 1), ("tp", 7 * NM + RA[v], z + 2)):
+            ts(lane(name, a, RW[v], e), J, 2.0 * QH * (v + 1) - (0.0 if v else 1.0), "add")
+    for a, w in ((0, 7), (7 * NM, 6)):
+        ms(lane("tp", a, w, 0), BIG)
+    ts(lane("tp", 7 * NM, 6, 2), J, 1.0, "subtract")
 
-    NL, V1, DX, VX, T1, DF = range(6)
+    NL, V1, DX, VX, T1, DF, N8, DH = range(8)
     OCOL, OXI, OCOL1, OKQ, OXR, OC0, OX0, OKF = range(8)
     SW = {"ps": (0, 7), "p1": (7, 6), "p2": (13, 6), "p3": (19, 7)}
 
@@ -407,7 +423,7 @@ def build(O):
     rnd = [0]
 
     def to_psum(s, h):
-        if h and O["pe_ds"][rnd[0]]:
+        if h and O["pe_ds"][rnd[0]] == 7 and O["fuse_s"][rnd[0]] | O["pe_ss"][rnd[0]] == 15:
             return
         if O["pe_copy"][h]:
             g = [(P1(s, h), R("ident", 0, 128), B("s1", s, h), True, True)]
@@ -415,12 +431,25 @@ def build(O):
         else:
             act(P1(s, h), B("s1", s, h))
 
-    def vote(s, tv, sv, w, b0, z, sp, pe_s=False, pe_t=False):
+    def fraction(s, steps):
+        o, nw = PS("ht", s), NWS[s]
+        for x in steps:
+            if isinstance(x, tuple):
+                k, y, on = x
+                for p, q in zip(halves(o, on), halves(y, on)):
+                    l = R("eb", 128 * k, 128 * k + 128)
+                    add("t", "mm", [(p, l, q, False, False)], [l, q], [p], goes_on=True)
+            else:
+                l, q = R("mc", 128 * x, 128 * x + 128, 1, 0, 33 if x else 1), R("oneb", 0, nw, 1, 0, 33 if x else 1)
+                add("t", "mm", [(o, l, q, x == 0, x % 2 == 1)], [l, q], [o], goes_on=x > 0)
+
+    def vote(s, tv, sv, w, b0, z, sp, pe_s=False, pe_t=False, yes="yes", hook=None):
         ds, m = B("ds", s), PS("ht" if pe_t else "m0", s)
+        hook = hook or {}
         if sv[0] == "ind":
             tt(ds, sv, B("s1", s, 1), "subtract")
         elif pe_s:
-            ds = P1(s, 1)
+            ds = PH(s, 1)
             pe_sum(ds, -1.0, B("s1", s, 1), 1.0, sv, "ds" in sp)
         else:
             for o, x, y in zip(*[halves(r, "ds" in sp) for r in (ds, sv, P1(s, 1))]):
@@ -433,11 +462,15 @@ def build(O):
         else:
             for o, x, y in zip(*[halves(r, "sub" in sp) for r in (m, tv, P1(s, 0))]):
                 tt(o, x, y, "subtract")
+        for f in hook.get("sub", ()):
+            f()
         for o, x in zip(*[halves(r, "mul" in sp) for r in (m, B("wg", s))]):
             tt(o, x, o, "mult")
-        for o, x, y in zip(*[halves(r, "yes" in sp) for r in (B("yes", s), m, B("rr", s))]):
+        for o, x, y in zip(*[halves(r, "yes" in sp) for r in (B(yes, s), m, B("rr", s))]):
             tt(o, x, y, "is_gt")
-        count(s, z, "yes%d" % s, "yes" in sp)
+        for f in hook.get("yes", ()):
+            f()
+        count(z, R("%s%d" % (yes, s), 0, 16 * _n(z)), "yes" in sp)
 
     def vote_turned(s, w, b0, z, sp):
         tt(B("ds", s), chosen(s, 1), B("sg", s), "subtract")
@@ -446,7 +479,7 @@ def build(O):
         tt(B("aa", s), w, B("dt", s), "mult")
         for o, x, y in zip(*[halves(r, "yes" in sp) for r in (B("yes", s), B("aa", s), PH(s, 0))]):
             tt(o, x, y, "is_lt")
-        count(s, z, "yes%d" % s, "yes" in sp)
+        count(z, B("yes", s), "yes" in sp)
 
     def levels(s, tab, a=0, b=2048):
         for h in (1, 0):
@@ -474,9 +507,9 @@ def build(O):
     def chosen(s, h):
         return IND(R("q%d" % s, QH * h, QH * (7 + h)), of(s, OKF))
 
-    def first_col(s, low, half):
-        tt(pin("p3", s, 6), pin("ps", s, 5), low, "subtract")
-        ts(of(s, OC0), pin("p3", s, 6), -0.5 if half else -1.0, "mult")
+    def first_col(s, cast, low, half):
+        tt(st(s, T1), low, cast, "subtract")
+        ts(of(s, OC0), st(s, T1), 0.0625 if half else 0.125, "mult")
 
     def hop(s, tab, wt, wend, co, nxt, even=None, turned=False):
         phase(s, "")
@@ -497,50 +530,75 @@ def build(O):
                     act(B("s1", s, h), chosen(s, h))
                     to_psum(s, h)
             else:
-                if not O["fuse_s"][j]:
-                    act(B("sg", s), sv)
-                    sv = B("sg", s)
-                vote(s, tg, sv, IND(win, of(s, ox)), b0, pin("ps", s, 1), O["split"], False, pe_t)
+                pe_s = O["pe_ss"][rnd[0]] >> j & 1
+                if pe_s or not O["fuse_s"][rnd[0]] >> j & 1:
+                    sg = B("hb" if pe_s and _two(ws_) else "sg", s)
+                    act(sg, sv)
+                    sv = sg
+                vote(s, tg, sv, IND(win, of(s, ox)), b0, pin("ps", s, 1), O["split"], O["pe_ss"][rnd[0]] >> j & 1, pe_t)
             scan(res("ps", s), PS("ps", s), R("cs", 7 * NM * j, 7 * NM * j + 7 * nc))
-            ts(of(s, OCOL), res("ps", s, 5), -0.5 if even and j < 3 else -1.0, "mult")
+            ts(of(s, OCOL), res("ps", s, 5), -0.0625 if even and j < 3 else -0.125, "mult")
             if j == 3:
-                ts(of(s, OCOL1), res("ps", s, 5), -1.0, "mult", 1.0, "add")
-                ts(of(s, OXI), res("ps", s, 6), 0.5, "add", 8.0, "mult")
+                ts(of(s, OCOL1), res("ps", s, 5), -0.125, "mult", 1.0, "add")
+            if j == 3 and "x3" not in O["on_g"]:
+                ts(of(s, OXI), res("ps", s, 6), 4.0, "add")
             else:
-                ts(of(s, OXI), res("ps", s, 6), 8.0, "mult")
+                to_list("v" if even else "xi", of(s, OXI), res("ps", s, 6))
             if j < 3 or nxt is not None:
                 act(pin("ps", s, 3), res("ps", s, 4), scale=-1.0)
-        act(pin("p3", s, 5), res("ps", s, 4), scale=-1.0 if nxt is None else -2.0)
-        for p in ("p1", "p2"):
-            act(pin(p, s, 5), res("ps", s, 6), scale=-1.0)
+            if j == 2 and "x3" in O["on_g"]:
+                act(pin("ps", s, 6), pin("ps", s, 6), bias=R("cf", 13, 14))
+        if nxt is not None:
+            act(pin("p3", s, 5), res("ps", s, 4))
+        act(pin("p1", s, 4), res("ps", s, 6), bias=R("cf", 12, 13))
         if nxt == "home":
-            act(pin("ps", s, 5), wrapped(64, s))
+            act(pin("ps", s, 5), wrapped(128, s))
         levels(s, tab)
         for h in (1, 0):
             tt(Qs(s, h, 1), PH(s, h), Qs(s, h, 0), "add")
-        for v, p in enumerate(("p1", "p2", "p3")):
-            if v:
-                at_depth(s, of(s, OKQ), [Qs(s, h, v + 1) for h in (0, 1)])
-            vote(s, Qs(s, 0, v + 1), Qs(s, 1, v + 1), IND(win, of(s, OXR if v else OXI)), b0, pin(p, s, 1), O["rsplit"], O["pe_ds"][rnd[0]])
-            scan(res(p, s), PS(p, s), R("cr", RA[v], RA[v] + RW[v] * nc))
-            if v < 2:
-                ts(of(s, OKQ), res(p, s, 4), 16.0, "mult")
-                ts(of(s, OXR), res(p, s, 5), -8.0, "mult")
-            if v == 0:
+        on, far = "yes" in O["rsplit"], nxt not in (None, "home")
+        if far:
+            act(B("yez", s, 1), IND(R(nxt, 0, 2048), of(s, OCOL)))
+
+        def pass_on(v):
+            if v == 1:
                 x, o = res("p1", s), PS("p2", s)
                 act(R(o[0], o[1], o[2] - 1, 2), R(x[0], x[1], x[2] - 1, 2), bias=R("cf", 10, 11))
-                if nxt not in (None, "home"):
-                    act(B("cug", s), IND(R(nxt, 0, 2048), of(s, OCOL)))
-                    count(s, pin("ps", s, 5), "cug%d" % s, False)
-                if nxt is not None:
-                    first_col(s, res("ps", s, 4), False)
-            elif v == 1:
+                if far:
+                    act(pin("ps", s, 5), pin("p2", s, 1))
+            else:
                 for e in (2, 4):
-                    act(pin("p3", s, e), res("p2", s, e))
-        ts(of(s, OKF), res("p3", s, 2), 0.125, "subtract")
+                    act(pin("p3", s, e - 1), res("p2", s, e))
+                if nxt is not None:
+                    act(pin("p3", s, 6), st(s, T1), bias=R("cf", 11, 12))
+
+        for v, p in enumerate(("p1", "p2", "p3")):
+            if v:
+                for h in (0, 1):
+                    tt(PS("m%d" % h, s), B("dd", s, h), PS("ht", s), "mult")
+                for h in (0, 1):
+                    tt(Qs(s, h, v + 1), PS("m%d" % h, s), Qs(s, h, 0), "add")
+            hook = {"sub": [], "yes": []}
+            z = pin(p, s, 1 if v < 2 else 0)
+            if far and v == 0:
+                z = lane(z[0], z[1], 6, 0, 2 * nc)
+            if v:
+                hook["sub"].append(lambda: pass_on(v))
+            if v < 2:
+                hook["sub"].append(lambda: fraction(s, ([2] if O["keep"] else [0, (0, B("yez", s), False), 2]) if v else [0]))
+                hook["yes"].append(lambda: fraction(s, [(1, B("yes", s), on), 3] if v else [(0, B("yez", s), on), 1]))
+            vote(s, Qs(s, 0, v + 1), Qs(s, 1, v + 1), IND(win, of(s, OXR if v else OXI)), b0, z, O["rsplit"], O["pe_ds"][rnd[0]] >> v & 1,
+                 yes="yes" if v else "yez", hook=hook)
+            scan(res(p, s), PS(p, s), R("cr", RA[v], RA[v] + RW[v] * nc), -EDGE if v == 2 else 0.0)
+            if v < 2:
+                to_list("xr", of(s, OXR), res(p, s, 4))
+            if v == 0 and nxt is not None:
+                first_col(s, pin("p2", s, 1) if far else wrapped(128, s), res("ps", s, 4), False)
+        to_list("kf", of(s, OKF), res("p3", s, 1))
         if nxt is not None:
-            ts(of(s, OX0), res("p3", s, 5), -8.0, "mult")
-            act(pin("ps", s, 6), res("p3", s, 6))
+            to_list("x0", of(s, OX0), res("p3", s, 5))
+            act(pin("ps", s, 6), res("p3", s, 6), scale=-1.0, bias=R("cf", 11, 12))
+            act(pin("p3", s, 4), res("p3", s, 4), scale=-1.0)
             if not O["first"]:
                 for h in (1, 0):
                     act(B("s1", s, h), chosen(s, h))
@@ -553,15 +611,12 @@ def build(O):
             old = R("own0", a, a + 4 * NWS[s] - 3, 4)
             df = B(("tg", "wg")[h], s)
             tt(df, chosen(s, h), old, "subtract")
-            act(PH(s, h), df, scale=0.25)
-            tt(R(out, 512 * h + I0[s], 512 * h + I0[s] + NWS[s]), PH(s, h), old, "add")
+            act(PS(("s1", "hs")[h], s), df, scale=0.25)
+            tt(R(out, 512 * h + I0[s], 512 * h + I0[s] + NWS[s]), PS(("s1", "hs")[h], s), old, "add")
 
-    def depart(out):
-        for s in range(NST):
-            act(st(s, T1), res("p3", s, 5), scale=-16.0)
-        tt(di(1), st(None, T1), di(0), "subtract")
-        ts(di(2), di(1), 1, "arith_shift_right")
-        tt(out, di(0), di(2), "add")
+    def depart(s):
+        tt(st(s, T1), st(s, DH), res("p3", s, 4), "subtract")
+        ts(di(0, s), st(s, T1), 0.25, "subtract")
 
     def spread(f, src, s, h, on):
         a = 2048 * h + 4 * I0[s]
@@ -574,19 +629,22 @@ def build(O):
         a, b = casts(s)
         if s == 0:
             tt(st(None, V1), st(None, NL), R("cf", 64, 96), "subtract")
-            tt(st(None, VX), st(None, dx), st(None, NL), "add")
-        act(pin("ps", s, 3), st(s, NL), scale=-1.0)
+            act(st(None, N8), st(None, NL), scale=8.0)
+            tt(st(None, VX), st(None, dx), st(None, N8), "add")
+        act(pin("ps", s, 3), st(s, NL), scale=-8.0)
+        act(pin("p3", s, 4), st(s, dx))
         ts(of(s, OCOL), st(s, V1), float(a), "subtract")
         if not half:
             ts(of(s, OCOL1), st(s, V1), a - 1.0, "subtract")
-        ts(of(s, OX0), st(s, VX), 8.0, "mult")
-        act(B("cug", s), IND(R("cu0", a, b), of(s, OCOL)))
-        count(s, pin("ps", s, 5), "cug%d" % s, False)
-        first_col(s, st(s, NL), half)
+        to_list("v" if half else "x0", of(s, OX0), st(s, VX))
+        act(B("yez", s, 1), IND(R("cu0", a, b), of(s, OCOL)))
+        count(pin("ps", s, 5), B("yez", s, 1), False)
+        first_col(s, pin("ps", s, 5), st(s, N8), half)
         tt(pin("ps", s, 6), pin("ps", s, 5), st(s, dx), "add")
 
     ts(di(0), R("cf", 32, 64), R("cf", 8, 9), "add")
     ts(st(None, NL), di(0), 0.0625, "mult")
+    ts(st(None, DH), di(0), 0.5, "mult")
     for s in range(NST):
         cur[0] = s
         nc = NWS[s] // 16
@@ -594,7 +652,7 @@ def build(O):
             act(PS(p, s), R("tp", a * NM, a * NM + w * nc))
         if NWS[s] < QH:
             ms(R("q%d" % s, NWS[s], 8 * QH), 0.0)
-        start(s, True, NL)
+        start(s, True, DH)
         act(P1(s, 0), R("own0", 4 * I0[s], 4 * (I0[s] + NWS[s]) - 3, 4))
         if O["pe_dt"][0]:
             act(B("s1", s, 0), R("own0", 4 * I0[s], 4 * (I0[s] + NWS[s]) - 3, 4))
@@ -625,14 +683,15 @@ def build(O):
             spread("f1", "new1", s, h, "v" if h and s == NST - 1 else "s")
             spread("f4", "new4s", s, h, "s")
     rnd[0] = 1
-    depart(di(0))
+    for s in range(NST):
+        depart(s)
+    ts(st(None, DH), di(0), 0.5, "mult")
     ts(di(1), di(0), 4, "arith_shift_right")
     cp(st(None, NL), di(1))
     ts(di(2), di(0), 15, "bitwise_and")
     ts(di(3), di(0), 1, "bitwise_and")
-    ts(st(None, T1), di(3), 2.0 * NX - 1, "mult")
-    tt(st(None, T1), st(None, T1), di(0), "add")
-    act(st(None, DX), st(None, T1), scale=0.0625)
+    ts(st(None, DF), di(3), NX - 0.5, "mult")
+    tt(st(None, DX), st(None, DF), st(None, DH), "add")
     for s in range(NST):
         cur[0] = s
         cp(of(s, OKQ), di(2, s))
@@ -650,13 +709,13 @@ def build(O):
         a, b = I0[s], I0[s] + NWS[s]
         for h, y in ((1, "ys"), (0, "yt")):
             dma("y", R(y, a, b), R("new1", 512 * h + a, 512 * h + b))
-    phase(None, "z")
-    depart(st(None, DF))
-    o = PS("m1", 0)[0]
-    g = [(R(o, e, 512, 16, 0, 8), R("ident", e, 128, 16), st(None, DF), True, True) for e in range(16)]
-    add("t", "mm", g, [R("ident", 0, 128), st(None, DF)], [R(o, 0, 512)])
-    act(R("new4s", 0, 512, 1, 0, 8), R(o, 0, 512, 1, 0, 8))
-    dma("s", R("yd", 0, 512, 1, 0, 8), R("new4s", 0, 512, 1, 0, 8))
+        depart(s)
+        cp(st(s, DF), di(0, s))
+        o, c, z = P1(s, 0)[:3]
+        g = [(R(o, c + e, z, 16, 0, 8), R("ident", e, 128, 16), st(s, DF), True, True) for e in range(16)]
+        add("t", "mm", g, [R("ident", 0, 128), st(s, DF)], [R(o, c, z)])
+        act(R("new4s", a, b, 1, 0, 8), R(o, c, z, 1, 0, 8))
+        dma("y", R("yd", a, b, 1, 0, 8), R("new4s", a, b, 1, 0, 8))
     return ops
 
 
@@ -1036,13 +1095,15 @@ def rank_program(g, core, T, topo):
             else:
                 ins = q.tensor_scalar(ap(a[0]), ap(a[1]), ap(a[2]), ap(a[3]), alu[a[4]], alu[a[5]])
         elif k == "scan":
-            ins = q.tensor_tensor_scan(ap(a[0]), ap(a[1]), ap(a[2]), 0.0, alu[a[3]], alu[a[4]])
+            ins = q.tensor_tensor_scan(ap(a[0]), ap(a[1]), ap(a[2]), a[5], alu[a[3]], alu[a[4]])
         elif k == "cp":
             ins = q.tensor_copy(ap(a[0]), ap(a[1]))
         elif k == "ms":
             ins = q.memset(ap(a[0]), a[1])
         elif k == "act":
-            if a[3] is not None:
+            if a[3] is not None and a[2] is not None:
+                ins = q.activation(ap(a[0]), ap(a[1]), F.Identity, bias=ap(a[3]), scale=ap(a[2]))
+            elif a[3] is not None:
                 ins = q.activation(ap(a[0]), ap(a[1]), F.Identity, bias=ap(a[3]))
             elif a[2] is not None:
                 ins = q.activation(ap(a[0]), ap(a[1]), F.Copy, scale=ap(a[2]))
@@ -1056,6 +1117,8 @@ def rank_program(g, core, T, topo):
                 ins = q.iota(ap(a[0]), a[1], a[2], a[3])
             else:
                 ins = q.iota(ap(a[0]), a[1], a[2], a[3], allow_small_or_imprecise_dtypes=True)
+        elif k == "gcp":
+            ins = q.affine_select(ap(a[0]), ap(a[1]), [[0, _n(a[0])]], A.is_equal, 0.0, 0, 0)
         elif k == "sel":
             ins = q.affine_select(ap(a[0]), ap(a[1]), [[-1, 128]], A.is_equal, 0.0, 0, 1)
         else:

@@ -4,17 +4,22 @@ from concourse.mybir import AluOpType, ActivationFunctionType
 
 OPT = dict(nw=(176, 176, 160),
            fuse_s=(15, 15),
-           fuse_n=(1, 1),
-           first=0,
            pe_copy=(0, 1),
+           fin_v=(0, 0),
            pe_ds=(2, 2),
-           pe_ss=(0, 0),
-           one_act=0, keep=0, on_g=("xi", "xr", "kf", "x0", "x3"),
-           pe_dt=(0, 0),
-           pe_h=((0, 0), (0, 0)),
-           split=("mul", "yes", "sub", "rr"), rsplit=("yes", "mul", "rr", "sub", "ds"), wt4_v=0)
+           on_g=("xi", "xr", "kf", "x0", "x3", "c0", "c1"),
+           pe_dt=(15, 0, 0, 0, 0, 0),
+           split=("mul", "yes", "sub"), rsplit=("yes", "mul", "sub", "ds"),
+           tab_n=8, tab_at=(None, 0, 1),
+           fin_pe=(1, 1),
+           off=0, po=0, apart=(0, 0, 0, 0, 0, 0),
+           far_g=1)
+EVEN = ((0, 512), (512, 1024), (1024, 1536), (1536, 1792), (1792, 2048))
 NREL = 4
-TUNE = dict(lead=600.0, look=0.0, noise=0.0, seed=1, role={}, leads=(600.0, 1400.0, 2000.0), widths=(120, 80, 160, 100), turns=300)
+TUNE = dict(lead=600.0, look=0.0, noise=0.0, seed=1, role={}, leads=(600.0, 1400.0, 2000.0), widths=(120, 80, 160), turns=200,
+            more=((1.0, 1.56, 200.0, 0.42, 45.0), (1.0, 1.2, 140.0, 0.42, 50.0), (1.15, 1.3, 250.0, 0.45, 45.0), (1.25, 1.56, 180.0, 0.42, 45.0),
+                  (1.05, 1.3, 165.0, 0.42, 50.0), (1.4, 1.9, 220.0, 0.45, 45.0), (1.1, 1.9, 160.0, 0.45, 45.0)),
+            passes=112, turns2=20, widths2=(100, 60, 140, 80, 120))
 PAR = dict(fix=0.0, fixs=0.0, fuse=0.0, cyc=0.95, g=1.56, wake=200.0, same=180.0, pe=0.5, dma=2000.0, bw=160.0, call=900.0, leg=2500.0, link=45.0)
 BIG = 2.0 ** 23
 ALPHA = 65536.0
@@ -27,21 +32,22 @@ def layout(O):
     nws = O["nw"]
     S = {
         "own0": ("sbuf", [128, 4096], "bfloat16"), "w1b": ("sbuf", [128, 4096], "bfloat16"),
-        "w4b": ("sbuf", [128, 4096], "bfloat16"), "stage4": ("sbuf", [128, 4096], "bfloat16"),
+        "w4b": ("sbuf", [128, 4096], "bfloat16"),
         "we0": ("sbuf", [128, 2048], "bfloat16"), "we1": ("sbuf", [128, 2048], "bfloat16"),
+        "wo0": ("sbuf", [128, 2048], "bfloat16"), "wo1": ("sbuf", [128, 2048], "bfloat16"),
         "f0": ("sbuf", [128, 4096], "float32"), "f1": ("sbuf", [128, 4096], "float32"), "f4": ("sbuf", [128, 4096], "float32"),
         "xs": ("sbuf", [128, 2 * NX], "float32"),
         "wt1": ("sbuf", [128, 2 * NX], "float32"), "wt4": ("sbuf", [128, NX], "float32"), "wt0": ("sbuf", [128, NX], "float32"),
-        "cu0": ("sbuf", [128, 2048], "bfloat16"), "cu1": ("sbuf", [128, 2048], "bfloat16"),
+        "cu0": ("sbuf", [128, 2048], "bfloat16"),
         "cui": ("sbuf", [128, 128], "int32"), "cub0": ("sbuf", [128, 128], "bfloat16"), "cub1": ("sbuf", [128, 128], "bfloat16"),
         "mm": ("sbuf", [128, 2048], "bfloat16"),
-        "ones": ("sbuf", [128, 128], "float32"), "ident": ("sbuf", [128, 512], "float32"),
+        "ones": ("sbuf", [128, 128], "float32"), "ident": ("sbuf", [128, 256], "float32"),
         "identb": ("sbuf", [128, 256], "bfloat16"),
         "misc": ("sbuf", [128, 132], "float32"), "misc1": ("sbuf", [128, 132], "float32"),
         "misc4": ("sbuf", [128, 33], "float32"), "co4": ("sbuf", [128, 4], "float32"),
         "newb": ("sbuf", [128, 1024], "float32"), "new1": ("sbuf", [128, 1024], "float32"),
         "new4": ("sbuf", [128, 1024], "float32"), "new4s": ("sbuf", [128, 1024], "float32"),
-        "st": ("sbuf", [128, 8 * 32], "float32"), "di": ("sbuf", [128, 4 * 32], "int32"),
+        "st": ("sbuf", [128, 11 * 32], "float32"), "di": ("sbuf", [128, 4 * 32], "int32"),
         "ci": ("sbuf", [128, 32], "int32"), "cf": ("sbuf", [128, 160], "float32"),
         "gi": ("sbuf", [128, 256], "int32"), "eb": ("sbuf", [128, 256], "bfloat16"), "mc": ("sbuf", [128, 512], "bfloat16"),
         "oneb": ("sbuf", [128, max(nws)], "bfloat16"),
@@ -50,7 +56,7 @@ def layout(O):
     qh = max(nws)
     for s, nw in enumerate(nws):
         nc = nw // 16
-        for n in ("tg", "sg", "wg", "rr", "ds", "kk", "dt", "aa"):
+        for n in ("tg", "sg", "wg", "rr", "ds"):
             S["%s%d" % (n, s)] = ("sbuf", [128, nw], "float32")
         for n in ("s1", "dd"):
             S["%s%d" % (n, s)] = ("sbuf", [128, 2 * nw], "float32")
@@ -58,8 +64,7 @@ def layout(O):
         S["yes%d" % s] = ("sbuf", [128, nw], "bfloat16")
         S["yez%d" % s] = ("sbuf", [128, 2 * nw], "bfloat16")
         S["tb%d" % s] = ("sbuf", [128, nw], "bfloat16")
-        S["hb%d" % s] = ("sbuf", [128, 2 * nw], "bfloat16")
-        S["so%d" % s] = ("sbuf", [128, 26 * nc], "float32")
+        S["so%d" % s] = ("sbuf", [128, 25 * nc], "float32")
         S["of%d" % s] = ("sbuf", [128, 8 * 16], "uint16")
     for b in range(8):
         S["bank%d" % b] = ("psum", [128, 512], "float32")
@@ -72,7 +77,7 @@ def layout(O):
         for names, b, a in zip(rows, banks, base):
             for n in names:
                 P[(n, s)] = ("bank%d" % b, a)
-                a += {"ps": 7 * nc, "p1": 6 * nc, "p2": 6 * nc, "p3": 7 * nc}.get(n, nw)
+                a += {"ps": 6 * nc, "p1": 6 * nc, "p2": 6 * nc, "p3": 7 * nc}.get(n, nw)
     return S, P
 
 
@@ -233,7 +238,7 @@ def build(O):
         return i
 
     def halves(r, on):
-        return [(r[0], r[1] + e, r[2], 2) + r[4:] for e in (0, 1)] if on else [r]
+        return [(r[0], r[1] + e * r[3], r[2], 2 * r[3]) + r[4:] for e in (0, 1)] if on else [r]
 
     def count(o, src, on):
         n, a, b = src[:3]
@@ -244,41 +249,52 @@ def build(O):
     def to_list(name, o, x):
         return add("g", "gcp", (o, x), [x], [o]) if name in O["on_g"] else cp(o, x)
 
-    ms(R("misc", 0, 4), 0.0)
     d0 = dma("y", R("cui", 0, 128), R("cu", 0, 2048, 1, 0, 8))
-    dma("s", R("misc", 0, 3), R("co", 0, 3))
-    ops[d0]["first"] = 5
-    for k in range(4):
-        d1 = dma("y", R("own0", 1024 * k, 1024 * k + 1024), R(("te", "sa")[k // 2], 1024 * (k % 2), 1024 * (k % 2) + 1024), ahead=k << 18)
-        ops[d1]["first"] = 4 - k
+    d1 = dma("s", R("misc", 0, 3), R("co", 0, 3))
+    ops[d0]["first"] = ops[d1]["first"] = 5
+    add("v", "ms", (R("misc", 3, 4), 0.0), [], [R("misc", 3, 4)], [d1], first=1)
+    load = []
+    for k, (a, b) in enumerate(EVEN):
+        load.append(dma("y", R("own0", 2 * a, 2 * b), R(("te", "sa")[a // 1024], 2 * a % 2048, (2 * b - 1) % 2048 + 1),
+                        load[(0, 0, 0, 1, 1)[k]:][:1] if k > 1 else (), ahead=(0, 4, 0, 1, 3)[k] << 16))
+        ops[load[k]]["first"], ops[load[k]]["late"], d0 = 4, d0, load[k]
     ops[cp(R("misc", 4, 132), R("cui", 0, 128))]["first"] = 1
     s_m = send("misc", [R("misc", 0, 132)], 1 << 16)
     s_e = []
-    for k in range(4):
-        ops[act(R("we0", 512 * k, 512 * k + 192), R("own0", 1024 * k, 1024 * k + 384, 2))]["first"] = 1
-        ops[cp(R("we0", 512 * k + 192, 512 * k + 512), R("own0", 1024 * k + 384, 1024 * k + 1024, 2))]["first"] = 1
-        s_e.append(send("even%d" % k, [R("we0", 512 * k, 512 * k + 512)], 1 << 17))
+    for k, (a, b) in enumerate(EVEN):
+        m = a + (b - a) * 3 // 8
+        pick = {"s": act(R("we0", a, m), R("own0", 2 * a, 2 * m, 2)), "v": cp(R("we0", m, b), R("own0", 2 * m, 2 * b, 2))}
+        for i in pick.values():
+            ops[i]["first"] = 1
+        s_e.append(send("even%d" % k, [R("we0", a, b)], (b - a) << 8))
         ops[s_e[k]]["late"] = s_e[k - 1] if k else s_m
-    s_e1 = s_e[3]
+    s_e1 = s_e[-1]
     arrive("am0", (1, 0), [R("misc1", 0, 33)], [s_m], 1, 0, (R("misc", 0, 33), 1))
     arrive("am1", (3, 0), [R("misc1", 33, 132)], [s_m], 1, 0, (R("misc", 33, 132), 1))
     arrive("am4", (0, 1), [R("misc4", 0, 33)], [s_m], 0, 0, (R("misc", 0, 33), 4))
     arrive("ae0", (4, 0), [R("we1", 0, 1024)], [s_e[1]], 1, 1 << 16, (R("we0", 0, 1024), 1))
-    a_e1 = arrive("ae1", (4, 0), [R("we1", 1024, 2048)], [s_e[3]], 1, 1 << 16, (R("we0", 1024, 2048), 1))
-    s_t = send("bulk0", [R("own0", 0, 2048)], 1 << 19, behind=[])
-    s_s = send("bulk1", [R("own0", 2048, 4096)], 1 << 19)
-    ops[s_t]["late"], ops[s_s]["late"] = s_e1, s_t
-    a_t = arrive("ab0", (2, 0), [R("w1b", 0, 2048)], [s_t, a_e1], 0, 1 << 18, (R("own0", 0, 2048), 1))
-    a_s = arrive("ab1", (2, 0), [R("w1b", 2048, 4096)], [s_s, a_t], 0, 1 << 18, (R("own0", 2048, 4096), 1))
-    dma("y", R("co4", 0, 4, 1, 0, 112), R("misc4", 0, 4, 1, 16, 128))
-    dma("y", R("co4", 0, 4, 1, 112, 128), R("misc4", 0, 4, 1, 0, 16))
-    for h, src in enumerate(("te", "sa")):
-        dma("y", R("stage4", 2048 * h, 2048 * h + 2048, 1, 0, 112), R(src, 0, 2048, 1, 16, 128), [a_e1], ahead=h << 19)
-        dma("y", R("stage4", 2048 * h, 2048 * h + 2048, 1, 112, 128), R(src, 0, 2048, 1, 0, 16), [a_e1], ahead=h << 19)
-    s_4 = send("bulk4", [R("stage4", 0, 4096)], 1 << 19, [a_t])
-    a_4 = arrive("ab4", (1, 1), [R("w4b", 0, 4096)], [s_4, a_s], 1, 1 << 19, (R("stage4", 0, 4096), 4))
-    for f, b in (("f1", "w1b"), ("f0", "own0"), ("f4", "w4b")):
-        dma("g", R(f, 0, 4096), R(b, 0, 4096), [a_4])
+    a_e1 = arrive("ae1", (6, 0), [R("we1", 1024, 2048)], [s_e1], 1, 1 << 15, (R("we0", 1024, 2048), 1))
+    for a in (0, 512):
+        act(R("wo0", a, a + 512), R("own0", 2 * a + 1, 2 * a + 1024, 2))
+    ops[cp(R("wo0", 1024, 2048), R("own0", 2049, 4096, 2))].update(late=pick["v"], first=1)
+    pick["v"] = len(ops) - 1
+    s_o = [send("odd%d" % h, [R("wo0", 1024 * h, 1024 * h + 1024)], 1 << 18) for h in (0, 1)]
+    s_s = send("whole", [R("own0", 0, 4096)], 1 << 20)
+    for i, j in zip(s_o + [s_s], [s_e1] + s_o):
+        ops[i]["late"] = j
+    a_t = arrive("ab0", (2, 0), [R("wo1", 0, 1024)], [s_o[0], a_e1], 0, 1 << 17, (R("wo0", 0, 1024), 1))
+    a_s = arrive("ab1", (2, 0), [R("wo1", 1024, 2048)], [s_o[1], a_t], 0, 1 << 17, (R("wo0", 1024, 2048), 1))
+    for e, src in enumerate(("we1", "wo1")):
+        for a in range(0, 2048, 1024 >> e):
+            o, x = R("w1b", 2 * a + e, 2 * a + (2048 >> e), 2), R(src, a, a + (1024 >> e))
+            woven = add("g", "gcp", (o, x), [x], [o], late=woven if e or a else s_s, first=1)
+    ops[dma("y", R("co4", 0, 4, 1, 0, 112), R("misc4", 0, 4, 1, 16, 128), ahead=1 << 18)]["late"] = load[-1]
+    ops[dma("y", R("co4", 0, 4, 1, 112, 128), R("misc4", 0, 4, 1, 0, 16), ahead=1 << 18)]["late"] = load[-1]
+    a_4 = arrive("ab4", (4, 0), [R("w4b", 0, 4096)], [a_s, s_s], 1, 1 << 19, (R("own0", 0, 4096), 4, 16))
+    for f, b in (("f0", "own0"), ("f1", "w1b"), ("f4", "w4b")):
+        d0 = dma("g", R(f, 0, 4096), R(b, 0, 4096))
+        if f == "f0":
+            ops[d0]["first"], ops[d0]["late"] = 1, woven
 
     iota(R("ci", 0, 8), [[-16, 8]], 0, 1)
     iota(R("ci", 8, 9), [[0, 1]], 0, 1)
@@ -293,7 +309,8 @@ def build(O):
     ts(R("ci", 9, 10), R("ci", 8, 9), 15, "bitwise_and")
     ts(R("cf", 8, 9), R("ci", 9, 10), 64.0, "mult")
     cp(R("cf", 9, 10), R("ci", 9, 10))
-    for k, val in enumerate((1.0, -8.5 * ALPHA, 2.0 if "x3" in O["on_g"] else 6.0, 4.0)):
+    for k, val in enumerate((1.0, -8.5 * ALPHA, 2.0 if "x3" in O["on_g"] else 6.0, 4.0, -16.0 * ALPHA,
+                             1.0 - (7.5 * ALPHA + (4.0 if "x3" in O["on_g"] else 0.0)) / 8)):
         ms(R("cf", 10 + k, 11 + k), val)
     ts(R("cf", 96, 112), R("cf", 96, 112), R("cf", 9, 10), "add")
     J = R("cf", 96, 96 + NM)
@@ -301,15 +318,16 @@ def build(O):
     for g in range(8):
         v = R("mm", 16 * g, 16 * g + 129 * 15 + 1, 129)
         ts(v, v, R("cf", g, g + 1), "add")
-    later = [iota(R("cu1", 1024 * h, 1024 * h + 1024), [[0, 1024]], 0, 0) for h in (0, 1)]
-    later += [iota(R("xs", NX + 508 * h, NX + 508 * h + 508), [[2, 508]], 1 + 1016 * h, 0) for h in range(4)]
-    for i in later:
-        ops[i]["late"] = s_s
+    for h in range(8):
+        ops[iota(R("xs", NX + 254 * h, NX + 254 * h + 254), [[2, 254]], 1 + 508 * h, 0)]["late"] = s_s
     ms(R("cu0", 0, 2048), 0.0)
     ts(R("cub0", 0, 128), R("misc", 4, 132), 1024.0 / ALPHA, "mult")
-    dma("y", R("cu0", 0, 2048, 1, 0, 128, 16), R("cub0", 0, 128))
+    ops[dma("y", R("cu0", 0, 2048, 1, 0, 128, 16), R("cub0", 0, 128), ahead=1 << 18)]["late"] = load[2]
     ts(R("cub1", 0, 128), R("misc1", 4, 132), 1024.0 / ALPHA, "mult")
-    dma("y", R("cu1", 0, 2048, 1, 0, 128, 16), R("cub1", 0, 128))
+
+    def currents(k):
+        dma("y", R("cu0", 0, 2048, 1, 0, 128, 16), R("cub%d" % k, 0, 128))
+
     ms(R("ones", 0, 128), 1.0)
     i_id = add("g", "sel", (R("ident", 0, 128), R("ones", 0, 128)), [R("ones", 0, 128)], [R("ident", 0, 128)])
     if not O["pe_dt"][0]:
@@ -317,7 +335,7 @@ def build(O):
     made = {("ident", 0)}
 
     def unit(val, x):
-        name, k = ("identb", (1.0, 0.5).index(val)) if _two(x) else ("ident", (1.0, -1.0, 0.5, -0.5).index(val))
+        name, k = "identb" if _two(x) else "ident", (1.0, -1.0).index(val)
         if (name, k) not in made:
             made.add((name, k))
             act(R(name, 128 * k, 128 * k + 128), R("ident", 0, 128), scale=val)
@@ -333,53 +351,48 @@ def build(O):
         act(R("xs", a, b), R("xs", 0, b - a), bias=float(2 * a))
     for a, b in ((0, 512), (512, 1024), (1024, 1536), (1536, NX)):
         ts(R("wt1", a, b), R("xs", a, b), R("misc1", 1, 2), "mult", R("misc1", 0, 1), "add")
-        for wt, co, off in (("wt0", "misc", 0), ("wt4", "co4", 0), ("wt1", "misc1", NX)):
-            if wt == "wt4" and O["wt4_v"]:
-                ts(R(wt, a, b), R("xs", a, b), R(co, 1, 2), "mult", R(co, 0, 1), "add")
-            elif O["one_act"]:
-                act(R(wt, off + a, off + b), R("xs", off + a, off + b), scale=R(co, 1, 2), bias=R(co, 0, 1))
-            else:
-                act(R(wt, off + a, off + b), R("xs", off + a, off + b), scale=R(co, 1, 2))
-                act(R(wt, off + a, off + b), R(wt, off + a, off + b), bias=R(co, 0, 1))
+    tables = []
+    for k, (wt, co, off) in enumerate((("wt4", "co4", 0), ("wt0", "misc", 0), ("wt1", "misc1", NX))):
+        for a in range(off, off + NX, NX // O["tab_n"]):
+            o, x = R(wt, a, a + NX // O["tab_n"]), R("xs", a, a + NX // O["tab_n"])
+            tables.append((k, act(o, x, scale=R(co, 1, 2))))
+            act(o, o, bias=R(co, 0, 1))
 
     def lane(name, a, width, e, n=NM):
         return R(name, a + e, a + width * (n - 1) + e + 1, width)
 
-    EDGE = 8.5 * ALPHA
-    ms(R("cs", 0, 28 * NM), BIG)
-    for e, val in ((0, -EDGE), (3, 0.0), (4, 8 * 126.0)):
-        ms(lane("cs", 0, 7, e, 4 * NM), val)
+    EDGE, EDGN = 8.5 * ALPHA, 7.5 * ALPHA
     for j in range(4):
-        for e in (1, 2):
-            ms(lane("cs", 7 * NM * j, 7, e), float(64 >> j))
+        ms(R("cs", 6 * NM * j, 6 * NM * (j + 1)), float(64 >> j))
+    for e, val in ((2, 8 * 126.0), (3, 0.0), (4, BIG), (5, BIG)):
+        ms(lane("cs", 0, 6, e, 4 * NM), val)
     iota(R("gi", 0, 128), [[-16, 8], [0, 16]], 0, 1)
     ts(R("gi", 128, 256), R("gi", 0, 128), 4, "arith_shift_right")
     for k in (0, 1):
         ts(R("eb", 128 * k, 128 * k + 128), R("gi", 128, 256), 0.0, "is_equal", EPS / (1 << k), "mult")
     ms(R("mc", 0, 512, 1, 0, 64), 0.0)
-    for k, (big, half) in enumerate(((M1, 0.0), (-M1, 0.25), (M1 / 2, -0.25) if O["keep"] else (-M1 / 2, 0.0), (-M1 / 2, 0.125))):
+    for k, (big, half) in enumerate(((M1, 0.0), (-M1, 0.25), (-M1 / 2, 0.0), (-M1 / 2, 0.125))):
         ms(R("mc", 128 * k, 128 * k + 128, 1, 0, 1), big)
         if half:
             ms(R("mc", 128 * k, 128 * k + 128, 1, 32, 33), half)
     ms(R("oneb", 0, QH), 1.0)
     RA, RW = (0, 6 * NM, 12 * NM), (6, 6, 7)
     ms(R("cr", 0, 19 * NM), BIG)
-    ms(R("tp", 0, 26 * NM), 0.0)
+    ms(R("tp", 0, 25 * NM), 0.0)
     for v in range(3):
         z = 1 if v < 2 else 0
         if z:
             ms(lane("cr", RA[v], RW[v], 0), -EDGE)
         ms(lane("cr", RA[v], RW[v], z), 0.0)
         ms(lane("cr", RA[v], RW[v], z + 2), float(4 >> v))
-        for name, a, e in (("cr", RA[v], z + 1), ("tp", 7 * NM + RA[v], z + 2)):
+        for name, a, e in (("cr", RA[v], z + 1), ("tp", 6 * NM + RA[v], z + 2)):
             ts(lane(name, a, RW[v], e), J, 2.0 * QH * (v + 1) - (0.0 if v else 1.0), "add")
-    for a, w in ((0, 7), (7 * NM, 6)):
-        ms(lane("tp", a, w, 0), BIG)
-    ts(lane("tp", 7 * NM, 6, 2), J, 1.0, "subtract")
+    ms(lane("tp", 6 * NM, 6, 0), BIG)
+    ts(lane("tp", 6 * NM, 6, 2), J, 1.0, "subtract")
 
-    NL, V1, DX, VX, T1, DF, N8, DH = range(8)
+    NL, V1, DX, VX, T1, DF, N8, DH, DK, C0, C1 = range(11)
     OCOL, OXI, OCOL1, OKQ, OXR, OC0, OX0, OKF = range(8)
-    SW = {"ps": (0, 7), "p1": (7, 6), "p2": (13, 6), "p3": (19, 7)}
+    SW = {"ps": (0, 6), "p1": (6, 6), "p2": (12, 6), "p3": (18, 7)}
 
     def st(s, i, name="st"):
         a, b = (0, 32) if s is None else (I0[s] // 16, (I0[s] + NWS[s]) // 16)
@@ -420,10 +433,10 @@ def build(O):
     def PH(s, h):
         return PS(("ht", "hs")[h], s)
 
-    rnd = [0]
+    rnd, mark = [0], {}
 
     def to_psum(s, h):
-        if h and O["pe_ds"][rnd[0]] == 7 and O["fuse_s"][rnd[0]] | O["pe_ss"][rnd[0]] == 15:
+        if h and O["pe_ds"][rnd[0]] == 7 and O["fuse_s"][rnd[0]] == 15:
             return
         if O["pe_copy"][h]:
             g = [(P1(s, h), R("ident", 0, 128), B("s1", s, h), True, True)]
@@ -443,8 +456,8 @@ def build(O):
                 l, q = R("mc", 128 * x, 128 * x + 128, 1, 0, 33 if x else 1), R("oneb", 0, nw, 1, 0, 33 if x else 1)
                 add("t", "mm", [(o, l, q, x == 0, x % 2 == 1)], [l, q], [o], goes_on=x > 0)
 
-    def vote(s, tv, sv, w, b0, z, sp, pe_s=False, pe_t=False, yes="yes", hook=None):
-        ds, m = B("ds", s), PS("ht" if pe_t else "m0", s)
+    def vote(s, tv, sv, w, b0, z, sp, pe_s=False, pe_t=None, yes="yes", hook=None, how="is_gt"):
+        ds, m = B("ds", s), PS("m0", s)
         hook = hook or {}
         if sv[0] == "ind":
             tt(ds, sv, B("s1", s, 1), "subtract")
@@ -457,103 +470,106 @@ def build(O):
         act(B("wg", s), w)
         for o, x in zip(*[halves(r, "rr" in sp) for r in (B("rr", s), ds)]):
             act(o, x, scale=b0)
+        dt = m
         if pe_t:
-            pe_sum(m, -1.0, B("s1", s, 0), 1.0, tv)
+            dt = PH(s, 0)
+            pe_sum(dt, -1.0, pe_t, 1.0, tv, "dt" in sp)
         else:
             for o, x, y in zip(*[halves(r, "sub" in sp) for r in (m, tv, P1(s, 0))]):
                 tt(o, x, y, "subtract")
         for f in hook.get("sub", ()):
             f()
-        for o, x in zip(*[halves(r, "mul" in sp) for r in (m, B("wg", s))]):
-            tt(o, x, o, "mult")
+        for o, x, y in zip(*[halves(r, "mul" in sp) for r in (m, B("wg", s), dt)]):
+            tt(o, x, y, "mult")
         for o, x, y in zip(*[halves(r, "yes" in sp) for r in (B(yes, s), m, B("rr", s))]):
-            tt(o, x, y, "is_gt")
+            tt(o, x, y, how)
         for f in hook.get("yes", ()):
             f()
         count(z, R("%s%d" % (yes, s), 0, 16 * _n(z)), "yes" in sp)
 
-    def vote_turned(s, w, b0, z, sp):
-        tt(B("ds", s), chosen(s, 1), B("sg", s), "subtract")
-        tt(B("dt", s), chosen(s, 0), B("tg", s), "subtract")
-        act(PH(s, 0), B("ds", s), scale=b0)
-        tt(B("aa", s), w, B("dt", s), "mult")
-        for o, x, y in zip(*[halves(r, "yes" in sp) for r in (B("yes", s), B("aa", s), PH(s, 0))]):
-            tt(o, x, y, "is_lt")
-        count(z, B("yes", s), "yes" in sp)
-
-    def levels(s, tab, a=0, b=2048):
+    def levels(s, tab, a=0, b=2048, half=True, apart=False):
         for h in (1, 0):
             win = R(tab, 2048 * h + a, 2048 * h + b)
             act(Qs(s, h, 0), IND(win, of(s, OCOL)))
-            if O["pe_h"][rnd[0]][h]:
-                hi = B("hb" if _two(win) else "dd", s, h)
-                act(hi, IND(win, of(s, OCOL1)))
-                pe_sum(PH(s, h), -0.5, Qs(s, h, 0), 0.5, hi)
-            elif O["fuse_n"][h]:
-                tt(B("dd", s, h), IND(win, of(s, OCOL1)), Qs(s, h, 0), "subtract")
-                act(PH(s, h), B("dd", s, h), scale=0.5)
-            else:
+            if h and apart:
                 act(PH(s, h), Qs(s, h, 0), scale=0.5)
                 act(B("dd", s, h), IND(win, of(s, OCOL1)), scale=0.5)
                 tt(PH(s, h), B("dd", s, h), PH(s, h), "subtract")
+                put_off.setdefault(s, []).append(lambda: act(B("dd", s, 1), PH(s, 1), scale=2.0))
+                continue
+            tt(B("dd", s, h), IND(win, of(s, OCOL1)), Qs(s, h, 0), "subtract")
+            if half:
+                act(PH(s, h), B("dd", s, h), scale=0.5)
 
     def at_depth(s, off, out):
-        act(B("kk", s), IND(R("cf", 16, 32), off), scale=0.125)
+        act(B("tg", s), IND(R("cf", 16, 32), off))
+        act(PH(s, 0), B("tg", s), scale=0.0625)
         for h in (1, 0):
-            tt(PS("m%d" % h, s), B("kk", s), PH(s, h), "mult")
+            tt(PS("m%d" % h, s), B("dd", s, h), PH(s, 0), "mult")
         for h in (1, 0):
             tt(out[h], PS("m%d" % h, s), Qs(s, h, 0), "add")
 
     def chosen(s, h):
-        return IND(R("q%d" % s, QH * h, QH * (7 + h)), of(s, OKF))
+        return IND(R("q%d" % s, QH * h, QH * (6 + h) + NWS[s]), of(s, OKF))
 
     def first_col(s, cast, low, half):
-        tt(st(s, T1), low, cast, "subtract")
-        ts(of(s, OC0), st(s, T1), 0.0625 if half else 0.125, "mult")
+        tt(st(s, T1), low, cast, "add")
+        if "c0" in O["on_g"] and not half:
+            act(st(s, C0), st(s, T1), scale=-0.125)
+            to_list("c0", of(s, OC0), st(s, C0))
+        else:
+            ts(of(s, OC0), st(s, T1), -0.0625 if half else -0.125, "mult")
 
-    def hop(s, tab, wt, wend, co, nxt, even=None, turned=False):
+    put_off = {}
+
+    def feed(s, k, o, x, scale=None, bias=None):
+        if O["off"] >> k & 1:
+            put_off.setdefault(s, []).append(lambda: act(o, x, scale, bias))
+        else:
+            act(o, x, scale, bias)
+
+    def hop(s, n, tab, wt, wend, co, nxt, even=None):
         phase(s, "")
         nc = NWS[s] // 16
         b0 = R(co, 2, 3)
         win = R(wt, 0, wend)
+        x3 = "x3" in O["on_g"]
         for j in range(4):
             oc, ox = (OC0, OX0) if j == 0 else (OCOL, OXI)
             wt_, ws_ = (R(even, 0, 1024), R(even, 1024, 2048)) if even else (R(tab, 0, 2048), R(tab, 2048, 4096))
-            pe_t = O["pe_dt"][rnd[0]] >> j & 1
-            tg = B("tb" if pe_t and _two(wt_) else "tg", s)
+            t1 = None
+            if O["pe_dt"][n] >> j & 1:
+                t1 = B("s1", s, 0) if n else R("own0", 4 * I0[s], 4 * (I0[s] + NWS[s]) - 3, 4)
+            tg = B("tb" if t1 and _two(wt_) else "tg", s)
             act(tg, IND(wt_, of(s, oc)))
             sv = IND(ws_, of(s, oc))
-            if j == 0 and turned:
+            if not O["fuse_s"][rnd[0]] >> j & 1:
                 act(B("sg", s), sv)
-                vote_turned(s, IND(win, of(s, ox)), b0, pin("ps", s, 1), O["split"])
-                for h in (0, 1):
-                    act(B("s1", s, h), chosen(s, h))
-                    to_psum(s, h)
+                sv = B("sg", s)
+            vote(s, tg, sv, IND(win, of(s, ox)), b0, pin("ps", s, 0), O["split"], False, t1, hook={"sub": put_off.pop(s, [])}, how="is_le")
+            scan(res("ps", s), PS("ps", s), R("cs", 6 * NM * j, 6 * NM * j + 6 * nc), -EDGN)
+            k = -0.0625 if even and j < 3 else -0.125
+            c = k * (EDGN + (4.0 if j == 3 and x3 else 0.0))
+            ts(of(s, OCOL), res("ps", s, 5), k, "mult", c, "add")
+            if j == 3 and "c1" in O["on_g"] and not even:
+                act(st(s, C1), res("ps", s, 5), scale=k, bias=R("cf", 15, 16))
+                to_list("c1", of(s, OCOL1), st(s, C1))
+            elif j == 3:
+                ts(of(s, OCOL1), res("ps", s, 5), k, "mult", c + 1.0, "add")
+            if j == 3 and not x3:
+                ts(of(s, OXI), res("ps", s, 4), 4.0, "add")
             else:
-                pe_s = O["pe_ss"][rnd[0]] >> j & 1
-                if pe_s or not O["fuse_s"][rnd[0]] >> j & 1:
-                    sg = B("hb" if pe_s and _two(ws_) else "sg", s)
-                    act(sg, sv)
-                    sv = sg
-                vote(s, tg, sv, IND(win, of(s, ox)), b0, pin("ps", s, 1), O["split"], O["pe_ss"][rnd[0]] >> j & 1, pe_t)
-            scan(res("ps", s), PS("ps", s), R("cs", 7 * NM * j, 7 * NM * j + 7 * nc))
-            ts(of(s, OCOL), res("ps", s, 5), -0.0625 if even and j < 3 else -0.125, "mult")
-            if j == 3:
-                ts(of(s, OCOL1), res("ps", s, 5), -0.125, "mult", 1.0, "add")
-            if j == 3 and "x3" not in O["on_g"]:
-                ts(of(s, OXI), res("ps", s, 6), 4.0, "add")
-            else:
-                to_list("v" if even else "xi", of(s, OXI), res("ps", s, 6))
+                to_list("v" if even else "xi", of(s, OXI), res("ps", s, 4))
             if j < 3 or nxt is not None:
-                act(pin("ps", s, 3), res("ps", s, 4), scale=-1.0)
-            if j == 2 and "x3" in O["on_g"]:
-                act(pin("ps", s, 6), pin("ps", s, 6), bias=R("cf", 13, 14))
+                feed(s, 0 if j < 3 else 1, pin("ps", s, 2), res("ps", s, 3), scale=-1.0)
+            if j == 2 and x3:
+                feed(s, 0, pin("ps", s, 4), pin("ps", s, 4), bias=R("cf", 13, 14))
         if nxt is not None:
-            act(pin("p3", s, 5), res("ps", s, 4))
-        act(pin("p1", s, 4), res("ps", s, 6), bias=R("cf", 12, 13))
-        if nxt == "home":
-            act(pin("ps", s, 5), wrapped(128, s))
-        levels(s, tab)
+            feed(s, 1, pin("p3", s, 5), res("ps", s, 3), scale=-1.0)
+        feed(s, 2, pin("p1", s, 4), res("ps", s, 4), bias=R("cf", 12, 13))
+        levels(s, tab, apart=O["apart"][n] >> s & 1)
+        if s == 0:
+            mark[n] = len(ops) - 1
         for h in (1, 0):
             tt(Qs(s, h, 1), PH(s, h), Qs(s, h, 0), "add")
         on, far = "yes" in O["rsplit"], nxt not in (None, "home")
@@ -564,13 +580,11 @@ def build(O):
             if v == 1:
                 x, o = res("p1", s), PS("p2", s)
                 act(R(o[0], o[1], o[2] - 1, 2), R(x[0], x[1], x[2] - 1, 2), bias=R("cf", 10, 11))
-                if far:
-                    act(pin("ps", s, 5), pin("p2", s, 1))
             else:
                 for e in (2, 4):
                     act(pin("p3", s, e - 1), res("p2", s, e))
                 if nxt is not None:
-                    act(pin("p3", s, 6), st(s, T1), bias=R("cf", 11, 12))
+                    act(pin("p3", s, 6), st(s, T1), scale=-1.0, bias=R("cf", 11, 12))
 
         for v, p in enumerate(("p1", "p2", "p3")):
             if v:
@@ -578,14 +592,14 @@ def build(O):
                     tt(PS("m%d" % h, s), B("dd", s, h), PS("ht", s), "mult")
                 for h in (0, 1):
                     tt(Qs(s, h, v + 1), PS("m%d" % h, s), Qs(s, h, 0), "add")
-            hook = {"sub": [], "yes": []}
+            hook = {"sub": put_off.pop(s, []), "yes": []}
             z = pin(p, s, 1 if v < 2 else 0)
             if far and v == 0:
                 z = lane(z[0], z[1], 6, 0, 2 * nc)
-            if v:
+            if v and not O["po"] >> (v - 1) & 1:
                 hook["sub"].append(lambda: pass_on(v))
             if v < 2:
-                hook["sub"].append(lambda: fraction(s, ([2] if O["keep"] else [0, (0, B("yez", s), False), 2]) if v else [0]))
+                hook["sub"].append(lambda: fraction(s, [0, (0, B("yez", s), False), 2] if v else [0]))
                 hook["yes"].append(lambda: fraction(s, [(1, B("yes", s), on), 3] if v else [(0, B("yez", s), on), 1]))
             vote(s, Qs(s, 0, v + 1), Qs(s, 1, v + 1), IND(win, of(s, OXR if v else OXI)), b0, z, O["rsplit"], O["pe_ds"][rnd[0]] >> v & 1,
                  yes="yes" if v else "yez", hook=hook)
@@ -593,26 +607,36 @@ def build(O):
             if v < 2:
                 to_list("xr", of(s, OXR), res(p, s, 4))
             if v == 0 and nxt is not None:
-                first_col(s, pin("p2", s, 1) if far else wrapped(128, s), res("ps", s, 4), False)
-        to_list("kf", of(s, OKF), res("p3", s, 1))
+                first_col(s, pin("p2", s, 1) if far else wrapped(128, s), res("ps", s, 3), False)
+            if v < 2 and O["po"] >> v & 1:
+                pass_on(v + 1)
+        to_list("kf" if nxt or not O["fin_v"][rnd[0]] >> s & 1 else "v", of(s, OKF), res("p3", s, 1))
         if nxt is not None:
             to_list("x0", of(s, OX0), res("p3", s, 5))
-            act(pin("ps", s, 6), res("p3", s, 6), scale=-1.0, bias=R("cf", 11, 12))
-            act(pin("p3", s, 4), res("p3", s, 4), scale=-1.0)
-            if not O["first"]:
-                for h in (1, 0):
-                    act(B("s1", s, h), chosen(s, h))
-                for h in (0, 1):
-                    to_psum(s, h)
+            feed(s, 3, pin("ps", s, 5), res("p3", s, 6), scale=-1.0, bias=R("cf", 14, 15))
+            for q in ("ps", "p3"):
+                feed(s, 3, pin(q, s, 4), res("p3", s, 4), scale=-1.0)
+            for h in (1, 0):
+                act(B("s1", s, h), chosen(s, h))
+            for h in (0, 1):
+                to_psum(s, h)
 
     def finish(s, rnd, out):
         for h in (1, 0):
             a = 2048 * h + 4 * I0[s] + rnd
             old = R("own0", a, a + 4 * NWS[s] - 3, 4)
-            df = B(("tg", "wg")[h], s)
-            tt(df, chosen(s, h), old, "subtract")
-            act(PS(("s1", "hs")[h], s), df, scale=0.25)
-            tt(R(out, 512 * h + I0[s], 512 * h + I0[s] + NWS[s]), PS(("s1", "hs")[h], s), old, "add")
+            df, part = B(("tg", "wg")[h], s), PH(s, h)
+            if O["fin_pe"][rnd] >> s & 1:
+                act(df, chosen(s, h))
+                pe_sum(part, -1.0, old, 1.0, df)
+                df = part
+            else:
+                tt(df, chosen(s, h), old, "subtract")
+            if O["fin_v"][rnd] >> s & 1:
+                ts(part, df, 0.25, "mult")
+            else:
+                act(part, df, scale=0.25)
+            tt(R(out, 512 * h + I0[s], 512 * h + I0[s] + NWS[s]), part, old, "add")
 
     def depart(s):
         tt(st(s, T1), st(s, DH), res("p3", s, 4), "subtract")
@@ -620,7 +644,11 @@ def build(O):
 
     def spread(f, src, s, h, on):
         a = 2048 * h + 4 * I0[s]
-        (cp if on == "v" else act)(R(f, a, a + 4 * NWS[s] - 3, 4), R(src, 512 * h + I0[s], 512 * h + I0[s] + NWS[s]))
+        o, x = R(f, a, a + 4 * NWS[s] - 3, 4), R(src, 512 * h + I0[s], 512 * h + I0[s] + NWS[s])
+        if on == "g":
+            add("g", "gcp", (o, x), [x], [o])
+        else:
+            (cp if on == "v" else act)(o, x)
 
     def casts(s):
         return 128 * (I0[s] // 32), 128 * -(-(I0[s] + NWS[s]) // 32)
@@ -629,10 +657,12 @@ def build(O):
         a, b = casts(s)
         if s == 0:
             tt(st(None, V1), st(None, NL), R("cf", 64, 96), "subtract")
-            act(st(None, N8), st(None, NL), scale=8.0)
-            tt(st(None, VX), st(None, dx), st(None, N8), "add")
-        act(pin("ps", s, 3), st(s, NL), scale=-8.0)
-        act(pin("p3", s, 4), st(s, dx))
+            act(st(None, N8), st(None, NL), scale=-8.0)
+            tt(st(None, VX), st(None, dx), st(None, N8), "subtract")
+            ts(st(None, DK), st(None, dx), EDGN, "subtract")
+        act(pin("ps", s, 2), st(s, NL), scale=8.0)
+        for q in ("ps", "p3"):
+            act(pin(q, s, 4), st(s, dx))
         ts(of(s, OCOL), st(s, V1), float(a), "subtract")
         if not half:
             ts(of(s, OCOL1), st(s, V1), a - 1.0, "subtract")
@@ -640,7 +670,7 @@ def build(O):
         act(B("yez", s, 1), IND(R("cu0", a, b), of(s, OCOL)))
         count(pin("ps", s, 5), B("yez", s, 1), False)
         first_col(s, pin("ps", s, 5), st(s, N8), half)
-        tt(pin("ps", s, 6), pin("ps", s, 5), st(s, dx), "add")
+        tt(pin("ps", s, 5), pin("ps", s, 5), st(s, DK), "add")
 
     ts(di(0), R("cf", 32, 64), R("cf", 8, 9), "add")
     ts(st(None, NL), di(0), 0.0625, "mult")
@@ -650,20 +680,20 @@ def build(O):
         nc = NWS[s] // 16
         for p, (a, w) in SW.items():
             act(PS(p, s), R("tp", a * NM, a * NM + w * nc))
-        if NWS[s] < QH:
-            ms(R("q%d" % s, NWS[s], 8 * QH), 0.0)
+        for k in range(7) if NWS[s] < QH else ():
+            ops[iota(R("q%d" % s, QH * k + NWS[s], QH * (k + 1)), [[0, QH - NWS[s]]], 0, 0)]["late"] = s_s
         start(s, True, DH)
         act(P1(s, 0), R("own0", 4 * I0[s], 4 * (I0[s] + NWS[s]) - 3, 4))
-        if O["pe_dt"][0]:
-            act(B("s1", s, 0), R("own0", 4 * I0[s], 4 * (I0[s] + NWS[s]) - 3, 4))
         act(B("s1", s, 1), R("own0", 2048 + 4 * I0[s], 2048 + 4 * (I0[s] + NWS[s]) - 3, 4))
         to_psum(s, 1)
+    currents(1)
     for s in range(NST):
-        hop(s, "w1b", "wt1", NX, "misc1", "cu1", "we1")
-        hop(s, "w4b", "wt4", NX, "co4", "home", turned=O["first"])
-        hop(s, "own0", "wt0", NX, "misc", None, turned=O["first"])
+        hop(s, 0, "w1b", "wt1", NX, "misc1", "cu0", "we1")
+        hop(s, 1, "w4b", "wt4", NX, "co4", "home")
+        hop(s, 2, "own0", "wt0", NX, "misc", None)
         finish(s, 0, "newb")
     phase(None, "m")
+    currents(0)
     arr = []
     for s in range(NST):
         new = [R("newb", 512 * h + I0[s], 512 * h + I0[s] + NWS[s]) for h in (0, 1)]
@@ -681,7 +711,7 @@ def build(O):
         for h in (0, 1):
             spread("f0", "newb", s, h, "s")
             spread("f1", "new1", s, h, "v" if h and s == NST - 1 else "s")
-            spread("f4", "new4s", s, h, "s")
+            spread("f4", "new4s", s, h, "g" if O["far_g"] else "s")
     rnd[0] = 1
     for s in range(NST):
         depart(s)
@@ -696,15 +726,16 @@ def build(O):
         cur[0] = s
         cp(of(s, OKQ), di(2, s))
         start(s, False, DX)
-        levels(s, "f0", *casts(s))
+        levels(s, "f0", *casts(s), half=False)
         at_depth(s, of(s, OKQ), [P1(s, 0), B("s1", s, 1)])
         to_psum(s, 1)
-        if O["pe_dt"][1]:
+        if O["pe_dt"][3]:
             act(B("s1", s, 0), P1(s, 0))
+    currents(1)
     for s in range(NST):
-        hop(s, "f1", "wt1", 2 * NX, "misc1", "cu1")
-        hop(s, "f4", "wt4", NX, "co4", "home", turned=O["first"])
-        hop(s, "f0", "wt0", NX, "misc", None, turned=O["first"])
+        hop(s, 3, "f1", "wt1", 2 * NX, "misc1", "cu0")
+        hop(s, 4, "f4", "wt4", NX, "co4", "home")
+        hop(s, 5, "f0", "wt0", NX, "misc", None)
         finish(s, 1, "new1")
         a, b = I0[s], I0[s] + NWS[s]
         for h, y in ((1, "ys"), (0, "yt")):
@@ -716,6 +747,21 @@ def build(O):
         add("t", "mm", g, [R("ident", 0, 128), st(s, DF)], [R(o, c, z)])
         act(R("new4s", a, b, 1, 0, 8), R(o, c, z, 1, 0, 8))
         dma("y", R("yd", a, b, 1, 0, 8), R("new4s", a, b, 1, 0, 8))
+    for k, i in tables:
+        if O["tab_at"][k] is not None:
+            ops[i]["late"] = mark[O["tab_at"][k]]
+    for i, o in enumerate(ops):
+        if o["e"] in pick and i > pick["v"] and "late" not in o and any(ops[d]["k"] == "arr" or (ops[d]["k"] == "dma" and d > load[-1]) for d in o["deps"]):
+            o["late"] = pick[o["e"]]
+    done = []
+    for o in ops:
+        hard, x = set(o["deps"] + o["sdeps"]), 0
+        for d in hard | set(o["soft"]):
+            x |= done[d]
+        o["near"] = sorted(d for d in hard if not x >> d & 1)
+        for d in hard:
+            x |= 1 << d
+        done.append(x)
     return ops
 
 
@@ -790,7 +836,7 @@ def lags(ops, P):
         p = {}
         for d in o["soft"] + ([o["late"]] if "late" in o else []):
             p[d] = cs[d][0]
-        for d in o["deps"] + o["sdeps"]:
+        for d in o["near"]:
             same = ops[d]["e"] == o["e"] and ops[d]["k"] not in ("dma", "send")
             p[d] = cs[d][1] + (P["same"] if same else P["wake"])
         pred.append(list(p.items()))
@@ -834,7 +880,37 @@ def squeeze(ops, P, end, rounds):
     return best[0], sorted(range(n), key=lambda i: best[1][i])
 
 
-def swaps(ops, P, seq, turns, width, x):
+def timings(ops, Ps):
+    eng = [o["e"] for o in ops]
+    L = [lags(ops, P) for P in Ps]
+    L = [([c[0] for c in cs], [c[1] for c in cs], pred) for cs, pred in L]
+    last = [i for i, o in enumerate(ops) if o["k"] == "dma"]
+    kept = [[[0.0] * len(ops) for _ in Ps], None]
+
+    def judge(seq, lo, limit):
+        out, new = 1.0, []
+        before = {eng[i]: i for i in seq[max(0, lo - 400):lo]}
+        for (hold, lat, pred), old in zip(L, kept[0]):
+            st = list(old)
+            free = {e: st[before[e]] + hold[before[e]] if e in before else 0.0 for e in "vstgy"}
+            for i in seq[lo:]:
+                e = eng[i]
+                t = free[e] if e else 0.0
+                for d, l in pred[i]:
+                    if st[d] + l > t:
+                        t = st[d] + l
+                st[i] = t
+                if e:
+                    free[e] = t + hold[i]
+            out *= max(st[i] + lat[i] for i in last)
+            new.append(st)
+        if out < limit:
+            kept[0] = new
+        return out
+    return judge
+
+
+def swaps(ops, P, seq, turns, width, x, judge=None):
     cs, pred = lags(ops, P)
     n = len(ops)
     hold, lat = [c[0] for c in cs], [c[1] for c in cs]
@@ -845,6 +921,7 @@ def swaps(ops, P, seq, turns, width, x):
     direct = [set(d for d, _ in p) for p in pred]
     mp, mn, seq = [-1] * n, [-1] * n, list(seq)
     head, tail = [0.0] * n, [0.0] * n
+    score = [judge(seq, 0, 1e300) if judge else 0.0]
 
     def link():
         last = {}
@@ -869,10 +946,21 @@ def swaps(ops, P, seq, turns, width, x):
 
     def mend(a, b, lo, hi):
         for i in seq[a:hi]:
-            head[i] = early(i, head[mp[i]] + hold[mp[i]] if mp[i] >= 0 else 0.0)
+            k = mp[i]
+            t = head[k] + hold[k] if k >= 0 else 0.0
+            for d, l in pred[i]:
+                if head[d] + l > t:
+                    t = head[d] + l
+            head[i] = t
         for i in reversed(seq[lo:b + 1]):
-            tail[i] = late(i, max(lat[i], tail[mn[i]] + hold[i]) if mn[i] >= 0 else lat[i])
-        return max(head[i] + tail[i] for i in seq[lo:hi])
+            k, t = mn[i], lat[i]
+            if k >= 0 and tail[k] + hold[i] > t:
+                t = tail[k] + hold[i]
+            for d, l in succ[i]:
+                if tail[d] + l > t:
+                    t = tail[d] + l
+            tail[i] = t
+        return max([head[i] + tail[i] for i in seq[lo:hi]])
 
     for lo in list(range(0, n, width // 2)) + list(range(width // 4, n, width // 2)):
         link()
@@ -881,7 +969,7 @@ def swaps(ops, P, seq, turns, width, x):
         hi = min(lo + width, n)
         pos = {seq[k]: k for k in range(lo, hi)}
         now = max(head[i] + tail[i] for i in seq[lo:hi])
-        best, barred = (now, seq[lo:hi]), {}
+        best, barred, was = (now, seq[lo:hi]), {}, seq[lo:hi]
         for turn in range(turns):
             cand = []
             for v in seq[lo:hi]:
@@ -921,6 +1009,12 @@ def swaps(ops, P, seq, turns, width, x):
             if now < best[0] - 1e-6:
                 best = (now, seq[lo:hi])
         seq[lo:hi] = best[1]
+        if judge and best[1] != was:
+            t = judge(seq, lo, score[0])
+            if t < score[0]:
+                score[0] = t
+            else:
+                seq[lo:hi] = was
     link()
     mend(0, n - 1, 0, n)
     return seq, [head[i] + lat[i] for i in range(n)]
@@ -932,6 +1026,10 @@ def plan(O, U):
     for k, width in enumerate(U["widths"]):
         seq, end = swaps(ops, PAR, seq, U["turns"], width, k + 1)
         seq = squeeze(ops, PAR, end, 2)[1]
+    Ps = [dict(PAR, cyc=0.83 * f, g=g, wake=w, same=0.9 * w, pe=pe * f, link=link) for f, g, w, pe, link in U["more"]]
+    judge = timings(ops, Ps)
+    for k in range(U["passes"]):
+        seq = swaps(ops, Ps[k % len(Ps)], seq, U["turns2"], U["widths2"][k % len(U["widths2"])], 100 + k, judge)[0]
     seq, end = swaps(ops, PAR, seq, 0, len(ops), 1)
     known = {e: 0 for e in "vstgy"}
     K, waits, raised, before, pre = {}, {}, set(), {}, {e: 0 for e in "vstgy"}
@@ -967,7 +1065,7 @@ def plan(O, U):
 
 OPS, SEQ, WAITS, SEM, _NAMES, TAIL, END = plan(OPT, TUNE)
 NST = len(OPT["nw"])
-SEMAPHORES = (_NAMES + ["am0", "am1", "am4", "ae0", "ae1", "ab0", "ab1", "ab4", "af", "sent", "rm", "re0", "re1", "rb0", "rf"]
+SEMAPHORES = (_NAMES + ["am0", "am1", "am4", "ae0", "ae1", "ab0", "ab1", "ab4", "af", "sent", "rm", "re0", "re1", "re2", "ro0", "rb0", "rf"]
               + ["an%d" % k for k in range(2 * NST)] + ["rn%d" % k for k in range(NST)])
 
 
@@ -986,11 +1084,14 @@ def piece(T, kind, k, landed):
     if kind == "m":
         return T["misc1" if landed else "misc"][:, 33 * k:33 * k + 33]
     if kind == "e":
-        return T["we1" if landed else "we0"][:, 256 * k:256 * k + 256]
+        a, b = EVEN[k // 2]
+        return T["we1" if landed else "we0"][:, a + (b - a) // 2 * (k % 2):a + (b - a) // 2 * (k % 2 + 1)]
+    if kind == "o":
+        return T["wo1" if landed else "wo0"][:, 512 * k:512 * k + 512]
     if kind == "b":
         return T["w1b" if landed else "own0"][:, 1024 * k:1024 * k + 1024]
     if kind == "f":
-        return T["w4b" if landed else "stage4"][:, 2048 * k:2048 * k + 2048]
+        return T.w4b[:, 1024 * k:1024 * k + 1024]
     w = OPT["nw"][k // 4] // 2
     a = 512 * (k // 2 % 2) + sum(OPT["nw"][:k // 4]) + w * (k % 2)
     return T["new1" if landed else "newb"][:, a:a + w]
@@ -1000,15 +1101,21 @@ def relay_program(g, core, T, topo, src, down, far, k):
     on, off = topo.engines(src, core), topo.engines(src, far)
     rest = len(on) - len(off)
     half = len(on) // 2
-    steps = [("m", k, rest // NREL, down, "am0" if k == 0 else "am1", "rm"), ("e", k, half, down, "ae0", "re0"),
-             ("e", k + 4, half, down, "ae1", "re1"), ("b", k, half, down, "ab%d" % (k // 2), "rb0")]
-    if k == 1:
-        steps.append(("f", 1, rest, far, "ab4", "rf"))
+    steps = [("m", k, rest // NREL, down, "am0" if k == 0 else "am1", "rm")]
+    steps += [("e", j, half, down, "ae%d" % (EVEN[j // 2][0] // 1024), "re%d" % (j // NREL)) for j in range(k, 2 * len(EVEN), NREL)]
+    steps.append(("o", k, half, down, "ab%d" % (k // 2), "ro0"))
+    steps.append(("f", k, 32, far, "ab4", "rf"))
+    a, b = 1024 * k, 1024 * k + 1024
+    g.sync.wait_ge(T.sem.rb0, len(on) // NREL)
+    g.sync.dma_start(T.w4b[0:112, a:b], T.w1b[16:128, a:b]).then_inc(T.sem.rf, 16)
+    g.sync.dma_start(T.w4b[112:128, a:b], T.w1b[0:16, a:b]).then_inc(T.sem.rf, 16)
     steps += [("n", k + NREL * s, len(on) // NREL, down, "an%d" % (k // 2 + 2 * s), "rn%d" % s) for s in range(NST)]
     total = 0
     for kind, j, n, dst, sem, got in steps:
         rid, pid = topo.addr(dst, core)
         g.wait_ge(T.sem[got], n)
+        if kind == "f":
+            g.wait_ge(T.sem.sent, total)
         p = piece(T, kind, j, True)
         g.remote_dma(p, p, T.sem[sem], T.sem.sent, pid, rid, topo.mask(core, dst))
         total += len(topo.engines(core, dst))
@@ -1036,7 +1143,7 @@ def rank_program(g, core, T, topo):
     Q = {"v": g.vector, "s": g.scalar, "t": g.tensor, "g": g, "y": g.sync}
     A, F = AluOpType, ActivationFunctionType
     alu = {"add": A.add, "subtract": A.subtract, "mult": A.mult, "max": A.max, "min": A.min, "is_ge": A.is_ge, "is_gt": A.is_gt,
-           "is_lt": A.is_lt, "is_equal": A.is_equal, "arith_shift_right": A.arith_shift_right, "bitwise_and": A.bitwise_and}
+           "is_le": A.is_le, "is_equal": A.is_equal, "arith_shift_right": A.arith_shift_right, "bitwise_and": A.bitwise_and}
     sent = [0]
 
     def ap(r):
@@ -1058,9 +1165,8 @@ def rank_program(g, core, T, topo):
             few = len(only_on) // NREL
             ts_ = [tr(rel[k], piece(T, "m", k, False), piece(T, "m", k, True), "rm", only_on[few * k:few * k + few]) for k in range(NREL)]
             ts_.append(tr(far, T.misc[:, 0:33], T.misc4[:, 0:33], "am4", off))
-        elif what == "bulk4":
-            ts_ = [tr(far, piece(T, "f", 0, False), piece(T, "f", 0, True), "ab4", off),
-                   tr(rel[1], piece(T, "f", 1, False), piece(T, "f", 1, True), "rf", only_on)]
+        elif what == "whole":
+            ts_ = [tr(rel[k], piece(T, "b", k, False), piece(T, "b", k, True), "rb0", on[k::NREL]) for k in range(NREL)]
         elif what == "far":
             ts_ = [tr(far, T.newb[:], T.new4[:], "af", off)]
         elif what[0] == "m":

import math
from concourse.bass import DstId, RemoteDMATransfer
from concourse.mybir import AluOpType, ActivationFunctionType

OPT = dict(nw=(176, 176, 160),
           fuse_s=(15, 15),
           pe_copy=(0, 1),
           fin_v=(0, 0),
           pe_ds=(2, 2),
           on_g=("xi", "xr", "kf", "x0", "x3", "c0", "c1"),
           pe_dt=(15, 0, 0, 0, 0, 0),
           split=("mul", "yes", "sub"), rsplit=("yes", "mul", "sub", "ds"),
           tab_n=8, tab_at=(None, 0, 1),
           fin_pe=(1, 1),
           off=0, po=0, apart=(0, 0, 0, 0, 0, 0),
           far_g=1)
EVEN = ((0, 512), (512, 1024), (1024, 1536), (1536, 1792), (1792, 2048))
NREL = 4
TUNE = dict(lead=600.0, look=0.0, noise=0.0, seed=1, role={}, leads=(600.0, 1400.0, 2000.0), widths=(120, 80, 160), turns=200,
            more=((1.0, 1.56, 200.0, 0.42, 45.0), (1.0, 1.2, 140.0, 0.42, 50.0), (1.15, 1.3, 250.0, 0.45, 45.0), (1.25, 1.56, 180.0, 0.42, 45.0),
                  (1.05, 1.3, 165.0, 0.42, 50.0), (1.4, 1.9, 220.0, 0.45, 45.0), (1.1, 1.9, 160.0, 0.45, 45.0)),
            passes=112, turns2=20, widths2=(100, 60, 140, 80, 120))
PAR = dict(fix=0.0, fixs=0.0, fuse=0.0, cyc=0.95, g=1.56, wake=200.0, same=180.0, pe=0.5, dma=2000.0, bw=160.0, call=900.0, leg=2500.0, link=45.0)
BIG = 2.0 ** 23
ALPHA = 65536.0
NX = 2032
M1 = 2.0 ** 22
EPS = 15.0 / 512


def layout(O):
    nws = O["nw"]
    S = {
        "own0": ("sbuf", [128, 4096], "bfloat16"), "w1b": ("sbuf", [128, 4096], "bfloat16"),
        "w4b": ("sbuf", [128, 4096], "bfloat16"),
        "we0": ("sbuf", [128, 2048], "bfloat16"), "we1": ("sbuf", [128, 2048], "bfloat16"),
        "wo0": ("sbuf", [128, 2048], "bfloat16"), "wo1": ("sbuf", [128, 2048], "bfloat16"),
        "f0": ("sbuf", [128, 4096], "float32"), "f1": ("sbuf", [128, 4096], "float32"), "f4": ("sbuf", [128, 4096], "float32"),
        "xs": ("sbuf", [128, 2 * NX], "float32"),
        "wt1": ("sbuf", [128, 2 * NX], "float32"), "wt4": ("sbuf", [128, NX], "float32"), "wt0": ("sbuf", [128, NX], "float32"),
        "cu0": ("sbuf", [128, 2048], "bfloat16"),
        "cui": ("sbuf", [128, 128], "int32"), "cub0": ("sbuf", [128, 128], "bfloat16"), "cub1": ("sbuf", [128, 128], "bfloat16"),
        "mm": ("sbuf", [128, 2048], "bfloat16"),
        "ones": ("sbuf", [128, 128], "float32"), "ident": ("sbuf", [128, 256], "float32"),
        "identb": ("sbuf", [128, 256], "bfloat16"),
        "misc": ("sbuf", [128, 132], "float32"), "misc1": ("sbuf", [128, 132], "float32"),
        "misc4": ("sbuf", [128, 33], "float32"), "co4": ("sbuf", [128, 4], "float32"),
        "newb": ("sbuf", [128, 1024], "float32"), "new1": ("sbuf", [128, 1024], "float32"),
        "new4": ("sbuf", [128, 1024], "float32"), "new4s": ("sbuf", [128, 1024], "float32"),
        "st": ("sbuf", [128, 11 * 32], "float32"), "di": ("sbuf", [128, 4 * 32], "int32"),
        "ci": ("sbuf", [128, 32], "int32"), "cf": ("sbuf", [128, 160], "float32"),
        "gi": ("sbuf", [128, 256], "int32"), "eb": ("sbuf", [128, 256], "bfloat16"), "mc": ("sbuf", [128, 512], "bfloat16"),
        "oneb": ("sbuf", [128, max(nws)], "bfloat16"),
        "cs": ("sbuf", [128, 28 * 16], "float32"), "cr": ("sbuf", [128, 19 * 16], "float32"), "tp": ("sbuf", [128, 26 * 16], "float32"),
    }
    qh = max(nws)
    for s, nw in enumerate(nws):
        nc = nw // 16
        for n in ("tg", "sg", "wg", "rr", "ds"):
            S["%s%d" % (n, s)] = ("sbuf", [128, nw], "float32")
        for n in ("s1", "dd"):
            S["%s%d" % (n, s)] = ("sbuf", [128, 2 * nw], "float32")
        S["q%d" % s] = ("sbuf", [128, 8 * qh], "float32")
        S["yes%d" % s] = ("sbuf", [128, nw], "bfloat16")
        S["yez%d" % s] = ("sbuf", [128, 2 * nw], "bfloat16")
        S["tb%d" % s] = ("sbuf", [128, nw], "bfloat16")
        S["so%d" % s] = ("sbuf", [128, 25 * nc], "float32")
        S["of%d" % s] = ("sbuf", [128, 8 * 16], "uint16")
    for b in range(8):
        S["bank%d" % b] = ("psum", [128, 512], "float32")
    P = {}
    for s, nw in enumerate(nws):
        nc = nw // 16
        rows = [("t1", "ht", "ps", "p3"), ("hs", "s1", "p1", "p2"), ("m0",), ("m1",)]
        banks = [2 * s, 2 * s + 1, 6, 7]
        base = [0, 0, sum(nws[:s]), sum(nws[:s])]
        for names, b, a in zip(rows, banks, base):
            for n in names:
                P[(n, s)] = ("bank%d" % b, a)
                a += {"ps": 6 * nc, "p1": 6 * nc, "p2": 6 * nc, "p3": 7 * nc}.get(n, nw)
    return S, P


SCRATCH, PLACE = layout(OPT)


def R(name, a, b, step=1, p0=0, p1=128, ps=1):
    return (name, a, b, step, p0, p1, ps)


def IND(win, off):
    return ("ind", win, off)


def _n(r):
    return 16 * _n(r[2]) if r[0] == "ind" else len(range(r[1], r[2], r[3]))


def _space(r):
    return "ind" if r[0] == "ind" else SCRATCH.get(r[0], ("hbm",))[0]


def _two(r):
    return r[0] != "ind" and r[0] in SCRATCH and SCRATCH[r[0]][2] in ("bfloat16", "uint16")


def _bytes(r):
    w = 2 if (r[0] in ("te", "sa") or _two(r)) else 4
    return _n(r) * len(range(r[4], r[5], r[6])) * w


def meet(x, r):
    return (x[1] < r[2] and r[1] < x[2] and x[4] < r[5] and r[4] < x[5] and (x[1] - r[1]) % math.gcd(x[3], r[3]) == 0)


def covers(r, x):
    return r[4] == 0 and r[5] == 128 and r[6] == 1 and r[1] <= x[1] and x[2] <= r[2] and x[3] % r[3] == 0 and (x[1] - r[1]) % r[3] == 0


def cost(op, P):
    k, a = op["k"], op["a"]
    c = P["cyc"]
    if k in ("tt", "ts", "cp", "act", "scan"):
        n = _n(a[0])
        if a[1][0] == "ind":
            t = (65 if k == "act" else 50) + n * P["g"] * c
        elif k == "tt":
            t = c * max(64, n * (2 if _space(a[1]) == "sbuf" and _space(a[2]) == "sbuf" else 1))
        elif k != "act" and _two(a[0]) and _two(a[1]):
            t = c * max(64, n / 2)
        else:
            t = c * max(64, n)
        if a[1][0] != "ind":
            t += P["fix"] + (P["fixs"] if k == "act" else 0.0)
        elif k == "tt":
            t += n * c * P["fuse"]
        return t, t
    if k == "ms":
        t = c * max(64, _n(a[0]) / (2 if _two(a[0]) else 1))
        return t, t
    if k == "mm":
        t = sum(P["pe"] * max(min(64, _n(m[1])), _n(m[2])) * (1 if _two(m[1]) else 4) for m in a)
        return t, t + 60
    if k in ("iota", "sel", "gcp"):
        t = 150 + 2 * c * _n(a[0])
        return t, t
    if k == "dma":
        return (P["call"] if op["e"] == "g" else 60), P["dma"] + op.get("ahead", 0) / P["bw"] + _bytes(a[0]) / P["bw"]
    if k == "send":
        return P["call"], P["leg"] + a[1] / P["bw"]
    if k == "arr":
        return 0, a[2] * P["leg"] + a[3] / P["link"]
    raise ValueError(k)


def build(O):
    ops, acc, bank, cur, seen, pe_last = [], {}, {}, [None, "a"], {}, {}
    NWS = O["nw"]
    NST = len(NWS)
    I0 = [sum(NWS[:s]) for s in range(NST)]
    QH = max(NWS)
    NM = QH // 16

    def add(e, k, a, rd, wr, after=(), **kw):
        i = len(ops)
        deps, soft = set(after), set()
        flat = []
        for r in rd:
            flat += [(r[1], False), (r[2], False)] if r[0] == "ind" else [(r, False)]
        flat += [(r, True) for r in wr]
        for r, w in flat:
            if r[0] not in SCRATCH:
                continue
            for (x, j, jw) in acc.setdefault(r[0], []):
                if (w or jw) and meet(x, r):
                    (soft if e == "t" and ops[j]["e"] == "t" and kw.get("goes_on") else deps).add(j)
            if SCRATCH[r[0]][0] == "psum":
                b = bank.setdefault(r[0], [e, [], []])
                if b[0] != e:
                    b[0], b[2], b[1] = e, b[1], []
                deps.update(b[2])
                b[1].append(i)
                if e == "t":
                    if r[0] in pe_last:
                        soft.add(pe_last[r[0]])
                    pe_last[r[0]] = i
        for r, w in flat:
            if r[0] not in SCRATCH:
                continue
            if w:
                acc[r[0]] = [t for t in acc[r[0]] if t[1] == i or not (t[0] == r or covers(r, t[0]))]
            acc[r[0]].append((r, i, w))
        deps.discard(i)
        key = "%s%s%d" % (e, wr[0][0], wr[0][1]) if wr else "send"
        seen[key] = seen.get(key, 0) + 1
        ops.append(dict(e=e, k=k, a=a, deps=sorted(deps), sdeps=[], soft=sorted(soft - deps - {i}), s=cur[0], role="%s%s.%d" % (cur[1], key, seen[key]), **kw))
        return i

    def phase(s, tag):
        cur[0], cur[1] = s, tag
        seen.clear()

    def refs(*xs):
        return [x for x in xs if isinstance(x, tuple)]

    def tt(o, x, y, op):
        return add("v", "tt", (o, x, y, op), [x, y], [o])

    def ts(o, x, s1, op0, s2=None, op1=None):
        return add("v", "ts", (o, x, s1, s2, op0, op1), refs(x, s1, s2), [o])

    def cp(o, x):
        return add("v", "cp", (o, x), [x], [o])

    def ms(o, val):
        return add("v", "ms", (o, val), [], [o])

    def act(o, x, scale=None, bias=None):
        return add("s", "act", (o, x, scale, bias), refs(x, scale, bias), [o])

    def scan(o, x, y, first=0.0):
        return add("v", "scan", (o, x, y, "subtract", "min", first), [x, y], [o])

    def iota(o, pat, base, cm):
        return add("g", "iota", (o, pat, base, cm), [], [o])

    def dma(q, o, x, after=(), ahead=0):
        return add(q, "dma", (o, x), [x], [o], after, ahead=ahead)

    def send(what, rd, nbytes, after=(), behind=()):
        i = add("g", "send", (what, nbytes), rd, [], after)
        ops[i]["sdeps"] += list(behind)
        return i

    def arrive(sem, n, wr, mirror, legs, nbytes, src):
        i = add(None, "arr", (sem, n, legs, nbytes, wr), [], wr, src=src)
        ops[i]["sdeps"] += list(mirror)
        return i

    def halves(r, on):
        return [(r[0], r[1] + e * r[3], r[2], 2 * r[3]) + r[4:] for e in (0, 1)] if on else [r]

    def count(o, src, on):
        n, a, b = src[:3]
        for es in ([range(0, 16, 2), range(1, 16, 2)] if on else [range(16)]):
            g = [(o, R("mm", 128 * e, 128 * e + 128), R(n, a + e, b, 16), e == 0, e == 15) for e in es]
            add("t", "mm", g, [R("mm", 0, 2048), R(n, a + es[0], b, es.step)], [o], goes_on=es[0] == 1)

    def to_list(name, o, x):
        return add("g", "gcp", (o, x), [x], [o]) if name in O["on_g"] else cp(o, x)

    d0 = dma("y", R("cui", 0, 128), R("cu", 0, 2048, 1, 0, 8))
    d1 = dma("s", R("misc", 0, 3), R("co", 0, 3))
    ops[d0]["first"] = ops[d1]["first"] = 5
    add("v", "ms", (R("misc", 3, 4), 0.0), [], [R("misc", 3, 4)], [d1], first=1)
    load = []
    for k, (a, b) in enumerate(EVEN):
        load.append(dma("y", R("own0", 2 * a, 2 * b), R(("te", "sa")[a // 1024], 2 * a % 2048, (2 * b - 1) % 2048 + 1),
                        load[(0, 0, 0, 1, 1)[k]:][:1] if k > 1 else (), ahead=(0, 4, 0, 1, 3)[k] << 16))
        ops[load[k]]["first"], ops[load[k]]["late"], d0 = 4, d0, load[k]
    ops[cp(R("misc", 4, 132), R("cui", 0, 128))]["first"] = 1
    s_m = send("misc", [R("misc", 0, 132)], 1 << 16)
    s_e = []
    for k, (a, b) in enumerate(EVEN):
        m = a + (b - a) * 3 // 8
        pick = {"s": act(R("we0", a, m), R("own0", 2 * a, 2 * m, 2)), "v": cp(R("we0", m, b), R("own0", 2 * m, 2 * b, 2))}
        for i in pick.values():
            ops[i]["first"] = 1
        s_e.append(send("even%d" % k, [R("we0", a, b)], (b - a) << 8))
        ops[s_e[k]]["late"] = s_e[k - 1] if k else s_m
    s_e1 = s_e[-1]
    arrive("am0", (1, 0), [R("misc1", 0, 33)], [s_m], 1, 0, (R("misc", 0, 33), 1))
    arrive("am1", (3, 0), [R("misc1", 33, 132)], [s_m], 1, 0, (R("misc", 33, 132), 1))
    arrive("am4", (0, 1), [R("misc4", 0, 33)], [s_m], 0, 0, (R("misc", 0, 33), 4))
    arrive("ae0", (4, 0), [R("we1", 0, 1024)], [s_e[1]], 1, 1 << 16, (R("we0", 0, 1024), 1))
    a_e1 = arrive("ae1", (6, 0), [R("we1", 1024, 2048)], [s_e1], 1, 1 << 15, (R("we0", 1024, 2048), 1))
    for a in (0, 512):
        act(R("wo0", a, a + 512), R("own0", 2 * a + 1, 2 * a + 1024, 2))
    ops[cp(R("wo0", 1024, 2048), R("own0", 2049, 4096, 2))].update(late=pick["v"], first=1)
    pick["v"] = len(ops) - 1
    s_o = [send("odd%d" % h, [R("wo0", 1024 * h, 1024 * h + 1024)], 1 << 18) for h in (0, 1)]
    s_s = send("whole", [R("own0", 0, 4096)], 1 << 20)
    for i, j in zip(s_o + [s_s], [s_e1] + s_o):
        ops[i]["late"] = j
    a_t = arrive("ab0", (2, 0), [R("wo1", 0, 1024)], [s_o[0], a_e1], 0, 1 << 17, (R("wo0", 0, 1024), 1))
    a_s = arrive("ab1", (2, 0), [R("wo1", 1024, 2048)], [s_o[1], a_t], 0, 1 << 17, (R("wo0", 1024, 2048), 1))
    for e, src in enumerate(("we1", "wo1")):
        for a in range(0, 2048, 1024 >> e):
            o, x = R("w1b", 2 * a + e, 2 * a + (2048 >> e), 2), R(src, a, a + (1024 >> e))
            woven = add("g", "gcp", (o, x), [x], [o], late=woven if e or a else s_s, first=1)
    ops[dma("y", R("co4", 0, 4, 1, 0, 112), R("misc4", 0, 4, 1, 16, 128), ahead=1 << 18)]["late"] = load[-1]
    ops[dma("y", R("co4", 0, 4, 1, 112, 128), R("misc4", 0, 4, 1, 0, 16), ahead=1 << 18)]["late"] = load[-1]
    a_4 = arrive("ab4", (4, 0), [R("w4b", 0, 4096)], [a_s, s_s], 1, 1 << 19, (R("own0", 0, 4096), 4, 16))
    for f, b in (("f0", "own0"), ("f1", "w1b"), ("f4", "w4b")):
        d0 = dma("g", R(f, 0, 4096), R(b, 0, 4096))
        if f == "f0":
            ops[d0]["first"], ops[d0]["late"] = 1, woven

    iota(R("ci", 0, 8), [[-16, 8]], 0, 1)
    iota(R("ci", 8, 9), [[0, 1]], 0, 1)
    iota(R("xs", 0, 256), [[2, 256]], 0, 0)
    iota(R("cf", 16, 32), [[1, 16]], 0, 0)
    iota(R("cf", 32, 64), [[0, 16], [1024, 2]], 0, 0)
    iota(R("cf", 64, 96), [[-128, 16], [0, 2]], 0, 0)
    iota(R("cf", 96, 112), [[16, 16]], 0, 0)
    iota(R("cf", 128, 160), [[-1024, 16], [0, 2]], 0, 0)
    ts(R("ci", 16, 24), R("ci", 0, 8), 4, "arith_shift_right")
    ts(R("cf", 0, 8), R("ci", 16, 24), 0.0, "is_equal", -ALPHA, "mult")
    ts(R("ci", 9, 10), R("ci", 8, 9), 15, "bitwise_and")
    ts(R("cf", 8, 9), R("ci", 9, 10), 64.0, "mult")
    cp(R("cf", 9, 10), R("ci", 9, 10))
    for k, val in enumerate((1.0, -8.5 * ALPHA, 2.0 if "x3" in O["on_g"] else 6.0, 4.0, -16.0 * ALPHA,
                             1.0 - (7.5 * ALPHA + (4.0 if "x3" in O["on_g"] else 0.0)) / 8)):
        ms(R("cf", 10 + k, 11 + k), val)
    ts(R("cf", 96, 112), R("cf", 96, 112), R("cf", 9, 10), "add")
    J = R("cf", 96, 96 + NM)
    ms(R("mm", 0, 2048), 0.0)
    for g in range(8):
        v = R("mm", 16 * g, 16 * g + 129 * 15 + 1, 129)
        ts(v, v, R("cf", g, g + 1), "add")
    for h in range(8):
        ops[iota(R("xs", NX + 254 * h, NX + 254 * h + 254), [[2, 254]], 1 + 508 * h, 0)]["late"] = s_s
    ms(R("cu0", 0, 2048), 0.0)
    ts(R("cub0", 0, 128), R("misc", 4, 132), 1024.0 / ALPHA, "mult")
    ops[dma("y", R("cu0", 0, 2048, 1, 0, 128, 16), R("cub0", 0, 128), ahead=1 << 18)]["late"] = load[2]
    ts(R("cub1", 0, 128), R("misc1", 4, 132), 1024.0 / ALPHA, "mult")

    def currents(k):
        dma("y", R("cu0", 0, 2048, 1, 0, 128, 16), R("cub%d" % k, 0, 128))

    ms(R("ones", 0, 128), 1.0)
    i_id = add("g", "sel", (R("ident", 0, 128), R("ones", 0, 128)), [R("ones", 0, 128)], [R("ident", 0, 128)])
    if not O["pe_dt"][0]:
        ops[i_id]["late"] = s_s
    made = {("ident", 0)}

    def unit(val, x):
        name, k = "identb" if _two(x) else "ident", (1.0, -1.0).index(val)
        if (name, k) not in made:
            made.add((name, k))
            act(R(name, 128 * k, 128 * k + 128), R("ident", 0, 128), scale=val)
        return R(name, 128 * k, 128 * k + 128)

    def pe_sum(o, a, x, b, y, on=False):
        add("t", "mm", [(o, unit(a, x), x, True, False)], [unit(a, x), x], [o])
        parts = list(zip(halves(o, on), halves(y, on)))
        for k, (p, q) in enumerate(parts):
            add("t", "mm", [(p, unit(b, q), q, False, k == len(parts) - 1)], [unit(b, q), q], [p], goes_on=True)

    for a, b in ((256, 512), (512, 1024), (1024, NX)):
        act(R("xs", a, b), R("xs", 0, b - a), bias=float(2 * a))
    for a, b in ((0, 512), (512, 1024), (1024, 1536), (1536, NX)):
        ts(R("wt1", a, b), R("xs", a, b), R("misc1", 1, 2), "mult", R("misc1", 0, 1), "add")
    tables = []
    for k, (wt, co, off) in enumerate((("wt4", "co4", 0), ("wt0", "misc", 0), ("wt1", "misc1", NX))):
        for a in range(off, off + NX, NX // O["tab_n"]):
            o, x = R(wt, a, a + NX // O["tab_n"]), R("xs", a, a + NX // O["tab_n"])
            tables.append((k, act(o, x, scale=R(co, 1, 2))))
            act(o, o, bias=R(co, 0, 1))

    def lane(name, a, width, e, n=NM):
        return R(name, a + e, a + width * (n - 1) + e + 1, width)

    EDGE, EDGN = 8.5 * ALPHA, 7.5 * ALPHA
    for j in range(4):
        ms(R("cs", 6 * NM * j, 6 * NM * (j + 1)), float(64 >> j))
    for e, val in ((2, 8 * 126.0), (3, 0.0), (4, BIG), (5, BIG)):
        ms(lane("cs", 0, 6, e, 4 * NM), val)
    iota(R("gi", 0, 128), [[-16, 8], [0, 16]], 0, 1)
    ts(R("gi", 128, 256), R("gi", 0, 128), 4, "arith_shift_right")
    for k in (0, 1):
        ts(R("eb", 128 * k, 128 * k + 128), R("gi", 128, 256), 0.0, "is_equal", EPS / (1 << k), "mult")
    ms(R("mc", 0, 512, 1, 0, 64), 0.0)
    for k, (big, half) in enumerate(((M1, 0.0), (-M1, 0.25), (-M1 / 2, 0.0), (-M1 / 2, 0.125))):
        ms(R("mc", 128 * k, 128 * k + 128, 1, 0, 1), big)
        if half:
            ms(R("mc", 128 * k, 128 * k + 128, 1, 32, 33), half)
    ms(R("oneb", 0, QH), 1.0)
    RA, RW = (0, 6 * NM, 12 * NM), (6, 6, 7)
    ms(R("cr", 0, 19 * NM), BIG)
    ms(R("tp", 0, 25 * NM), 0.0)
    for v in range(3):
        z = 1 if v < 2 else 0
        if z:
            ms(lane("cr", RA[v], RW[v], 0), -EDGE)
        ms(lane("cr", RA[v], RW[v], z), 0.0)
        ms(lane("cr", RA[v], RW[v], z + 2), float(4 >> v))
        for name, a, e in (("cr", RA[v], z + 1), ("tp", 6 * NM + RA[v], z + 2)):
            ts(lane(name, a, RW[v], e), J, 2.0 * QH * (v + 1) - (0.0 if v else 1.0), "add")
    ms(lane("tp", 6 * NM, 6, 0), BIG)
    ts(lane("tp", 6 * NM, 6, 2), J, 1.0, "subtract")

    NL, V1, DX, VX, T1, DF, N8, DH, DK, C0, C1 = range(11)
    OCOL, OXI, OCOL1, OKQ, OXR, OC0, OX0, OKF = range(8)
    SW = {"ps": (0, 6), "p1": (6, 6), "p2": (12, 6), "p3": (18, 7)}

    def st(s, i, name="st"):
        a, b = (0, 32) if s is None else (I0[s] // 16, (I0[s] + NWS[s]) // 16)
        return R(name, 32 * i + a, 32 * i + b)

    def of(s, i):
        return R("of%d" % s, 16 * i, 16 * i + NWS[s] // 16)

    def di(i, s=None):
        return st(s, i, "di")

    def B(name, s, h=0):
        return R("%s%d" % (name, s), NWS[s] * h, NWS[s] * (h + 1))

    def PS(name, s):
        b, a = PLACE[(name, s)]
        return R(b, a, a + (SW[name][1] * NWS[s] // 16 if name in SW else NWS[s]))

    def pin(name, s, e):
        b, a = PLACE[(name, s)]
        return lane(b, a, SW[name][1], e, NWS[s] // 16)

    def res(name, s, e=None):
        nc = NWS[s] // 16
        a, w = SW[name]
        return R("so%d" % s, a * nc, (a + w) * nc) if e is None else lane("so%d" % s, a * nc, w, e, nc)

    def wrapped(a, s):
        return R("cf", a + I0[s] // 16, a + (I0[s] + NWS[s]) // 16)

    def Qs(s, h, k):
        a = QH * (2 * k + h)
        return R("q%d" % s, a, a + NWS[s])

    def P1(s, h):
        return PS(("t1", "s1")[h], s)

    def PH(s, h):
        return PS(("ht", "hs")[h], s)

    rnd, mark = [0], {}

    def to_psum(s, h):
        if h and O["pe_ds"][rnd[0]] == 7 and O["fuse_s"][rnd[0]] == 15:
            return
        if O["pe_copy"][h]:
            g = [(P1(s, h), R("ident", 0, 128), B("s1", s, h), True, True)]
            add("t", "mm", g, [R("ident", 0, 128), B("s1", s, h)], [P1(s, h)])
        else:
            act(P1(s, h), B("s1", s, h))

    def fraction(s, steps):
        o, nw = PS("ht", s), NWS[s]
        for x in steps:
            if isinstance(x, tuple):
                k, y, on = x
                for p, q in zip(halves(o, on), halves(y, on)):
                    l = R("eb", 128 * k, 128 * k + 128)
                    add("t", "mm", [(p, l, q, False, False)], [l, q], [p], goes_on=True)
            else:
                l, q = R("mc", 128 * x, 128 * x + 128, 1, 0, 33 if x else 1), R("oneb", 0, nw, 1, 0, 33 if x else 1)
                add("t", "mm", [(o, l, q, x == 0, x % 2 == 1)], [l, q], [o], goes_on=x > 0)

    def vote(s, tv, sv, w, b0, z, sp, pe_s=False, pe_t=None, yes="yes", hook=None, how="is_gt"):
        ds, m = B("ds", s), PS("m0", s)
        hook = hook or {}
        if sv[0] == "ind":
            tt(ds, sv, B("s1", s, 1), "subtract")
        elif pe_s:
            ds = PH(s, 1)
            pe_sum(ds, -1.0, B("s1", s, 1), 1.0, sv, "ds" in sp)
        else:
            for o, x, y in zip(*[halves(r, "ds" in sp) for r in (ds, sv, P1(s, 1))]):
                tt(o, x, y, "subtract")
        act(B("wg", s), w)
        for o, x in zip(*[halves(r, "rr" in sp) for r in (B("rr", s), ds)]):
            act(o, x, scale=b0)
        dt = m
        if pe_t:
            dt = PH(s, 0)
            pe_sum(dt, -1.0, pe_t, 1.0, tv, "dt" in sp)
        else:
            for o, x, y in zip(*[halves(r, "sub" in sp) for r in (m, tv, P1(s, 0))]):
                tt(o, x, y, "subtract")
        for f in hook.get("sub", ()):
            f()
        for o, x, y in zip(*[halves(r, "mul" in sp) for r in (m, B("wg", s), dt)]):
            tt(o, x, y, "mult")
        for o, x, y in zip(*[halves(r, "yes" in sp) for r in (B(yes, s), m, B("rr", s))]):
            tt(o, x, y, how)
        for f in hook.get("yes", ()):
            f()
        count(z, R("%s%d" % (yes, s), 0, 16 * _n(z)), "yes" in sp)

    def levels(s, tab, a=0, b=2048, half=True, apart=False):
        for h in (1, 0):
            win = R(tab, 2048 * h + a, 2048 * h + b)
            act(Qs(s, h, 0), IND(win, of(s, OCOL)))
            if h and apart:
                act(PH(s, h), Qs(s, h, 0), scale=0.5)
                act(B("dd", s, h), IND(win, of(s, OCOL1)), scale=0.5)
                tt(PH(s, h), B("dd", s, h), PH(s, h), "subtract")
                put_off.setdefault(s, []).append(lambda: act(B("dd", s, 1), PH(s, 1), scale=2.0))
                continue
            tt(B("dd", s, h), IND(win, of(s, OCOL1)), Qs(s, h, 0), "subtract")
            if half:
                act(PH(s, h), B("dd", s, h), scale=0.5)

    def at_depth(s, off, out):
        act(B("tg", s), IND(R("cf", 16, 32), off))
        act(PH(s, 0), B("tg", s), scale=0.0625)
        for h in (1, 0):
            tt(PS("m%d" % h, s), B("dd", s, h), PH(s, 0), "mult")
        for h in (1, 0):
            tt(out[h], PS("m%d" % h, s), Qs(s, h, 0), "add")

    def chosen(s, h):
        return IND(R("q%d" % s, QH * h, QH * (6 + h) + NWS[s]), of(s, OKF))

    def first_col(s, cast, low, half):
        tt(st(s, T1), low, cast, "add")
        if "c0" in O["on_g"] and not half:
            act(st(s, C0), st(s, T1), scale=-0.125)
            to_list("c0", of(s, OC0), st(s, C0))
        else:
            ts(of(s, OC0), st(s, T1), -0.0625 if half else -0.125, "mult")

    put_off = {}

    def feed(s, k, o, x, scale=None, bias=None):
        if O["off"] >> k & 1:
            put_off.setdefault(s, []).append(lambda: act(o, x, scale, bias))
        else:
            act(o, x, scale, bias)

    def hop(s, n, tab, wt, wend, co, nxt, even=None):
        phase(s, "")
        nc = NWS[s] // 16
        b0 = R(co, 2, 3)
        win = R(wt, 0, wend)
        x3 = "x3" in O["on_g"]
        for j in range(4):
            oc, ox = (OC0, OX0) if j == 0 else (OCOL, OXI)
            wt_, ws_ = (R(even, 0, 1024), R(even, 1024, 2048)) if even else (R(tab, 0, 2048), R(tab, 2048, 4096))
            t1 = None
            if O["pe_dt"][n] >> j & 1:
                t1 = B("s1", s, 0) if n else R("own0", 4 * I0[s], 4 * (I0[s] + NWS[s]) - 3, 4)
            tg = B("tb" if t1 and _two(wt_) else "tg", s)
            act(tg, IND(wt_, of(s, oc)))
            sv = IND(ws_, of(s, oc))
            if not O["fuse_s"][rnd[0]] >> j & 1:
                act(B("sg", s), sv)
                sv = B("sg", s)
            vote(s, tg, sv, IND(win, of(s, ox)), b0, pin("ps", s, 0), O["split"], False, t1, hook={"sub": put_off.pop(s, [])}, how="is_le")
            scan(res("ps", s), PS("ps", s), R("cs", 6 * NM * j, 6 * NM * j + 6 * nc), -EDGN)
            k = -0.0625 if even and j < 3 else -0.125
            c = k * (EDGN + (4.0 if j == 3 and x3 else 0.0))
            ts(of(s, OCOL), res("ps", s, 5), k, "mult", c, "add")
            if j == 3 and "c1" in O["on_g"] and not even:
                act(st(s, C1), res("ps", s, 5), scale=k, bias=R("cf", 15, 16))
                to_list("c1", of(s, OCOL1), st(s, C1))
            elif j == 3:
                ts(of(s, OCOL1), res("ps", s, 5), k, "mult", c + 1.0, "add")
            if j == 3 and not x3:
                ts(of(s, OXI), res("ps", s, 4), 4.0, "add")
            else:
                to_list("v" if even else "xi", of(s, OXI), res("ps", s, 4))
            if j < 3 or nxt is not None:
                feed(s, 0 if j < 3 else 1, pin("ps", s, 2), res("ps", s, 3), scale=-1.0)
            if j == 2 and x3:
                feed(s, 0, pin("ps", s, 4), pin("ps", s, 4), bias=R("cf", 13, 14))
        if nxt is not None:
            feed(s, 1, pin("p3", s, 5), res("ps", s, 3), scale=-1.0)
        feed(s, 2, pin("p1", s, 4), res("ps", s, 4), bias=R("cf", 12, 13))
        levels(s, tab, apart=O["apart"][n] >> s & 1)
        if s == 0:
            mark[n] = len(ops) - 1
        for h in (1, 0):
            tt(Qs(s, h, 1), PH(s, h), Qs(s, h, 0), "add")
        on, far = "yes" in O["rsplit"], nxt not in (None, "home")
        if far:
            act(B("yez", s, 1), IND(R(nxt, 0, 2048), of(s, OCOL)))

        def pass_on(v):
            if v == 1:
                x, o = res("p1", s), PS("p2", s)
                act(R(o[0], o[1], o[2] - 1, 2), R(x[0], x[1], x[2] - 1, 2), bias=R("cf", 10, 11))
            else:
                for e in (2, 4):
                    act(pin("p3", s, e - 1), res("p2", s, e))
                if nxt is not None:
                    act(pin("p3", s, 6), st(s, T1), scale=-1.0, bias=R("cf", 11, 12))

        for v, p in enumerate(("p1", "p2", "p3")):
            if v:
                for h in (0, 1):
                    tt(PS("m%d" % h, s), B("dd", s, h), PS("ht", s), "mult")
                for h in (0, 1):
                    tt(Qs(s, h, v + 1), PS("m%d" % h, s), Qs(s, h, 0), "add")
            hook = {"sub": put_off.pop(s, []), "yes": []}
            z = pin(p, s, 1 if v < 2 else 0)
            if far and v == 0:
                z = lane(z[0], z[1], 6, 0, 2 * nc)
            if v and not O["po"] >> (v - 1) & 1:
                hook["sub"].append(lambda: pass_on(v))
            if v < 2:
                hook["sub"].append(lambda: fraction(s, [0, (0, B("yez", s), False), 2] if v else [0]))
                hook["yes"].append(lambda: fraction(s, [(1, B("yes", s), on), 3] if v else [(0, B("yez", s), on), 1]))
            vote(s, Qs(s, 0, v + 1), Qs(s, 1, v + 1), IND(win, of(s, OXR if v else OXI)), b0, z, O["rsplit"], O["pe_ds"][rnd[0]] >> v & 1,
                 yes="yes" if v else "yez", hook=hook)
            scan(res(p, s), PS(p, s), R("cr", RA[v], RA[v] + RW[v] * nc), -EDGE if v == 2 else 0.0)
            if v < 2:
                to_list("xr", of(s, OXR), res(p, s, 4))
            if v == 0 and nxt is not None:
                first_col(s, pin("p2", s, 1) if far else wrapped(128, s), res("ps", s, 3), False)
            if v < 2 and O["po"] >> v & 1:
                pass_on(v + 1)
        to_list("kf" if nxt or not O["fin_v"][rnd[0]] >> s & 1 else "v", of(s, OKF), res("p3", s, 1))
        if nxt is not None:
            to_list("x0", of(s, OX0), res("p3", s, 5))
            feed(s, 3, pin("ps", s, 5), res("p3", s, 6), scale=-1.0, bias=R("cf", 14, 15))
            for q in ("ps", "p3"):
                feed(s, 3, pin(q, s, 4), res("p3", s, 4), scale=-1.0)
            for h in (1, 0):
                act(B("s1", s, h), chosen(s, h))
            for h in (0, 1):
                to_psum(s, h)

    def finish(s, rnd, out):
        for h in (1, 0):
            a = 2048 * h + 4 * I0[s] + rnd
            old = R("own0", a, a + 4 * NWS[s] - 3, 4)
            df, part = B(("tg", "wg")[h], s), PH(s, h)
            if O["fin_pe"][rnd] >> s & 1:
                act(df, chosen(s, h))
                pe_sum(part, -1.0, old, 1.0, df)
                df = part
            else:
                tt(df, chosen(s, h), old, "subtract")
            if O["fin_v"][rnd] >> s & 1:
                ts(part, df, 0.25, "mult")
            else:
                act(part, df, scale=0.25)
            tt(R(out, 512 * h + I0[s], 512 * h + I0[s] + NWS[s]), part, old, "add")

    def depart(s):
        tt(st(s, T1), st(s, DH), res("p3", s, 4), "subtract")
        ts(di(0, s), st(s, T1), 0.25, "subtract")

    def spread(f, src, s, h, on):
        a = 2048 * h + 4 * I0[s]
        o, x = R(f, a, a + 4 * NWS[s] - 3, 4), R(src, 512 * h + I0[s], 512 * h + I0[s] + NWS[s])
        if on == "g":
            add("g", "gcp", (o, x), [x], [o])
        else:
            (cp if on == "v" else act)(o, x)

    def casts(s):
        return 128 * (I0[s] // 32), 128 * -(-(I0[s] + NWS[s]) // 32)

    def start(s, half, dx):
        a, b = casts(s)
        if s == 0:
            tt(st(None, V1), st(None, NL), R("cf", 64, 96), "subtract")
            act(st(None, N8), st(None, NL), scale=-8.0)
            tt(st(None, VX), st(None, dx), st(None, N8), "subtract")
            ts(st(None, DK), st(None, dx), EDGN, "subtract")
        act(pin("ps", s, 2), st(s, NL), scale=8.0)
        for q in ("ps", "p3"):
            act(pin(q, s, 4), st(s, dx))
        ts(of(s, OCOL), st(s, V1), float(a), "subtract")
        if not half:
            ts(of(s, OCOL1), st(s, V1), a - 1.0, "subtract")
        to_list("v" if half else "x0", of(s, OX0), st(s, VX))
        act(B("yez", s, 1), IND(R("cu0", a, b), of(s, OCOL)))
        count(pin("ps", s, 5), B("yez", s, 1), False)
        first_col(s, pin("ps", s, 5), st(s, N8), half)
        tt(pin("ps", s, 5), pin("ps", s, 5), st(s, DK), "add")

    ts(di(0), R("cf", 32, 64), R("cf", 8, 9), "add")
    ts(st(None, NL), di(0), 0.0625, "mult")
    ts(st(None, DH), di(0), 0.5, "mult")
    for s in range(NST):
        cur[0] = s
        nc = NWS[s] // 16
        for p, (a, w) in SW.items():
            act(PS(p, s), R("tp", a * NM, a * NM + w * nc))
        for k in range(7) if NWS[s] < QH else ():
            ops[iota(R("q%d" % s, QH * k + NWS[s], QH * (k + 1)), [[0, QH - NWS[s]]], 0, 0)]["late"] = s_s
        start(s, True, DH)
        act(P1(s, 0), R("own0", 4 * I0[s], 4 * (I0[s] + NWS[s]) - 3, 4))
        act(B("s1", s, 1), R("own0", 2048 + 4 * I0[s], 2048 + 4 * (I0[s] + NWS[s]) - 3, 4))
        to_psum(s, 1)
    currents(1)
    for s in range(NST):
        hop(s, 0, "w1b", "wt1", NX, "misc1", "cu0", "we1")
        hop(s, 1, "w4b", "wt4", NX, "co4", "home")
        hop(s, 2, "own0", "wt0", NX, "misc", None)
        finish(s, 0, "newb")
    phase(None, "m")
    currents(0)
    arr = []
    for s in range(NST):
        new = [R("newb", 512 * h + I0[s], 512 * h + I0[s] + NWS[s]) for h in (0, 1)]
        sn = send("mid%d" % s, new, 1024 * NWS[s])
        if arr:
            ops[sn]["late"] = last_sn
        last_sn = sn
        for h in (1, 0):
            arr.append(arrive("an%d" % (2 * s + h), (2, 0), [("new1",) + new[h][1:]], [sn], 1, 256 * NWS[s], (new[h], 1)))
    s_n = send("far", [R("newb", 0, 1024)], 0, arr)
    arrive("af", (0, 1), [R("new4", 0, 1024)], [s_n], 0, 1 << 19, (R("newb", 0, 1024), 4))
    dma("y", R("new4s", 0, 1024, 1, 0, 112), R("new4", 0, 1024, 1, 16, 128))
    dma("y", R("new4s", 0, 1024, 1, 112, 128), R("new4", 0, 1024, 1, 0, 16))
    for s in range(NST):
        for h in (0, 1):
            spread("f0", "newb", s, h, "s")
            spread("f1", "new1", s, h, "v" if h and s == NST - 1 else "s")
            spread("f4", "new4s", s, h, "g" if O["far_g"] else "s")
    rnd[0] = 1
    for s in range(NST):
        depart(s)
    ts(st(None, DH), di(0), 0.5, "mult")
    ts(di(1), di(0), 4, "arith_shift_right")
    cp(st(None, NL), di(1))
    ts(di(2), di(0), 15, "bitwise_and")
    ts(di(3), di(0), 1, "bitwise_and")
    ts(st(None, DF), di(3), NX - 0.5, "mult")
    tt(st(None, DX), st(None, DF), st(None, DH), "add")
    for s in range(NST):
        cur[0] = s
        cp(of(s, OKQ), di(2, s))
        start(s, False, DX)
        levels(s, "f0", *casts(s), half=False)
        at_depth(s, of(s, OKQ), [P1(s, 0), B("s1", s, 1)])
        to_psum(s, 1)
        if O["pe_dt"][3]:
            act(B("s1", s, 0), P1(s, 0))
    currents(1)
    for s in range(NST):
        hop(s, 3, "f1", "wt1", 2 * NX, "misc1", "cu0")
        hop(s, 4, "f4", "wt4", NX, "co4", "home")
        hop(s, 5, "f0", "wt0", NX, "misc", None)
        finish(s, 1, "new1")
        a, b = I0[s], I0[s] + NWS[s]
        for h, y in ((1, "ys"), (0, "yt")):
            dma("y", R(y, a, b), R("new1", 512 * h + a, 512 * h + b))
        depart(s)
        cp(st(s, DF), di(0, s))
        o, c, z = P1(s, 0)[:3]
        g = [(R(o, c + e, z, 16, 0, 8), R("ident", e, 128, 16), st(s, DF), True, True) for e in range(16)]
        add("t", "mm", g, [R("ident", 0, 128), st(s, DF)], [R(o, c, z)])
        act(R("new4s", a, b, 1, 0, 8), R(o, c, z, 1, 0, 8))
        dma("y", R("yd", a, b, 1, 0, 8), R("new4s", a, b, 1, 0, 8))
    for k, i in tables:
        if O["tab_at"][k] is not None:
            ops[i]["late"] = mark[O["tab_at"][k]]
    for i, o in enumerate(ops):
        if o["e"] in pick and i > pick["v"] and "late" not in o and any(ops[d]["k"] == "arr" or (ops[d]["k"] == "dma" and d > load[-1]) for d in o["deps"]):
            o["late"] = pick[o["e"]]
    done = []
    for o in ops:
        hard, x = set(o["deps"] + o["sdeps"]), 0
        for d in hard | set(o["soft"]):
            x |= done[d]
        o["near"] = sorted(d for d in hard if not x >> d & 1)
        for d in hard:
            x |= 1 << d
        done.append(x)
    return ops


def order(ops, P, U):
    n = len(ops)
    cs = [cost(o, P) for o in ops]
    succ = [[] for _ in ops]
    left = [0] * n
    for i, o in enumerate(ops):
        for d in o["deps"] + o["sdeps"]:
            succ[d].append(i)
            left[i] += 1
    pri = [0.0] * n
    behind = [[] for _ in ops]
    for i, o in enumerate(ops):
        for d in o["soft"]:
            behind[d].append(i)
    for i in range(n - 1, -1, -1):
        pri[i] = cs[i][1] + max([pri[j] + P["wake"] for j in succ[i]] + [pri[j] for j in behind[i]] + [0.0])
    x = U["seed"]
    for i, o in enumerate(ops):
        x = (x * 1103515245 + 12345) % 2147483648
        pri[i] += U["noise"] * x / 2147483648 - (U["lead"] * o["s"] if o["s"] is not None else 0.0) + 1e9 * o.get("first", 0) + U["role"].get(o["role"], 0)
    ready = [0.0] * n
    pool = {e: [] for e in "vstgy"}
    free = {e: 0.0 for e in "vstgy"}
    seq, end = [], [0.0] * n
    held = {}
    for i, o in enumerate(ops):
        for j in o["soft"] + ([o["late"]] if "late" in o else []):
            held.setdefault(j, []).append(i)
            left[i] += 1

    def done(i):
        for j in succ[i]:
            same = ops[j]["e"] == ops[i]["e"] and ops[i]["k"] not in ("dma", "send")
            ready[j] = max(ready[j], end[i] + (P["same"] if same else P["wake"]))
            left[j] -= 1
            if left[j] == 0:
                enter(j)
        for j in held.get(i, []):
            left[j] -= 1
            if left[j] == 0:
                enter(j)

    def enter(j):
        if ops[j]["e"] is None:
            end[j] = ready[j] + cs[j][1]
            seq.append(j)
            done(j)
        else:
            pool[ops[j]["e"]].append(j)

    for i in [i for i in range(n) if left[i] == 0]:
        enter(i)
    while len(seq) < n:
        t, e = min((max(free[e], min(ready[j] for j in pool[e])), e) for e in pool if pool[e])
        i = max((j for j in pool[e] if ready[j] <= t + U["look"]), key=lambda j: (pri[j], -j))
        t = max(t, ready[i])
        pool[e].remove(i)
        free[e] = t + cs[i][0]
        end[i] = t + cs[i][1]
        seq.append(i)
        done(i)
    return seq, end


def lags(ops, P):
    cs = [cost(o, P) for o in ops]
    pred = []
    for o in ops:
        p = {}
        for d in o["soft"] + ([o["late"]] if "late" in o else []):
            p[d] = cs[d][0]
        for d in o["near"]:
            same = ops[d]["e"] == o["e"] and ops[d]["k"] not in ("dma", "send")
            p[d] = cs[d][1] + (P["same"] if same else P["wake"])
        pred.append(list(p.items()))
    return cs, pred


def place(seq, eng, hold, pred):
    st = [0.0] * len(eng)
    A, Z = {e: [] for e in "vstgy"}, {e: [] for e in "vstgy"}
    for i in seq:
        t = max([st[d] + l for d, l in pred[i]] + [0.0])
        if eng[i] is not None:
            a, z = A[eng[i]], Z[eng[i]]
            k = len(z)
            while k and z[k - 1] > t:
                k -= 1
            while k < len(a) and a[k] < t + hold[i]:
                t = z[k]
                k += 1
            a.insert(k, t)
            z.insert(k, t + hold[i])
        st[i] = t
    return st


def squeeze(ops, P, end, rounds):
    cs, pred = lags(ops, P)
    n = len(ops)
    hold, eng = [c[0] for c in cs], [o["e"] for o in ops]
    back = [[] for _ in ops]
    for j in range(n):
        for d, l in pred[j]:
            back[d].append((j, l + hold[j] - hold[d]))
    back = [b or [(n, cs[i][1] - hold[i])] for i, b in enumerate(back)] + [[]]
    st = [end[i] - cs[i][1] for i in range(n)]
    best = (max(end), st)
    for _ in range(rounds):
        rs = place([n] + sorted(range(n), key=lambda i: -st[i] - hold[i]), eng + [None], hold + [0], back)
        st = place(sorted(range(n), key=lambda i: -rs[i] - hold[i]), eng, hold, pred)
        best = min(best, (max(st[i] + cs[i][1] for i in range(n)), st))
    return best[0], sorted(range(n), key=lambda i: best[1][i])


def timings(ops, Ps):
    eng = [o["e"] for o in ops]
    L = [lags(ops, P) for P in Ps]
    L = [([c[0] for c in cs], [c[1] for c in cs], pred) for cs, pred in L]
    last = [i for i, o in enumerate(ops) if o["k"] == "dma"]
    kept = [[[0.0] * len(ops) for _ in Ps], None]

    def judge(seq, lo, limit):
        out, new = 1.0, []
        before = {eng[i]: i for i in seq[max(0, lo - 400):lo]}
        for (hold, lat, pred), old in zip(L, kept[0]):
            st = list(old)
            free = {e: st[before[e]] + hold[before[e]] if e in before else 0.0 for e in "vstgy"}
            for i in seq[lo:]:
                e = eng[i]
                t = free[e] if e else 0.0
                for d, l in pred[i]:
                    if st[d] + l > t:
                        t = st[d] + l
                st[i] = t
                if e:
                    free[e] = t + hold[i]
            out *= max(st[i] + lat[i] for i in last)
            new.append(st)
        if out < limit:
            kept[0] = new
        return out
    return judge


def swaps(ops, P, seq, turns, width, x, judge=None):
    cs, pred = lags(ops, P)
    n = len(ops)
    hold, lat = [c[0] for c in cs], [c[1] for c in cs]
    succ = [[] for _ in ops]
    for j in range(n):
        for d, l in pred[j]:
            succ[d].append((j, l))
    direct = [set(d for d, _ in p) for p in pred]
    mp, mn, seq = [-1] * n, [-1] * n, list(seq)
    head, tail = [0.0] * n, [0.0] * n
    score = [judge(seq, 0, 1e300) if judge else 0.0]

    def link():
        last = {}
        for i in seq:
            e = ops[i]["e"]
            mp[i], mn[i] = -1, -1
            if e in last and e is not None:
                mp[i], mn[last[e]] = last[e], i
            last[e] = i

    def early(i, t):
        for d, l in pred[i]:
            if head[d] + l > t:
                t = head[d] + l
        return t

    def late(i, t):
        for d, l in succ[i]:
            if tail[d] + l > t:
                t = tail[d] + l
        return t

    def mend(a, b, lo, hi):
        for i in seq[a:hi]:
            k = mp[i]
            t = head[k] + hold[k] if k >= 0 else 0.0
            for d, l in pred[i]:
                if head[d] + l > t:
                    t = head[d] + l
            head[i] = t
        for i in reversed(seq[lo:b + 1]):
            k, t = mn[i], lat[i]
            if k >= 0 and tail[k] + hold[i] > t:
                t = tail[k] + hold[i]
            for d, l in succ[i]:
                if tail[d] + l > t:
                    t = tail[d] + l
            tail[i] = t
        return max([head[i] + tail[i] for i in seq[lo:hi]])

    for lo in list(range(0, n, width // 2)) + list(range(width // 4, n, width // 2)):
        link()
        mend(0, n - 1, 0, n)
        seq.sort(key=lambda i: head[i])
        hi = min(lo + width, n)
        pos = {seq[k]: k for k in range(lo, hi)}
        now = max(head[i] + tail[i] for i in seq[lo:hi])
        best, barred, was = (now, seq[lo:hi]), {}, seq[lo:hi]
        for turn in range(turns):
            cand = []
            for v in seq[lo:hi]:
                u = mp[v]
                if head[v] + tail[v] > now - 1e-6 and u in pos and head[u] + hold[u] > head[v] - 1e-6 and u not in direct[v]:
                    hv = early(v, head[mp[u]] + hold[mp[u]] if mp[u] >= 0 else 0.0)
                    tu = late(u, max(lat[u], tail[mn[v]] + hold[u]) if mn[v] >= 0 else lat[u])
                    est = max(hv + late(v, max(lat[v], tu + hold[v])), early(u, hv + hold[v]) + tu)
                    x = (x * 1103515245 + 12345) % 2147483648
                    if barred.get((v, u), 0) <= turn or est < best[0] - 1e-6:
                        cand.append((est + 30.0 * x / 2147483648, u, v))
            if not cand:
                if not barred:
                    break
                barred.clear()
                continue
            _, u, v = min(cand)
            a, b = mp[u], mn[v]
            if a >= 0:
                mn[a] = v
            if b >= 0:
                mp[b] = u
            mp[v], mn[v], mp[u], mn[u] = a, u, v, b
            barred[(u, v)] = turn + 8 + (x >> 8) % 13
            pu, pv = pos[u], pos[v]
            behind, ahead, after = {u}, [], [u]
            for i in seq[pu + 1:pv + 1]:
                if i != v and (direct[i] & behind or mp[i] in behind):
                    behind.add(i)
                    after.append(i)
                else:
                    ahead.append(i)
            seq[pu:pv + 1] = ahead + after
            for k in range(pu, pv + 1):
                pos[seq[k]] = k
            now = mend(pu, pv, lo, hi)
            if now < best[0] - 1e-6:
                best = (now, seq[lo:hi])
        seq[lo:hi] = best[1]
        if judge and best[1] != was:
            t = judge(seq, lo, score[0])
            if t < score[0]:
                score[0] = t
            else:
                seq[lo:hi] = was
    link()
    mend(0, n - 1, 0, n)
    return seq, [head[i] + lat[i] for i in range(n)]


def plan(O, U):
    ops = build(O)
    seq = min(squeeze(ops, PAR, order(ops, PAR, dict(U, lead=lead))[1], 6) for lead in U["leads"])[1]
    for k, width in enumerate(U["widths"]):
        seq, end = swaps(ops, PAR, seq, U["turns"], width, k + 1)
        seq = squeeze(ops, PAR, end, 2)[1]
    Ps = [dict(PAR, cyc=0.83 * f, g=g, wake=w, same=0.9 * w, pe=pe * f, link=link) for f, g, w, pe, link in U["more"]]
    judge = timings(ops, Ps)
    for k in range(U["passes"]):
        seq = swaps(ops, Ps[k % len(Ps)], seq, U["turns2"], U["widths2"][k % len(U["widths2"])], 100 + k, judge)[0]
    seq, end = swaps(ops, PAR, seq, 0, len(ops), 1)
    known = {e: 0 for e in "vstgy"}
    K, waits, raised, before, pre = {}, {}, set(), {}, {e: 0 for e in "vstgy"}
    for i in seq:
        e = ops[i]["e"]
        if e is None:
            K[i] = 0
            continue
        w = []
        for d in sorted(ops[i]["deps"], key=lambda d: -end[d]):
            if not known[e] >> d & 1:
                w.append(d)
                raised.add(d)
                known[e] |= K[d] | (1 << d) | before.get(d, 0)
        K[i], waits[i] = known[e], w
        if ops[i]["k"] not in ("dma", "send"):
            before[i] = pre[e]
            pre[e] |= (1 << i) | K[i]
    sem, names, turn, tail = {}, [], {e: 0 for e in "vstg"}, []
    for i in seq:
        o = ops[i]
        if o["k"] == "dma":
            names.append("d%d" % len(names))
            sem[i] = (names[-1], 16)
            if i not in raised:
                tail.append(i)
        elif o["k"] not in ("arr", "send") and i in raised:
            turn[o["e"]] += 1
            sem[i] = (o["e"] + "0", turn[o["e"]])
    names += [e + "0" for e in "vstg"]
    return ops, seq, waits, sem, names, tail, end


OPS, SEQ, WAITS, SEM, _NAMES, TAIL, END = plan(OPT, TUNE)
NST = len(OPT["nw"])
SEMAPHORES = (_NAMES + ["am0", "am1", "am4", "ae0", "ae1", "ab0", "ab1", "ab4", "af", "sent", "rm", "re0", "re1", "re2", "ro0", "rb0", "rf"]
              + ["an%d" % k for k in range(2 * NST)] + ["rn%d" % k for k in range(NST)])


def bits(es):
    return sum(1 << e for e in es)


def relays(T, topo, core, dst):
    cs = [c for c in topo.cores_of(core) if c != core and T.rank_of(c) is None and topo.may_write(c, dst)]
    near = [c for c in cs if topo.die(c) == topo.die(core)]
    far = [c for c in cs if topo.die(c) != topo.die(core)]
    return [near[0], far[0], near[1], far[1]]


def piece(T, kind, k, landed):
    if kind == "m":
        return T["misc1" if landed else "misc"][:, 33 * k:33 * k + 33]
    if kind == "e":
        a, b = EVEN[k // 2]
        return T["we1" if landed else "we0"][:, a + (b - a) // 2 * (k % 2):a + (b - a) // 2 * (k % 2 + 1)]
    if kind == "o":
        return T["wo1" if landed else "wo0"][:, 512 * k:512 * k + 512]
    if kind == "b":
        return T["w1b" if landed else "own0"][:, 1024 * k:1024 * k + 1024]
    if kind == "f":
        return T.w4b[:, 1024 * k:1024 * k + 1024]
    w = OPT["nw"][k // 4] // 2
    a = 512 * (k // 2 % 2) + sum(OPT["nw"][:k // 4]) + w * (k % 2)
    return T["new1" if landed else "newb"][:, a:a + w]


def relay_program(g, core, T, topo, src, down, far, k):
    on, off = topo.engines(src, core), topo.engines(src, far)
    rest = len(on) - len(off)
    half = len(on) // 2
    steps = [("m", k, rest // NREL, down, "am0" if k == 0 else "am1", "rm")]
    steps += [("e", j, half, down, "ae%d" % (EVEN[j // 2][0] // 1024), "re%d" % (j // NREL)) for j in range(k, 2 * len(EVEN), NREL)]
    steps.append(("o", k, half, down, "ab%d" % (k // 2), "ro0"))
    steps.append(("f", k, 32, far, "ab4", "rf"))
    a, b = 1024 * k, 1024 * k + 1024
    g.sync.wait_ge(T.sem.rb0, len(on) // NREL)
    g.sync.dma_start(T.w4b[0:112, a:b], T.w1b[16:128, a:b]).then_inc(T.sem.rf, 16)
    g.sync.dma_start(T.w4b[112:128, a:b], T.w1b[0:16, a:b]).then_inc(T.sem.rf, 16)
    steps += [("n", k + NREL * s, len(on) // NREL, down, "an%d" % (k // 2 + 2 * s), "rn%d" % s) for s in range(NST)]
    total = 0
    for kind, j, n, dst, sem, got in steps:
        rid, pid = topo.addr(dst, core)
        g.wait_ge(T.sem[got], n)
        if kind == "f":
            g.wait_ge(T.sem.sent, total)
        p = piece(T, kind, j, True)
        g.remote_dma(p, p, T.sem[sem], T.sem.sent, pid, rid, topo.mask(core, dst))
        total += len(topo.engines(core, dst))
    g.wait_ge(T.sem.sent, total)


def rank_program(g, core, T, topo):
    N = len(T.cores)
    rank = T.rank_of(core)
    if rank is None:
        for r, c in enumerate(T.cores):
            if c in topo.cores_of(core):
                down, far = T.cores[(r - 1) % N], T.cores[(r - 4) % N]
                rel = relays(T, topo, c, down)
                if core in rel:
                    relay_program(g, core, T, topo, c, down, far, rel.index(core))
        return
    down, far = T.cores[(rank - 1) % N], T.cores[(rank - 4) % N]
    rel = relays(T, topo, core, down)
    on, off = topo.engines(core, rel[0]), topo.engines(core, far)
    only_on = [e for e in on if e not in off]
    up = T.cores[(rank + 1) % N]
    n_in = len(topo.engines(relays(T, topo, up, core)[0], core))
    n_far = len(topo.engines(T.cores[(rank + 4) % N], core))
    Q = {"v": g.vector, "s": g.scalar, "t": g.tensor, "g": g, "y": g.sync}
    A, F = AluOpType, ActivationFunctionType
    alu = {"add": A.add, "subtract": A.subtract, "mult": A.mult, "max": A.max, "min": A.min, "is_ge": A.is_ge, "is_gt": A.is_gt,
           "is_le": A.is_le, "is_equal": A.is_equal, "arith_shift_right": A.arith_shift_right, "bitwise_and": A.bitwise_and}
    sent = [0]

    def ap(r):
        if not isinstance(r, tuple):
            return r
        if r[0] == "ind":
            return ap(r[1]).indirect(ap(r[2]))
        p = slice(r[4], r[5]) if r[6] == 1 else slice(r[4], r[5], r[6])
        c = slice(r[1], r[2]) if r[3] == 1 else slice(r[1], r[2], r[3])
        return T[r[0]][p, c]

    def tr(dst, src_ap, dst_ap, sem, es):
        rid, pid = topo.addr(dst, core)
        sent[0] += len(es)
        return RemoteDMATransfer(dst_ids=[DstId(rid=rid, pnc=pid)], dma_engine_mask=bits(es), remote_sem=T.sem[sem], src=src_ap, dst=dst_ap)

    def do_send(what):
        if what == "misc":
            few = len(only_on) // NREL
            ts_ = [tr(rel[k], piece(T, "m", k, False), piece(T, "m", k, True), "rm", only_on[few * k:few * k + few]) for k in range(NREL)]
            ts_.append(tr(far, T.misc[:, 0:33], T.misc4[:, 0:33], "am4", off))
        elif what == "whole":
            ts_ = [tr(rel[k], piece(T, "b", k, False), piece(T, "b", k, True), "rb0", on[k::NREL]) for k in range(NREL)]
        elif what == "far":
            ts_ = [tr(far, T.newb[:], T.new4[:], "af", off)]
        elif what[0] == "m":
            s = int(what[-1])
            ts_ = [tr(rel[k], piece(T, "n", NREL * s + k, False), piece(T, "n", NREL * s + k, True), "rn%d" % s, on[k::NREL]) for k in range(NREL)]
        else:
            kind, h = what[0], int(what[-1])
            ts_ = [tr(rel[(2 * h + j) % NREL], piece(T, kind, 2 * h + j, False), piece(T, kind, 2 * h + j, True), "r%s%d" % (kind, h // 2), on[j::2])
                   for j in range(2)]
        g.remote_dma_fused(ts_, local_sem=T.sem.sent)

    for i in SEQ:
        o = OPS[i]
        e, k, a = o["e"], o["k"], o["a"]
        if e is None:
            continue
        q = Q[e]
        for d in WAITS[i]:
            if OPS[d]["k"] == "arr":
                nm, n = OPS[d]["a"][0], OPS[d]["a"][1]
                q.wait_ge(T.sem[nm], n[0] * n_in + n[1] * n_far)
            else:
                q.wait_ge(T.sem[SEM[d][0]], SEM[d][1])
        if k == "send":
            do_send(a[0])
            continue
        if k == "tt":
            ins = q.tensor_tensor(ap(a[0]), ap(a[1]), ap(a[2]), alu[a[3]])
        elif k == "ts":
            if a[5] is None:
                ins = q.tensor_scalar(ap(a[0]), ap(a[1]), ap(a[2]), None, alu[a[4]])
            else:
                ins = q.tensor_scalar(ap(a[0]), ap(a[1]), ap(a[2]), ap(a[3]), alu[a[4]], alu[a[5]])
        elif k == "scan":
            ins = q.tensor_tensor_scan(ap(a[0]), ap(a[1]), ap(a[2]), a[5], alu[a[3]], alu[a[4]])
        elif k == "cp":
            ins = q.tensor_copy(ap(a[0]), ap(a[1]))
        elif k == "ms":
            ins = q.memset(ap(a[0]), a[1])
        elif k == "act":
            if a[3] is not None and a[2] is not None:
                ins = q.activation(ap(a[0]), ap(a[1]), F.Identity, bias=ap(a[3]), scale=ap(a[2]))
            elif a[3] is not None:
                ins = q.activation(ap(a[0]), ap(a[1]), F.Identity, bias=ap(a[3]))
            elif a[2] is not None:
                ins = q.activation(ap(a[0]), ap(a[1]), F.Copy, scale=ap(a[2]))
            else:
                ins = q.activation(ap(a[0]), ap(a[1]), F.Copy)
        elif k == "mm":
            for m in a:
                ins = q.matmul(ap(m[0]), ap(m[1]), ap(m[2]), m[3], m[4])
        elif k == "iota":
            if SCRATCH[a[0][0]][2] == "int32":
                ins = q.iota(ap(a[0]), a[1], a[2], a[3])
            else:
                ins = q.iota(ap(a[0]), a[1], a[2], a[3], allow_small_or_imprecise_dtypes=True)
        elif k == "gcp":
            ins = q.affine_select(ap(a[0]), ap(a[1]), [[0, _n(a[0])]], A.is_equal, 0.0, 0, 0)
        elif k == "sel":
            ins = q.affine_select(ap(a[0]), ap(a[1]), [[-1, 128]], A.is_equal, 0.0, 0, 1)
        else:
            ins = q.dma_start(ap(a[0]), ap(a[1]))
        if i in SEM:
            ins.then_inc(T.sem[SEM[i][0]], 16 if k == "dma" else 1)
    for i in TAIL:
        Q[OPS[i]["e"]].wait_ge(T.sem[SEM[i][0]], 16)
    g.wait_ge(T.sem.sent, sent[0])
